import numpy as np
import ml_dtypes


def mxq(x, axis, fmt="e4m3"):
    dtype, down = {"e4m3": (ml_dtypes.float8_e4m3fn, 7), "e5m2": (ml_dtypes.float8_e5m2, 14)}[fmt]
    v = np.moveaxis(np.asarray(x, np.float32).astype(ml_dtypes.bfloat16).astype(np.float64), axis, -1)
    blocks = v.reshape(v.shape[:-1] + (-1, 32))
    amax = np.abs(blocks).max(-1, keepdims=True)
    byte = np.maximum(np.where(amax > 0, np.frexp(amax)[1] - 1 + 127, 0) - down, 1)
    scale = np.exp2(byte - 127.0)
    codes = (blocks / scale).astype(np.float32).astype(dtype).astype(np.float64)
    return np.moveaxis((codes * scale).reshape(v.shape), -1, axis)


WIDE = False


def mx_kscale(k):
    if not WIDE:
        return np.ones(k)
    levels = np.array([10, -10, 5, -5, 0])
    if k % 512:
        return np.exp2(np.random.permutation(np.resize(levels, k // 32))).repeat(32)
    a = np.empty((k // 512, 16))
    for p in range(k // 512):
        a[p, :8] = np.random.permutation(np.resize(levels, 8))
        for g in range(8):
            far = levels[np.abs(levels - a[p, g]) >= 10]
            a[p, g + 8] = far[np.random.randint(len(far))]
    return np.exp2(a.ravel()).repeat(32)


def f64(x):
    return np.asarray(x).astype(np.float64)


def striped(idx):
    return np.tile(idx.reshape(-1, 16).T, (8, 1)).astype(np.uint16)


def unstriped(offs):
    return offs[:16].T.reshape(-1).astype(np.int64)


def striped8(idx):
    return np.concatenate([x.reshape(-1, 16).T for x in idx]).astype(np.uint16)


def runs(offs, k):
    lists = np.stack([offs[16 * r : 16 * r + 16].T.reshape(-1) for r in range(8)]).astype(np.int64)
    return lists[np.arange(k) % 512 // 64]


def pack_weight(w):
    k, n = w.shape
    w = f64(np.asarray(w, np.float32).astype(ml_dtypes.bfloat16)).reshape(k // 32, 32, n)
    amax = np.abs(w).max(1)
    byte = np.clip(np.where(amax > 0, np.frexp(amax)[1] - 1 + 127 - 7, 1), 1, 254)
    scaled = (w * np.exp2(127.0 - byte)[:, None, :]).reshape(k, n).astype(np.float32)
    words = np.ascontiguousarray(scaled.reshape(k // 512, 128, 4, n).transpose(0, 1, 3, 2)).astype(ml_dtypes.float8_e4m3fn).view(np.uint8)
    return words, np.ascontiguousarray(byte.astype(np.uint8).reshape(k // 512, 16, n))


def unpack_weight(words, scales):
    g, p, n, _ = words.shape
    vals = np.ascontiguousarray(words).view(ml_dtypes.float8_e4m3fn).astype(np.float64) * np.repeat(np.exp2(scales.astype(np.float64) - 127.0), 8, axis=1)[..., None]
    return vals.transpose(0, 1, 3, 2).reshape(g * 512, n)


def relu(v):
    return np.maximum(v, 0.0)

def planes(y):
    n, m = y.shape
    v = y.astype(np.float32).astype(ml_dtypes.bfloat16).astype(np.float64).reshape(n // 32, 32, m)
    top = np.abs(v).max(1)
    byte = np.clip(np.where(top > 0, np.frexp(top)[1] - 1 + 127 - 7, 1), 1, 254)
    codes = (v * np.exp2(127.0 - byte)[:, None, :]).reshape(n, m).astype(np.float32).astype(ml_dtypes.float8_e4m3fn).view(np.uint8)
    words = codes.reshape(n // 512, 128, 4, m).transpose(0, 1, 3, 2)
    return np.ascontiguousarray(words), np.ascontiguousarray(byte.astype(np.uint8).reshape(n // 512, 16, m))


K, T, S, N, U, H = 512, 2048, 512, 512, 1024, 512


def setup_inputs():
    n = np.random.standard_normal
    s = mx_kscale(K)[:, None]
    u = mx_kscale(H)
    packed_xT = pack_weight(n((K, T)) * s)
    packed_w2 = pack_weight(n((H, N)) / np.sqrt(2 * H) / u[:, None])
    packed_w3 = pack_weight(n((K, N)) / np.sqrt(2 * K) / s)
    return {
        "x_words": packed_xT[0],
        "x_scales": packed_xT[1],
        "w1": (n((K, H)) / np.sqrt(K) / s * u).astype(np.float32),
        "w2_words": packed_w2[0],
        "w2_scales": packed_w2[1],
        "w3_words": packed_w3[0],
        "w3_scales": packed_w3[1],
        "offs": striped(np.random.permutation(T)[:S]),
        "where": striped8(np.stack([np.random.permutation(U)[:S] for _ in range(8)])),
        "skip": striped(np.random.permutation(T)[:U]),
    }


def reference(x_words, x_scales, w1, w2_words, w2_scales, w3_words, w3_scales, offs, where, skip):
    xq = unpack_weight(x_words, x_scales)[:, unstriped(offs)]
    y = relu(mxq(f64(w1), 0, "e4m3").T @ xq)
    z = np.zeros((H, U))
    z[np.arange(H)[:, None], runs(where, H)] = y
    x_skip = unpack_weight(x_words, x_scales)[:, unstriped(skip)]
    out_0 = unpack_weight(w2_words, w2_scales).T @ mxq(z, 0, "e4m3") + unpack_weight(w3_words, w3_scales).T @ x_skip
    return (out_0,) + planes(out_0)

@@ -1,0 +1,212 @@
+from contextlib import ExitStack
+
+import concourse.mybir as mybir
+
+K, T, S, N, U, H = 512, 2048, 512, 512, 1024, 512
+FLOPS = 2 * K * H * S + 2 * H * N * U + 2 * K * N * U
+
+F32 = mybir.dt.float32
+BF16 = mybir.dt.bfloat16
+I32 = mybir.dt.int32
+U32 = mybir.dt.uint32
+U16 = mybir.dt.uint16
+U8 = mybir.dt.uint8
+FP8X4 = mybir.dt.float8_e4m3fn_x4
+ACT = mybir.ActivationFunctionType
+
+P = 128
+PACK = 4
+HALF = U // 2
+W3_ROW = 4
+SCALAR_CELLS = 160
+
+
+def words_view(dram):
+    return dram[0].rearrange("p c r -> p (c r)").bitcast(I32)
+
+
+def load_scale_rows(nc, tile, first_row, dram):
+    for q in range(4):
+        nc.sync.dma_start(
+            out=tile[32 * q + first_row : 32 * q + first_row + 4, :].bitcast(I32),
+            in_=dram[0, 4 * q : 4 * q + 4, :].bitcast(I32),
+        )
+
+
+def deal(nc, out, in_):
+    nc.vector.tensor_copy(
+        out=out.rearrange("p w (t m) -> p w m t", t=PACK),
+        in_=in_.rearrange("p w (m t) -> p w m t", t=PACK),
+    )
+
+
+def tile_picked_segunpool_relu_po_kernel(
+    tc, x_words, x_scales, w1, w2_words, w2_scales, w3_words, w3_scales, offs, where, skip, out_0, out_1, out_2
+):
+    nc = tc.nc
+    with ExitStack() as ctx:
+        lists = ctx.enter_context(tc.tile_pool(name="lists", bufs=1))
+        sb = ctx.enter_context(tc.tile_pool(name="sb", bufs=1))
+        psum = ctx.enter_context(tc.psum_pool(name="psum", bufs=1))
+
+        def tile(shape, dtype, name, tag=None):
+            return sb.tile(shape, dtype, name=name, tag=tag or name, align_bytes=64)
+
+        offs_sb = lists.tile([P, S // 16], U16, name="offs_sb")
+        skip_sb = lists.tile([P, U // 16], U16, name="skip_sb")
+        where_sb = lists.tile([P, S // 16], U16, name="where_sb")
+        x_bytes = tile([P, T], U8, "x_bytes")
+        w_bytes_raw = tile([P, N], U8, "w_bytes_raw")
+        z = [tile([P, U], F32, f"z{t}") for t in range(PACK)]
+
+        nc.vector.memset(x_bytes[:].bitcast(I32), 0)
+        with tc.tile_pool(name="early", bufs=1) as early:
+            zeros = early.tile([P, N // 4], I32, name="zeros")
+            nc.vector.memset(zeros[:], 0)
+            nc.vector.tensor_copy(out=w_bytes_raw[:].bitcast(I32), in_=zeros[:])
+        loads = ctx.enter_context(tc.tile_pool(name="loads", bufs=1))
+        x_codes = loads.tile([P, T], U32, name="x_codes")
+        w1_raw = loads.tile([P, PACK, H], F32, name="w1_raw")
+        w_raw = loads.tile([P, 2, N], U32, name="w_raw")
+        for t in range(PACK):
+            nc.vector.memset(z[t][:].bitcast(I32), 0)
+
+        nc.sync.dma_start(offs_sb[:], offs)
+        nc.sync.dma_start(skip_sb[:], skip)
+        nc.sync.dma_start(where_sb[:], where)
+        load_scale_rows(nc, x_bytes, 0, x_scales)
+        nc.sync.dma_start(out=x_codes[:].bitcast(I32), in_=words_view(x_words))
+        load_scale_rows(nc, w_bytes_raw, W3_ROW, w3_scales)
+        nc.sync.dma_start(out=w1_raw[:], in_=w1.rearrange("(p j) h -> p j h", j=PACK))
+        load_scale_rows(nc, w_bytes_raw, 0, w2_scales)
+        nc.sync.dma_start(out=w_raw[:, 0, :].bitcast(I32), in_=words_view(w2_words))
+        nc.sync.dma_start(out=w_raw[:, 1, :].bitcast(I32), in_=words_view(w3_words))
+
+        picked_bytes = tile([P, S], U8, "picked_bytes")
+        skip_bytes = tile([P, U], U8, "skip_bytes")
+        picked_codes = tile([P, S], U32, "picked_codes")
+        nc.vector.tensor_copy(out=picked_bytes[:], in_=x_bytes[:].indirect(offs_sb[:]))
+        nc.vector.tensor_copy(out=skip_bytes[:], in_=x_bytes[:].indirect(skip_sb[:]))
+        nc.vector.tensor_copy(out=picked_codes[:], in_=x_codes[:].indirect(offs_sb[:]))
+
+        def gather_skip_codes(h, tag):
+            codes = tile([P, HALF], U32, f"skip_codes{h}", tag)
+            cols = slice(h * HALF // 16, (h + 1) * HALF // 16)
+            nc.vector.tensor_copy(out=codes[:], in_=x_codes[:].indirect(skip_sb[:, cols]))
+            return codes
+
+        skip_codes = [gather_skip_codes(0, None)]
+
+        w1_codes, w1_bytes = [], []
+        for u in range(2):
+            grouped = tile([P, 2, P, PACK], BF16, f"w1_grouped{u}")
+            nc.scalar.activation(
+                out=grouped[:].rearrange("p t m j -> p m j t"),
+                in_=w1_raw[:].rearrange("p j (m t) -> p m j t", t=PACK)[:, :, :, 2 * u : 2 * u + 2],
+                func=ACT.Copy,
+            )
+            codes = tile([P, 2 * P], U32, f"w1_codes{u}")
+            scale = tile([P, 2 * P], U8, f"w1_bytes{u}")
+            nc.vector.quantize_mx(
+                out=codes[:].bitcast(FP8X4), scales=scale[:], in_=grouped[:].rearrange("p t m j -> p (t m j)")
+            )
+            w1_codes.append(codes)
+            w1_bytes.append(scale)
+            if u == 0:
+                skip_codes.append(gather_skip_codes(1, "w1_grouped0"))
+
+        y = []
+        for t in range(PACK):
+            cols = slice((t % 2) * P, (t % 2 + 1) * P)
+            acc = psum.tile([P, S], F32, name=f"y_acc{t}", tag=f"bank{PACK + t}")
+            nc.tensor.matmul_mx(
+                out=acc[:],
+                lhsT=w1_codes[t // 2][:, cols].bitcast(FP8X4),
+                lhsT_scale=w1_bytes[t // 2][:, cols],
+                rhs=picked_codes[:].bitcast(FP8X4),
+                rhs_scale=picked_bytes[:],
+                start=True,
+                stop=True,
+            )
+            y.append(tile([P, S], F32, f"y{t}"))
+            nc.scalar.activation(out=y[t][:], in_=acc[:], func=ACT.Relu)
+
+        z_grouped = [tile([P, HALF, PACK], BF16, f"z_grouped{h}") for h in range(2)]
+        for t in range(PACK):
+            nc.vector.tensor_copy(out=z[t][:].indirect(where_sb[:]), in_=y[t][:])
+            if t == 1:
+                w_bytes = tile([P, N], U8, "w_bytes", "y1")
+                deal(nc, w_bytes[:].unsqueeze(1), w_bytes_raw[:].unsqueeze(1))
+            if t == 0:
+                w_codes = tile([P, 2, N], U32, "w_codes", "y0")
+                deal(nc, w_codes[:], w_raw[:])
+            if t < PACK - 1:
+                for h in range(2):
+                    src = z[t][:, h * HALF : (h + 1) * HALF]
+                    if t < 2:
+                        nc.scalar.copy(out=z_grouped[h][:, :, t], in_=src)
+                    else:
+                        nc.scalar.copy(out=z_grouped[h][:, :, 2:4], in_=src.unsqueeze(2).to_broadcast([P, HALF, 2]))
+
+        acc = [[psum.tile([P, HALF], F32, name=f"acc{h}{t}", tag=f"bank{PACK * h + t}") for t in range(PACK)] for h in range(2)]
+        for h in range(2):
+            for t in range(PACK):
+                cols = slice(t * P, (t + 1) * P)
+                nc.tensor.matmul_mx(
+                    out=acc[h][t][:],
+                    lhsT=w_codes[:, 1, cols].bitcast(FP8X4),
+                    lhsT_scale=w_bytes[W3_ROW:P, cols],
+                    rhs=skip_codes[h][:].bitcast(FP8X4),
+                    rhs_scale=skip_bytes[:, h * HALF : (h + 1) * HALF],
+                    start=True,
+                    stop=False,
+                )
+
+        nc.vector.tensor_copy(out=z_grouped[0][:, :, 3], in_=z[3][:, 0:HALF])
+        nc.scalar.copy(out=z_grouped[1][:, :, 3], in_=z[3][:, HALF:U])
+        for h in range(2):
+            z_codes = tile([P, HALF], U32, f"z_codes{h}")
+            z_bytes = tile([P, HALF], U8, f"z_bytes{h}")
+            nc.vector.quantize_mx(
+                out=z_codes[:].bitcast(FP8X4), scales=z_bytes[:], in_=z_grouped[h][:].rearrange("p c t -> p (c t)")
+            )
+            for t in range(PACK):
+                cols = slice(t * P, (t + 1) * P)
+                nc.tensor.matmul_mx(
+                    out=acc[h][t][:],
+                    lhsT=w_codes[:, 0, cols].bitcast(FP8X4),
+                    lhsT_scale=w_bytes[:, cols],
+                    rhs=z_codes[:].bitcast(FP8X4),
+                    rhs_scale=z_bytes[:],
+                    start=False,
+                    stop=True,
+                )
+
+        out_rows = out_0.rearrange("(p t) w -> p t w", t=PACK)
+        out_bytes = tile([P, U], U8, "out_bytes")
+        for h in range(2):
+            cells = slice(h * HALF, (h + 1) * HALF)
+            result = tile([P, PACK, HALF], F32, f"result{h}")
+            for t in range(PACK):
+                if h == 0 and t >= 2:
+                    nc.vector.tensor_copy(out=result[:, t, :], in_=acc[h][t][:])
+                else:
+                    nc.scalar.copy(out=result[:, t, :], in_=acc[h][t][:])
+                nc.sync.dma_start(out=out_rows[:, t, cells], in_=result[:, t, :])
+            grouped = tile([P, HALF, PACK], BF16, f"out_grouped{h}")
+            src = result[:].rearrange("p t (c i) -> p c t i", i=4)
+            dst = grouped[:].rearrange("p (c i) t -> p c t i", i=4)
+            split = SCALAR_CELLS // 4 if h == 1 else 0
+            if split:
+                nc.scalar.copy(out=dst[:, :split], in_=src[:, :split])
+            nc.vector.tensor_copy(out=dst[:, split:], in_=src[:, split:])
+            out_codes = tile([P, HALF], U32, f"out_codes{h}")
+            nc.vector.quantize_mx(
+                out=out_codes[:].bitcast(FP8X4), scales=out_bytes[:, cells], in_=grouped[:].rearrange("p c t -> p (c t)")
+            )
+            queue = nc.scalar if h == 1 else nc.sync
+            queue.dma_start(out=words_view(out_1)[:, cells], in_=out_codes[:].bitcast(I32))
+        for q in range(4):
+            nc.sync.dma_start(
+                out=out_2[0, 4 * q : 4 * q + 4, :].bitcast(I32), in_=out_bytes[32 * q : 32 * q + 4, :].bitcast(I32)
+            )

@@ -18,7 +18,8 @@ P = 128
 PACK = 4
 HALF = U // 2
 W3_ROW = 4
-SCALAR_CELLS = 160
+QUARTER = U // 4
+SCALAR_CELLS = 80
 
 
 def words_view(dram):
@@ -57,7 +58,6 @@ def tile_picked_segunpool_relu_po_kernel(
         where_sb = lists.tile([P, S // 16], U16, name="where_sb")
         x_bytes = tile([P, T], U8, "x_bytes")
         w_bytes_raw = tile([P, N], U8, "w_bytes_raw")
-        z = [tile([P, U], F32, f"z{t}") for t in range(PACK)]
 
         nc.vector.memset(x_bytes[:].bitcast(I32), 0)
         with tc.tile_pool(name="early", bufs=1) as early:
@@ -66,10 +66,11 @@ def tile_picked_segunpool_relu_po_kernel(
             nc.vector.tensor_copy(out=w_bytes_raw[:].bitcast(I32), in_=zeros[:])
         loads = ctx.enter_context(tc.tile_pool(name="loads", bufs=1))
         x_codes = loads.tile([P, T], U32, name="x_codes")
-        w1_raw = loads.tile([P, PACK, H], F32, name="w1_raw")
+        w1_raw = [loads.tile([P, PACK, H // 2], F32, name=f"w1_raw{a}") for a in range(2)]
         w_raw = loads.tile([P, 2, N], U32, name="w_raw")
+        z = [loads.tile([P, U], F32, name=f"z{t}") for t in range(PACK)]
         for t in range(PACK):
-            nc.vector.memset(z[t][:].bitcast(I32), 0)
+            nc.gpsimd.memset(z[t][:], 0.0)
 
         nc.sync.dma_start(offs_sb[:], offs)
         nc.sync.dma_start(skip_sb[:], skip)
@@ -77,7 +78,9 @@ def tile_picked_segunpool_relu_po_kernel(
         load_scale_rows(nc, x_bytes, 0, x_scales)
         nc.sync.dma_start(out=x_codes[:].bitcast(I32), in_=words_view(x_words))
         load_scale_rows(nc, w_bytes_raw, W3_ROW, w3_scales)
-        nc.sync.dma_start(out=w1_raw[:], in_=w1.rearrange("(p j) h -> p j h", j=PACK))
+        for a in range(2):
+            cols = slice(a * H // 2, (a + 1) * H // 2)
+            nc.sync.dma_start(out=w1_raw[a][:], in_=w1.rearrange("(p j) h -> p j h", j=PACK)[:, :, cols])
         load_scale_rows(nc, w_bytes_raw, 0, w2_scales)
         nc.sync.dma_start(out=w_raw[:, 0, :].bitcast(I32), in_=words_view(w2_words))
         nc.sync.dma_start(out=w_raw[:, 1, :].bitcast(I32), in_=words_view(w3_words))
@@ -100,11 +103,12 @@ def tile_picked_segunpool_relu_po_kernel(
         w1_codes, w1_bytes = [], []
         for u in range(2):
             grouped = tile([P, 2, P, PACK], BF16, f"w1_grouped{u}")
-            nc.scalar.activation(
-                out=grouped[:].rearrange("p t m j -> p m j t"),
-                in_=w1_raw[:].rearrange("p j (m t) -> p m j t", t=PACK)[:, :, :, 2 * u : 2 * u + 2],
-                func=ACT.Copy,
-            )
+            for a in range(2):
+                nc.scalar.activation(
+                    out=grouped[:, :, a * P // 2 : (a + 1) * P // 2, :].rearrange("p t m j -> p m j t"),
+                    in_=w1_raw[a][:].rearrange("p j (m t) -> p m j t", t=PACK)[:, :, :, 2 * u : 2 * u + 2],
+                    func=ACT.Copy,
+                )
             codes = tile([P, 2 * P], U32, f"w1_codes{u}")
             scale = tile([P, 2 * P], U8, f"w1_bytes{u}")
             nc.vector.quantize_mx(
@@ -132,48 +136,60 @@ def tile_picked_segunpool_relu_po_kernel(
             nc.scalar.activation(out=y[t][:], in_=acc[:], func=ACT.Relu)
 
         z_grouped = [tile([P, HALF, PACK], BF16, f"z_grouped{h}") for h in range(2)]
-        for t in range(PACK):
+        for t in range(PACK - 1):
             nc.vector.tensor_copy(out=z[t][:].indirect(where_sb[:]), in_=y[t][:])
-            if t == 1:
-                w_bytes = tile([P, N], U8, "w_bytes", "y1")
-                deal(nc, w_bytes[:].unsqueeze(1), w_bytes_raw[:].unsqueeze(1))
             if t == 0:
                 w_codes = tile([P, 2, N], U32, "w_codes", "y0")
                 deal(nc, w_codes[:], w_raw[:])
-            if t < PACK - 1:
-                for h in range(2):
-                    src = z[t][:, h * HALF : (h + 1) * HALF]
-                    if t < 2:
-                        nc.scalar.copy(out=z_grouped[h][:, :, t], in_=src)
-                    else:
-                        nc.scalar.copy(out=z_grouped[h][:, :, 2:4], in_=src.unsqueeze(2).to_broadcast([P, HALF, 2]))
+            for h in range(2):
+                src = z[t][:, h * HALF : (h + 1) * HALF]
+                if t < 2:
+                    nc.scalar.copy(out=z_grouped[h][:, :, t], in_=src)
+                else:
+                    nc.scalar.copy(out=z_grouped[h][:, :, 2:4], in_=src.unsqueeze(2).to_broadcast([P, HALF, 2]))
+        nc.vector.tensor_copy(out=z[3][:].indirect(where_sb[:, : S // 32]), in_=y[3][:, : S // 2])
+        w_bytes = tile([P, N], U8, "w_bytes", "y2")
+        deal(nc, w_bytes[:].unsqueeze(1), w_bytes_raw[:].unsqueeze(1))
+        nc.vector.tensor_copy(out=z[3][:].indirect(where_sb[:, S // 32 :]), in_=y[3][:, S // 2 :])
 
-        acc = [[psum.tile([P, HALF], F32, name=f"acc{h}{t}", tag=f"bank{PACK * h + t}") for t in range(PACK)] for h in range(2)]
-        for h in range(2):
-            for t in range(PACK):
-                cols = slice(t * P, (t + 1) * P)
-                nc.tensor.matmul_mx(
-                    out=acc[h][t][:],
-                    lhsT=w_codes[:, 1, cols].bitcast(FP8X4),
-                    lhsT_scale=w_bytes[W3_ROW:P, cols],
-                    rhs=skip_codes[h][:].bitcast(FP8X4),
-                    rhs_scale=skip_bytes[:, h * HALF : (h + 1) * HALF],
-                    start=True,
-                    stop=False,
-                )
+        acc = [
+            [psum.tile([P, 2, QUARTER], F32, name=f"acc{c}{u}", tag=f"bank{2 * c + u}") for u in range(2)]
+            for c in range(4)
+        ]
+
+        def skip_pass(c, t):
+            cols = slice(t * P, (t + 1) * P)
+            nc.tensor.matmul_mx(
+                out=acc[c][t // 2][:, t % 2, :],
+                lhsT=w_codes[:, 1, cols].bitcast(FP8X4),
+                lhsT_scale=w_bytes[W3_ROW:P, cols],
+                rhs=skip_codes[c // 2][:, (c % 2) * QUARTER : (c % 2 + 1) * QUARTER].bitcast(FP8X4),
+                rhs_scale=skip_bytes[:, c * QUARTER : (c + 1) * QUARTER],
+                start=True,
+                stop=False,
+            )
+
+        for c in range(4):
+            for u in range(2):
+                skip_pass(c, 2 * u)
 
         nc.vector.tensor_copy(out=z_grouped[0][:, :, 3], in_=z[3][:, 0:HALF])
         nc.scalar.copy(out=z_grouped[1][:, :, 3], in_=z[3][:, HALF:U])
-        for h in range(2):
-            z_codes = tile([P, HALF], U32, f"z_codes{h}")
-            z_bytes = tile([P, HALF], U8, f"z_bytes{h}")
+        for c in range(4):
+            part = slice((c % 2) * QUARTER, (c % 2 + 1) * QUARTER)
+            z_codes = tile([P, QUARTER], U32, f"z_codes{c}")
+            z_bytes = tile([P, QUARTER], U8, f"z_bytes{c}")
             nc.vector.quantize_mx(
-                out=z_codes[:].bitcast(FP8X4), scales=z_bytes[:], in_=z_grouped[h][:].rearrange("p c t -> p (c t)")
+                out=z_codes[:].bitcast(FP8X4),
+                scales=z_bytes[:],
+                in_=z_grouped[c // 2][:, part, :].rearrange("p c t -> p (c t)"),
             )
             for t in range(PACK):
                 cols = slice(t * P, (t + 1) * P)
+                if t % 2 == 1:
+                    skip_pass(c, t)
                 nc.tensor.matmul_mx(
-                    out=acc[h][t][:],
+                    out=acc[c][t // 2][:, t % 2, :],
                     lhsT=w_codes[:, 0, cols].bitcast(FP8X4),
                     lhsT_scale=w_bytes[:, cols],
                     rhs=z_codes[:].bitcast(FP8X4),
@@ -184,28 +200,38 @@ def tile_picked_segunpool_relu_po_kernel(
 
         out_rows = out_0.rearrange("(p t) w -> p t w", t=PACK)
         out_bytes = tile([P, U], U8, "out_bytes")
-        for h in range(2):
-            cells = slice(h * HALF, (h + 1) * HALF)
-            result = tile([P, PACK, HALF], F32, f"result{h}")
-            for t in range(PACK):
-                if h == 0 and t >= 2:
-                    nc.vector.tensor_copy(out=result[:, t, :], in_=acc[h][t][:])
+        out_codes = [tile([P, HALF], U32, f"out_codes{h}") for h in range(2)]
+        for c in range(4):
+            cells = slice(c * QUARTER, (c + 1) * QUARTER)
+            result = tile([P, PACK, QUARTER], F32, f"result{c}")
+            for u in range(2):
+                pair = slice(2 * u, 2 * u + 2)
+                if u == 1 and c == 0:
+                    nc.vector.tensor_copy(out=result[:, pair, :], in_=acc[c][u][:])
                 else:
-                    nc.scalar.copy(out=result[:, t, :], in_=acc[h][t][:])
-                nc.sync.dma_start(out=out_rows[:, t, cells], in_=result[:, t, :])
-            grouped = tile([P, HALF, PACK], BF16, f"out_grouped{h}")
+                    nc.scalar.copy(out=result[:, pair, :], in_=acc[c][u][:])
+                if c in (0, 3):
+                    nc.sync.dma_start(out=out_rows[:, pair, cells], in_=result[:, pair, :])
+            if c in (1, 2):
+                nc.sync.dma_start(out=out_rows[:, :, cells], in_=result[:])
+            grouped = tile([P, QUARTER, PACK], BF16, f"out_grouped{c}")
             src = result[:].rearrange("p t (c i) -> p c t i", i=4)
             dst = grouped[:].rearrange("p (c i) t -> p c t i", i=4)
-            split = SCALAR_CELLS // 4 if h == 1 else 0
+            split = SCALAR_CELLS // 4 if c == 3 else 0
             if split:
                 nc.scalar.copy(out=dst[:, :split], in_=src[:, :split])
             nc.vector.tensor_copy(out=dst[:, split:], in_=src[:, split:])
-            out_codes = tile([P, HALF], U32, f"out_codes{h}")
+            part = slice((c % 2) * QUARTER, (c % 2 + 1) * QUARTER)
             nc.vector.quantize_mx(
-                out=out_codes[:].bitcast(FP8X4), scales=out_bytes[:, cells], in_=grouped[:].rearrange("p c t -> p (c t)")
+                out=out_codes[c // 2][:, part].bitcast(FP8X4),
+                scales=out_bytes[:, cells],
+                in_=grouped[:].rearrange("p c t -> p (c t)"),
             )
-            queue = nc.scalar if h == 1 else nc.sync
-            queue.dma_start(out=words_view(out_1)[:, cells], in_=out_codes[:].bitcast(I32))
+            if c % 2 == 1:
+                queue = nc.scalar if c == 3 else nc.sync
+                queue.dma_start(
+                    out=words_view(out_1)[:, (c - 1) * QUARTER : (c + 1) * QUARTER], in_=out_codes[c // 2][:].bitcast(I32)
+                )
         for q in range(4):
             nc.sync.dma_start(
                 out=out_2[0, 4 * q : 4 * q + 4, :].bitcast(I32), in_=out_bytes[32 * q : 32 * q + 4, :].bitcast(I32)

@@ -19,25 +19,25 @@ PACK = 4
 HALF = U // 2
 W3_ROW = 4
 QUARTER = U // 4
-SCALAR_CELLS = 80
+SCALAR_CELLS = 64
 
 
 def words_view(dram):
     return dram[0].rearrange("p c r -> p (c r)").bitcast(I32)
 
 
-def load_scale_rows(nc, tile, first_row, dram):
+def load_scale_rows(queues, tile, first_row, dram):
     for q in range(4):
-        nc.sync.dma_start(
+        queues[q % len(queues)].dma_start(
             out=tile[32 * q + first_row : 32 * q + first_row + 4, :].bitcast(I32),
             in_=dram[0, 4 * q : 4 * q + 4, :].bitcast(I32),
         )
 
 
-def deal(nc, out, in_):
-    nc.vector.tensor_copy(
-        out=out.rearrange("p w (t m) -> p w m t", t=PACK),
-        in_=in_.rearrange("p w (m t) -> p w m t", t=PACK),
+def deal(engine, out, in_, run):
+    engine.tensor_copy(
+        out=out.rearrange("p w (t b i) -> p w b t i", t=PACK, i=run),
+        in_=in_.rearrange("p w (b i t) -> p w b t i", t=PACK, i=run),
     )
 
 
@@ -75,13 +75,13 @@ def tile_picked_segunpool_relu_po_kernel(
         nc.sync.dma_start(offs_sb[:], offs)
         nc.sync.dma_start(skip_sb[:], skip)
         nc.sync.dma_start(where_sb[:], where)
-        load_scale_rows(nc, x_bytes, 0, x_scales)
+        load_scale_rows((nc.sync, nc.scalar), x_bytes, 0, x_scales)
         nc.sync.dma_start(out=x_codes[:].bitcast(I32), in_=words_view(x_words))
-        load_scale_rows(nc, w_bytes_raw, W3_ROW, w3_scales)
+        load_scale_rows((nc.sync,), w_bytes_raw, W3_ROW, w3_scales)
         for a in range(2):
             cols = slice(a * H // 2, (a + 1) * H // 2)
             nc.sync.dma_start(out=w1_raw[a][:], in_=w1.rearrange("(p j) h -> p j h", j=PACK)[:, :, cols])
-        load_scale_rows(nc, w_bytes_raw, 0, w2_scales)
+        load_scale_rows((nc.sync,), w_bytes_raw, 0, w2_scales)
         nc.sync.dma_start(out=w_raw[:, 0, :].bitcast(I32), in_=words_view(w2_words))
         nc.sync.dma_start(out=w_raw[:, 1, :].bitcast(I32), in_=words_view(w3_words))
 
@@ -140,7 +140,7 @@ def tile_picked_segunpool_relu_po_kernel(
             nc.vector.tensor_copy(out=z[t][:].indirect(where_sb[:]), in_=y[t][:])
             if t == 0:
                 w_codes = tile([P, 2, N], U32, "w_codes", "y0")
-                deal(nc, w_codes[:], w_raw[:])
+                deal(nc.gpsimd, w_codes[:], w_raw[:], 4)
             for h in range(2):
                 src = z[t][:, h * HALF : (h + 1) * HALF]
                 if t < 2:
@@ -149,7 +149,7 @@ def tile_picked_segunpool_relu_po_kernel(
                     nc.scalar.copy(out=z_grouped[h][:, :, 2:4], in_=src.unsqueeze(2).to_broadcast([P, HALF, 2]))
         nc.vector.tensor_copy(out=z[3][:].indirect(where_sb[:, : S // 32]), in_=y[3][:, : S // 2])
         w_bytes = tile([P, N], U8, "w_bytes", "y2")
-        deal(nc, w_bytes[:].unsqueeze(1), w_bytes_raw[:].unsqueeze(1))
+        deal(nc.vector, w_bytes[:].unsqueeze(1), w_bytes_raw[:].unsqueeze(1), 16)
         nc.vector.tensor_copy(out=z[3][:].indirect(where_sb[:, S // 32 :]), in_=y[3][:, S // 2 :])
 
         acc = [
@@ -227,12 +227,12 @@ def tile_picked_segunpool_relu_po_kernel(
                 scales=out_bytes[:, cells],
                 in_=grouped[:].rearrange("p c t -> p (c t)"),
             )
-            if c % 2 == 1:
+            if c == 1:
+                nc.sync.dma_start(out=words_view(out_1)[:, :HALF], in_=out_codes[0][:].bitcast(I32))
+            if c > 1:
                 queue = nc.scalar if c == 3 else nc.sync
-                queue.dma_start(
-                    out=words_view(out_1)[:, (c - 1) * QUARTER : (c + 1) * QUARTER], in_=out_codes[c // 2][:].bitcast(I32)
-                )
+                queue.dma_start(out=words_view(out_1)[:, cells], in_=out_codes[1][:, part].bitcast(I32))
         for q in range(4):
-            nc.sync.dma_start(
+            (nc.sync if q < 3 else nc.scalar).dma_start(
                 out=out_2[0, 4 * q : 4 * q + 4, :].bitcast(I32), in_=out_bytes[32 * q : 32 * q + 4, :].bitcast(I32)
             )

@@ -19,7 +19,8 @@ PACK = 4
 HALF = U // 2
 W3_ROW = 4
 QUARTER = U // 4
-SCALAR_CELLS = 64
+SCALAR_CELLS = 128
+PIECE = 64
 
 
 def words_view(dram):
@@ -132,8 +133,13 @@ def tile_picked_segunpool_relu_po_kernel(
                 start=True,
                 stop=True,
             )
-            y.append(tile([P, S], F32, f"y{t}"))
-            nc.scalar.activation(out=y[t][:], in_=acc[:], func=ACT.Relu)
+            if t < PACK - 1:
+                y.append(tile([P, S], F32, f"y{t}"))
+                nc.scalar.activation(out=y[t][:], in_=acc[:], func=ACT.Relu)
+            else:
+                for a in range(2):
+                    y.append(tile([P, S // 2], F32, f"y{t + a}"))
+                    nc.scalar.activation(out=y[t + a][:], in_=acc[:, a * S // 2 : (a + 1) * S // 2], func=ACT.Relu)
 
         z_grouped = [tile([P, HALF, PACK], BF16, f"z_grouped{h}") for h in range(2)]
         for t in range(PACK - 1):
@@ -147,10 +153,10 @@ def tile_picked_segunpool_relu_po_kernel(
                     nc.scalar.copy(out=z_grouped[h][:, :, t], in_=src)
                 else:
                     nc.scalar.copy(out=z_grouped[h][:, :, 2:4], in_=src.unsqueeze(2).to_broadcast([P, HALF, 2]))
-        nc.vector.tensor_copy(out=z[3][:].indirect(where_sb[:, : S // 32]), in_=y[3][:, : S // 2])
-        w_bytes = tile([P, N], U8, "w_bytes", "y2")
+        nc.vector.tensor_copy(out=z[3][:].indirect(where_sb[:, : S // 32]), in_=y[3][:])
+        w_bytes = tile([P, N], U8, "w_bytes", "y3")
         deal(nc.vector, w_bytes[:].unsqueeze(1), w_bytes_raw[:].unsqueeze(1), 16)
-        nc.vector.tensor_copy(out=z[3][:].indirect(where_sb[:, S // 32 :]), in_=y[3][:, S // 2 :])
+        nc.vector.tensor_copy(out=z[3][:].indirect(where_sb[:, S // 32 :]), in_=y[4][:])
 
         acc = [
             [psum.tile([P, 2, QUARTER], F32, name=f"acc{c}{u}", tag=f"bank{2 * c + u}") for u in range(2)]
@@ -173,10 +179,12 @@ def tile_picked_segunpool_relu_po_kernel(
             for u in range(2):
                 skip_pass(c, 2 * u)
 
-        nc.vector.tensor_copy(out=z_grouped[0][:, :, 3], in_=z[3][:, 0:HALF])
-        nc.scalar.copy(out=z_grouped[1][:, :, 3], in_=z[3][:, HALF:U])
         for c in range(4):
             part = slice((c % 2) * QUARTER, (c % 2 + 1) * QUARTER)
+            copy = nc.vector.tensor_copy if c in (0, 3) else nc.scalar.copy
+            width = PIECE if c == 3 else QUARTER
+            for first in range(c * QUARTER, (c + 1) * QUARTER, width):
+                copy(out=z_grouped[c // 2][:, first % HALF : first % HALF + width, 3], in_=z[3][:, first : first + width])
             z_codes = tile([P, QUARTER], U32, f"z_codes{c}")
             z_bytes = tile([P, QUARTER], U8, f"z_bytes{c}")
             nc.vector.quantize_mx(
@@ -200,20 +208,17 @@ def tile_picked_segunpool_relu_po_kernel(
 
         out_rows = out_0.rearrange("(p t) w -> p t w", t=PACK)
         out_bytes = tile([P, U], U8, "out_bytes")
-        out_codes = [tile([P, HALF], U32, f"out_codes{h}") for h in range(2)]
+        out_codes = tile([P, U], U32, "out_codes")
         for c in range(4):
             cells = slice(c * QUARTER, (c + 1) * QUARTER)
             result = tile([P, PACK, QUARTER], F32, f"result{c}")
             for u in range(2):
                 pair = slice(2 * u, 2 * u + 2)
-                if u == 1 and c == 0:
+                if u == 1 and c < 2:
                     nc.vector.tensor_copy(out=result[:, pair, :], in_=acc[c][u][:])
                 else:
                     nc.scalar.copy(out=result[:, pair, :], in_=acc[c][u][:])
-                if c in (0, 3):
-                    nc.sync.dma_start(out=out_rows[:, pair, cells], in_=result[:, pair, :])
-            if c in (1, 2):
-                nc.sync.dma_start(out=out_rows[:, :, cells], in_=result[:])
+                nc.sync.dma_start(out=out_rows[:, pair, cells], in_=result[:, pair, :])
             grouped = tile([P, QUARTER, PACK], BF16, f"out_grouped{c}")
             src = result[:].rearrange("p t (c i) -> p c t i", i=4)
             dst = grouped[:].rearrange("p (c i) t -> p c t i", i=4)
@@ -221,17 +226,14 @@ def tile_picked_segunpool_relu_po_kernel(
             if split:
                 nc.scalar.copy(out=dst[:, :split], in_=src[:, :split])
             nc.vector.tensor_copy(out=dst[:, split:], in_=src[:, split:])
-            part = slice((c % 2) * QUARTER, (c % 2 + 1) * QUARTER)
             nc.vector.quantize_mx(
-                out=out_codes[c // 2][:, part].bitcast(FP8X4),
+                out=out_codes[:, cells].bitcast(FP8X4),
                 scales=out_bytes[:, cells],
                 in_=grouped[:].rearrange("p c t -> p (c t)"),
             )
-            if c == 1:
-                nc.sync.dma_start(out=words_view(out_1)[:, :HALF], in_=out_codes[0][:].bitcast(I32))
-            if c > 1:
-                queue = nc.scalar if c == 3 else nc.sync
-                queue.dma_start(out=words_view(out_1)[:, cells], in_=out_codes[1][:, part].bitcast(I32))
+        last = U - QUARTER
+        nc.sync.dma_start(out=words_view(out_1)[:, :last], in_=out_codes[:, :last].bitcast(I32))
+        nc.scalar.dma_start(out=words_view(out_1)[:, last:], in_=out_codes[:, last:].bitcast(I32))
         for q in range(4):
             (nc.sync if q < 3 else nc.scalar).dma_start(
                 out=out_2[0, 4 * q : 4 * q + 4, :].bitcast(I32), in_=out_bytes[32 * q : 32 * q + 4, :].bitcast(I32)

@@ -60,46 +60,49 @@ def tile_picked_segunpool_relu_po_kernel(
         x_bytes = tile([P, T], U8, "x_bytes")
         w_bytes_raw = tile([P, N], U8, "w_bytes_raw")
 
-        nc.vector.memset(x_bytes[:].bitcast(I32), 0)
+        nc.gpsimd.memset(x_bytes[:].bitcast(I32), 0)
         with tc.tile_pool(name="early", bufs=1) as early:
             zeros = early.tile([P, N // 4], I32, name="zeros")
             nc.vector.memset(zeros[:], 0)
             nc.vector.tensor_copy(out=w_bytes_raw[:].bitcast(I32), in_=zeros[:])
+        warm = tile([P, 2], F32, "warm")
+        nc.vector.memset(warm[:, 0:1], 0.0)
+        nc.scalar.activation(out=warm[:, 1:2], in_=warm[:, 0:1], func=ACT.Relu)
         loads = ctx.enter_context(tc.tile_pool(name="loads", bufs=1))
         x_codes = loads.tile([P, T], U32, name="x_codes")
         w1_raw = [loads.tile([P, PACK, H // 2], F32, name=f"w1_raw{a}") for a in range(2)]
         w_raw = loads.tile([P, 2, N], U32, name="w_raw")
-        z = [loads.tile([P, U], F32, name=f"z{t}") for t in range(PACK)]
-        for t in range(PACK):
-            nc.gpsimd.memset(z[t][:], 0.0)
+        z = [loads.tile([P, U], F32, name=f"z{t}", align_bytes=64) for t in range(PACK)]
 
         nc.sync.dma_start(offs_sb[:], offs)
         nc.sync.dma_start(skip_sb[:], skip)
         nc.sync.dma_start(where_sb[:], where)
-        load_scale_rows((nc.sync, nc.scalar), x_bytes, 0, x_scales)
+        load_scale_rows((nc.sync,), x_bytes, 0, x_scales)
         nc.sync.dma_start(out=x_codes[:].bitcast(I32), in_=words_view(x_words))
-        load_scale_rows((nc.sync,), w_bytes_raw, W3_ROW, w3_scales)
         for a in range(2):
             cols = slice(a * H // 2, (a + 1) * H // 2)
             nc.sync.dma_start(out=w1_raw[a][:], in_=w1.rearrange("(p j) h -> p j h", j=PACK)[:, :, cols])
-        load_scale_rows((nc.sync,), w_bytes_raw, 0, w2_scales)
         nc.sync.dma_start(out=w_raw[:, 0, :].bitcast(I32), in_=words_view(w2_words))
         nc.sync.dma_start(out=w_raw[:, 1, :].bitcast(I32), in_=words_view(w3_words))
+        load_scale_rows((nc.sync,), w_bytes_raw, W3_ROW, w3_scales)
+        load_scale_rows((nc.sync,), w_bytes_raw, 0, w2_scales)
 
         picked_bytes = tile([P, S], U8, "picked_bytes")
-        skip_bytes = tile([P, U], U8, "skip_bytes")
+        last = U - QUARTER
+        skip_bytes = tile([P, last], U8, "skip_bytes")
         picked_codes = tile([P, S], U32, "picked_codes")
         nc.vector.tensor_copy(out=picked_bytes[:], in_=x_bytes[:].indirect(offs_sb[:]))
-        nc.vector.tensor_copy(out=skip_bytes[:], in_=x_bytes[:].indirect(skip_sb[:]))
+        nc.vector.tensor_copy(out=skip_bytes[:], in_=x_bytes[:].indirect(skip_sb[:, : last // 16]))
         nc.vector.tensor_copy(out=picked_codes[:], in_=x_codes[:].indirect(offs_sb[:]))
 
-        def gather_skip_codes(h, tag):
-            codes = tile([P, HALF], U32, f"skip_codes{h}", tag)
-            cols = slice(h * HALF // 16, (h + 1) * HALF // 16)
+        def gather_skip_codes(first, count, tag):
+            codes = tile([P, count], U32, f"skip_codes{first}", tag)
+            cols = slice(first // 16, (first + count) // 16)
             nc.vector.tensor_copy(out=codes[:], in_=x_codes[:].indirect(skip_sb[:, cols]))
             return codes
 
-        skip_codes = [gather_skip_codes(0, None)]
+        skip_codes = [None, gather_skip_codes(QUARTER, HALF, None), None]
+        skip_scales = [skip_bytes[:, :QUARTER], skip_bytes[:, QUARTER:], None]
 
         w1_codes, w1_bytes = [], []
         for u in range(2):
@@ -118,120 +121,158 @@ def tile_picked_segunpool_relu_po_kernel(
             w1_codes.append(codes)
             w1_bytes.append(scale)
             if u == 0:
-                skip_codes.append(gather_skip_codes(1, "w1_grouped0"))
+                skip_codes[0] = gather_skip_codes(0, QUARTER, "w1_grouped0")
 
-        y = []
         for t in range(PACK):
+            nc.gpsimd.memset(z[t][:], 0.0)
+
+        def project(t, part, bank, name):
             cols = slice((t % 2) * P, (t % 2 + 1) * P)
-            acc = psum.tile([P, S], F32, name=f"y_acc{t}", tag=f"bank{PACK + t}")
+            width = part.stop - part.start
+            acc = psum.tile([P, width], F32, name=f"acc_{name}", tag=f"bank{bank}")
             nc.tensor.matmul_mx(
                 out=acc[:],
                 lhsT=w1_codes[t // 2][:, cols].bitcast(FP8X4),
                 lhsT_scale=w1_bytes[t // 2][:, cols],
-                rhs=picked_codes[:].bitcast(FP8X4),
-                rhs_scale=picked_bytes[:],
+                rhs=picked_codes[:, part].bitcast(FP8X4),
+                rhs_scale=picked_bytes[:, part],
                 start=True,
                 stop=True,
             )
-            if t < PACK - 1:
-                y.append(tile([P, S], F32, f"y{t}"))
-                nc.scalar.activation(out=y[t][:], in_=acc[:], func=ACT.Relu)
-            else:
-                for a in range(2):
-                    y.append(tile([P, S // 2], F32, f"y{t + a}"))
-                    nc.scalar.activation(out=y[t + a][:], in_=acc[:, a * S // 2 : (a + 1) * S // 2], func=ACT.Relu)
+            values = tile([P, width], F32, name)
+            nc.scalar.activation(out=values[:], in_=acc[:], func=ACT.Relu)
+            return values
 
-        z_grouped = [tile([P, HALF, PACK], BF16, f"z_grouped{h}") for h in range(2)]
-        for t in range(PACK - 1):
-            nc.vector.tensor_copy(out=z[t][:].indirect(where_sb[:]), in_=y[t][:])
+        y_first = project(0, slice(0, S // 2), 0, "y_first")
+        y = [project(0, slice(S // 2, S), PACK, "y0")]
+        y.extend(project(t, slice(0, S), PACK + t, f"y{t}") for t in range(1, PACK))
+
+        z_grouped = tile([P, U, PACK], BF16, "z_grouped")
+        for t in range(PACK):
+            if t == 0:
+                nc.vector.tensor_copy(out=z[t][:].indirect(where_sb[:, : S // 32]), in_=y_first[:])
+                nc.vector.tensor_copy(out=z[t][:].indirect(where_sb[:, S // 32 :]), in_=y[t][:])
+            else:
+                nc.vector.tensor_copy(out=z[t][:].indirect(where_sb[:]), in_=y[t][:])
             if t == 0:
                 w_codes = tile([P, 2, N], U32, "w_codes", "y0")
                 deal(nc.gpsimd, w_codes[:], w_raw[:], 4)
-            for h in range(2):
-                src = z[t][:, h * HALF : (h + 1) * HALF]
-                if t < 2:
-                    nc.scalar.copy(out=z_grouped[h][:, :, t], in_=src)
-                else:
-                    nc.scalar.copy(out=z_grouped[h][:, :, 2:4], in_=src.unsqueeze(2).to_broadcast([P, HALF, 2]))
-        nc.vector.tensor_copy(out=z[3][:].indirect(where_sb[:, : S // 32]), in_=y[3][:])
-        w_bytes = tile([P, N], U8, "w_bytes", "y3")
-        deal(nc.vector, w_bytes[:].unsqueeze(1), w_bytes_raw[:].unsqueeze(1), 16)
-        nc.vector.tensor_copy(out=z[3][:].indirect(where_sb[:, S // 32 :]), in_=y[4][:])
+            if t == 2:
+                w_bytes = tile([P, N], U8, "w_bytes", "y2")
+                deal(nc.gpsimd, w_bytes[:].unsqueeze(1), w_bytes_raw[:].unsqueeze(1), 16)
+            if t == 3:
+                break
+            if t < 2:
+                nc.scalar.copy(out=z_grouped[:, :, t], in_=z[t][:])
+            else:
+                nc.scalar.copy(out=z_grouped[:, :, 2:4], in_=z[t][:].unsqueeze(2).to_broadcast([P, U, 2]))
 
-        acc = [
-            [psum.tile([P, 2, QUARTER], F32, name=f"acc{c}{u}", tag=f"bank{2 * c + u}") for u in range(2)]
-            for c in range(4)
-        ]
+        pieces = [(0, QUARTER), (QUARTER, HALF), (U - QUARTER, QUARTER)]
 
-        def skip_pass(c, t):
+        def open_bank(i, t):
+            first, width = pieces[i]
+            acc = psum.tile([P, width], F32, name=f"acc{i}{t}", tag=f"bank{PACK * (i % 2) + t}")
             cols = slice(t * P, (t + 1) * P)
             nc.tensor.matmul_mx(
-                out=acc[c][t // 2][:, t % 2, :],
+                out=acc[:],
                 lhsT=w_codes[:, 1, cols].bitcast(FP8X4),
                 lhsT_scale=w_bytes[W3_ROW:P, cols],
-                rhs=skip_codes[c // 2][:, (c % 2) * QUARTER : (c % 2 + 1) * QUARTER].bitcast(FP8X4),
-                rhs_scale=skip_bytes[:, c * QUARTER : (c + 1) * QUARTER],
+                rhs=skip_codes[i][:].bitcast(FP8X4),
+                rhs_scale=skip_scales[i],
                 start=True,
                 stop=False,
             )
+            return acc
 
-        for c in range(4):
-            for u in range(2):
-                skip_pass(c, 2 * u)
+        acc = [[open_bank(i, t) for t in range(PACK)] for i in range(2)]
 
-        for c in range(4):
-            part = slice((c % 2) * QUARTER, (c % 2 + 1) * QUARTER)
-            copy = nc.vector.tensor_copy if c in (0, 3) else nc.scalar.copy
-            width = PIECE if c == 3 else QUARTER
-            for first in range(c * QUARTER, (c + 1) * QUARTER, width):
-                copy(out=z_grouped[c // 2][:, first % HALF : first % HALF + width, 3], in_=z[3][:, first : first + width])
-            z_codes = tile([P, QUARTER], U32, f"z_codes{c}")
-            z_bytes = tile([P, QUARTER], U8, f"z_bytes{c}")
+        z_codes = [tile([P, width], U32, f"z_codes{i}") for i, (first, width) in enumerate(pieces)]
+        z_bytes = [tile([P, width], U8, f"z_bytes{i}") for i, (first, width) in enumerate(pieces)]
+
+        def regroup(copy, c):
+            cells = slice(c * QUARTER, (c + 1) * QUARTER)
+            copy(out=z_grouped[:, cells, 3], in_=z[3][:, cells])
+
+        def quantize_z(i):
+            first, width = pieces[i]
             nc.vector.quantize_mx(
-                out=z_codes[:].bitcast(FP8X4),
-                scales=z_bytes[:],
-                in_=z_grouped[c // 2][:, part, :].rearrange("p c t -> p (c t)"),
+                out=z_codes[i][:].bitcast(FP8X4),
+                scales=z_bytes[i][:],
+                in_=z_grouped[:, first : first + width, :].rearrange("p c t -> p (c t)"),
             )
-            for t in range(PACK):
-                cols = slice(t * P, (t + 1) * P)
-                if t % 2 == 1:
-                    skip_pass(c, t)
-                nc.tensor.matmul_mx(
-                    out=acc[c][t // 2][:, t % 2, :],
-                    lhsT=w_codes[:, 0, cols].bitcast(FP8X4),
-                    lhsT_scale=w_bytes[:, cols],
-                    rhs=z_codes[:].bitcast(FP8X4),
-                    rhs_scale=z_bytes[:],
-                    start=False,
-                    stop=True,
-                )
+
+        regroup(nc.vector.tensor_copy, 0)
+        regroup(nc.scalar.copy, 1)
+        regroup(nc.vector.tensor_copy, 2)
+        quantize_z(0)
+        regroup(nc.vector.tensor_copy, 3)
+        quantize_z(1)
+        last_codes = loads.tile([P, QUARTER], U32, name="last_codes", tag="z2", align_bytes=64)
+        nc.vector.tensor_copy(out=last_codes[:], in_=x_codes[:].indirect(skip_sb[:, last // 16 :]))
+        skip_codes[2] = last_codes
+        last_bytes = loads.tile([P, QUARTER], U8, name="last_bytes", tag="z3", align_bytes=64)
+        nc.vector.tensor_copy(out=last_bytes[:], in_=x_bytes[:].indirect(skip_sb[:, last // 16 :]))
+        skip_scales[2] = last_bytes[:]
+        quantize_z(2)
+
+        def close_bank(i, t, bank):
+            cols = slice(t * P, (t + 1) * P)
+            nc.tensor.matmul_mx(
+                out=bank[:],
+                lhsT=w_codes[:, 0, cols].bitcast(FP8X4),
+                lhsT_scale=w_bytes[:, cols],
+                rhs=z_codes[i][:].bitcast(FP8X4),
+                rhs_scale=z_bytes[i][:],
+                start=False,
+                stop=True,
+            )
 
         out_rows = out_0.rearrange("(p t) w -> p t w", t=PACK)
         out_bytes = tile([P, U], U8, "out_bytes")
         out_codes = tile([P, U], U32, "out_codes")
-        for c in range(4):
+        result = [tile([P, PACK, width], F32, f"result{i}") for i, (first, width) in enumerate(pieces)]
+        grouped = [tile([P, QUARTER, PACK], BF16, f"out_grouped{c}") for c in range(4)]
+
+        def empty(i, t, copy):
+            first, width = pieces[i]
+            cells = slice(first, first + width)
+            bank = acc[i][t] if i < 2 else open_bank(i, t)
+            close_bank(i, t, bank)
+            copy(out=result[i][:, t, :], in_=bank[:])
+            if i < 2:
+                nc.sync.dma_start(out=out_rows[:, t, cells], in_=result[i][:, t, :])
+            elif t % 2 == 1:
+                nc.sync.dma_start(out=out_rows[:, t - 1 : t + 1, cells], in_=result[i][:, t - 1 : t + 1, :])
+
+        def interleave(c, i, at, copy, lo, hi):
+            src = result[i][:, :, at + lo : at + hi].rearrange("p t (c i) -> p c t i", i=4)
+            dst = grouped[c][:, lo:hi, :].rearrange("p (c i) t -> p c t i", i=4)
+            copy(out=dst, in_=src)
+
+        def quantize_out(c):
             cells = slice(c * QUARTER, (c + 1) * QUARTER)
-            result = tile([P, PACK, QUARTER], F32, f"result{c}")
-            for u in range(2):
-                pair = slice(2 * u, 2 * u + 2)
-                if u == 1 and c < 2:
-                    nc.vector.tensor_copy(out=result[:, pair, :], in_=acc[c][u][:])
-                else:
-                    nc.scalar.copy(out=result[:, pair, :], in_=acc[c][u][:])
-                nc.sync.dma_start(out=out_rows[:, pair, cells], in_=result[:, pair, :])
-            grouped = tile([P, QUARTER, PACK], BF16, f"out_grouped{c}")
-            src = result[:].rearrange("p t (c i) -> p c t i", i=4)
-            dst = grouped[:].rearrange("p (c i) t -> p c t i", i=4)
-            split = SCALAR_CELLS // 4 if c == 3 else 0
-            if split:
-                nc.scalar.copy(out=dst[:, :split], in_=src[:, :split])
-            nc.vector.tensor_copy(out=dst[:, split:], in_=src[:, split:])
             nc.vector.quantize_mx(
                 out=out_codes[:, cells].bitcast(FP8X4),
                 scales=out_bytes[:, cells],
-                in_=grouped[:].rearrange("p c t -> p (c t)"),
+                in_=grouped[c][:].rearrange("p c t -> p (c t)"),
             )
-        last = U - QUARTER
+
+        on_s, on_v = nc.scalar.copy, nc.vector.tensor_copy
+        for t in range(PACK):
+            empty(0, t, on_s)
+        interleave(0, 0, 0, on_v, 0, QUARTER)
+        for t in range(PACK):
+            empty(1, t, on_v if t == 1 else on_s)
+        quantize_out(0)
+        interleave(1, 1, 0, on_v, 0, QUARTER)
+        interleave(2, 1, QUARTER, on_v, 0, QUARTER)
+        quantize_out(1)
+        for t in range(PACK):
+            empty(2, t, on_s)
+        interleave(3, 2, 0, on_s, 0, SCALAR_CELLS)
+        interleave(3, 2, 0, on_v, SCALAR_CELLS, QUARTER)
+        quantize_out(2)
+        quantize_out(3)
         nc.sync.dma_start(out=words_view(out_1)[:, :last], in_=out_codes[:, :last].bitcast(I32))
         nc.scalar.dma_start(out=words_view(out_1)[:, last:], in_=out_codes[:, last:].bitcast(I32))
         for q in range(4):

@@ -72,7 +72,8 @@ def tile_picked_segunpool_relu_po_kernel(
         x_codes = loads.tile([P, T], U32, name="x_codes")
         w1_raw = [loads.tile([P, PACK, H // 2], F32, name=f"w1_raw{a}") for a in range(2)]
         w_raw = loads.tile([P, 2, N], U32, name="w_raw")
-        z = [loads.tile([P, U], F32, name=f"z{t}", align_bytes=64) for t in range(PACK)]
+        z = [loads.tile([P, U], F32, name=f"z{t}", align_bytes=64) for t in range(PACK - 1)]
+        z.append(z[2])
 
         nc.sync.dma_start(offs_sb[:], offs)
         nc.sync.dma_start(skip_sb[:], skip)
@@ -104,8 +105,8 @@ def tile_picked_segunpool_relu_po_kernel(
         skip_codes = [None, gather_skip_codes(QUARTER, HALF, None), None]
         skip_scales = [skip_bytes[:, :QUARTER], skip_bytes[:, QUARTER:], None]
 
-        w1_codes, w1_bytes = [], []
-        for u in range(2):
+        w1_codes, w1_bytes = {}, {}
+        for u in (1, 0):
             grouped = tile([P, 2, P, PACK], BF16, f"w1_grouped{u}")
             for a in range(2):
                 nc.scalar.activation(
@@ -118,12 +119,12 @@ def tile_picked_segunpool_relu_po_kernel(
             nc.vector.quantize_mx(
                 out=codes[:].bitcast(FP8X4), scales=scale[:], in_=grouped[:].rearrange("p t m j -> p (t m j)")
             )
-            w1_codes.append(codes)
-            w1_bytes.append(scale)
-            if u == 0:
-                skip_codes[0] = gather_skip_codes(0, QUARTER, "w1_grouped0")
+            w1_codes[u] = codes
+            w1_bytes[u] = scale
+            if u == 1:
+                skip_codes[0] = gather_skip_codes(0, QUARTER, "w1_grouped1")
 
-        for t in range(PACK):
+        for t in (2, 0, 1):
             nc.gpsimd.memset(z[t][:], 0.0)
 
         def project(t, part, bank, name):
@@ -143,29 +144,25 @@ def tile_picked_segunpool_relu_po_kernel(
             nc.scalar.activation(out=values[:], in_=acc[:], func=ACT.Relu)
             return values
 
-        y_first = project(0, slice(0, S // 2), 0, "y_first")
-        y = [project(0, slice(S // 2, S), PACK, "y0")]
-        y.extend(project(t, slice(0, S), PACK + t, f"y{t}") for t in range(1, PACK))
+        y_first = project(2, slice(0, S // 2), 0, "y_first")
+        y = {2: project(2, slice(S // 2, S), PACK + 2, "y2")}
+        for t in (0, 1, 3):
+            y[t] = project(t, slice(0, S), PACK + t, f"y{t}")
 
         z_grouped = tile([P, U, PACK], BF16, "z_grouped")
-        for t in range(PACK):
-            if t == 0:
+        for t in (2, 0, 1, 3):
+            if t == 2:
                 nc.vector.tensor_copy(out=z[t][:].indirect(where_sb[:, : S // 32]), in_=y_first[:])
                 nc.vector.tensor_copy(out=z[t][:].indirect(where_sb[:, S // 32 :]), in_=y[t][:])
+                w_codes = tile([P, 2, N], U32, "w_codes", "y2")
+                deal(nc.gpsimd, w_codes[:], w_raw[:], 4)
             else:
                 nc.vector.tensor_copy(out=z[t][:].indirect(where_sb[:]), in_=y[t][:])
-            if t == 0:
-                w_codes = tile([P, 2, N], U32, "w_codes", "y0")
-                deal(nc.gpsimd, w_codes[:], w_raw[:], 4)
-            if t == 2:
-                w_bytes = tile([P, N], U8, "w_bytes", "y2")
+            if t == 1:
+                w_bytes = tile([P, N], U8, "w_bytes", "y1")
                 deal(nc.gpsimd, w_bytes[:].unsqueeze(1), w_bytes_raw[:].unsqueeze(1), 16)
-            if t == 3:
-                break
-            if t < 2:
+            if t < 3:
                 nc.scalar.copy(out=z_grouped[:, :, t], in_=z[t][:])
-            else:
-                nc.scalar.copy(out=z_grouped[:, :, 2:4], in_=z[t][:].unsqueeze(2).to_broadcast([P, U, 2]))
 
         pieces = [(0, QUARTER), (QUARTER, HALF), (U - QUARTER, QUARTER)]
 
@@ -189,8 +186,8 @@ def tile_picked_segunpool_relu_po_kernel(
         z_codes = [tile([P, width], U32, f"z_codes{i}") for i, (first, width) in enumerate(pieces)]
         z_bytes = [tile([P, width], U8, f"z_bytes{i}") for i, (first, width) in enumerate(pieces)]
 
-        def regroup(copy, c):
-            cells = slice(c * QUARTER, (c + 1) * QUARTER)
+        def regroup(copy, lo, hi):
+            cells = slice(lo, hi)
             copy(out=z_grouped[:, cells, 3], in_=z[3][:, cells])
 
         def quantize_z(i):
@@ -201,16 +198,16 @@ def tile_picked_segunpool_relu_po_kernel(
                 in_=z_grouped[:, first : first + width, :].rearrange("p c t -> p (c t)"),
             )
 
-        regroup(nc.vector.tensor_copy, 0)
-        regroup(nc.scalar.copy, 1)
-        regroup(nc.vector.tensor_copy, 2)
+        regroup(nc.vector.tensor_copy, 0, QUARTER)
+        regroup(nc.scalar.copy, QUARTER, HALF)
+        regroup(nc.vector.tensor_copy, HALF, last)
+        regroup(nc.scalar.copy, last, U)
         quantize_z(0)
-        regroup(nc.vector.tensor_copy, 3)
         quantize_z(1)
-        last_codes = loads.tile([P, QUARTER], U32, name="last_codes", tag="z2", align_bytes=64)
+        last_codes = loads.tile([P, QUARTER], U32, name="last_codes", tag="z1", align_bytes=64)
         nc.vector.tensor_copy(out=last_codes[:], in_=x_codes[:].indirect(skip_sb[:, last // 16 :]))
         skip_codes[2] = last_codes
-        last_bytes = loads.tile([P, QUARTER], U8, name="last_bytes", tag="z3", align_bytes=64)
+        last_bytes = loads.tile([P, QUARTER], U8, name="last_bytes", tag="z2", align_bytes=64)
         nc.vector.tensor_copy(out=last_bytes[:], in_=x_bytes[:].indirect(skip_sb[:, last // 16 :]))
         skip_scales[2] = last_bytes[:]
         quantize_z(2)

@@ -58,42 +58,54 @@ def tile_picked_segunpool_relu_po_kernel(
         skip_sb = lists.tile([P, U // 16], U16, name="skip_sb")
         where_sb = lists.tile([P, S // 16], U16, name="where_sb")
         x_bytes = tile([P, T], U8, "x_bytes")
-        w_bytes_raw = tile([P, N], U8, "w_bytes_raw")
+        picked_bytes = tile([P, S], U8, "picked_bytes")
 
         nc.gpsimd.memset(x_bytes[:].bitcast(I32), 0)
         with tc.tile_pool(name="early", bufs=1) as early:
             zeros = early.tile([P, N // 4], I32, name="zeros")
             nc.vector.memset(zeros[:], 0)
-            nc.vector.tensor_copy(out=w_bytes_raw[:].bitcast(I32), in_=zeros[:])
+            nc.vector.tensor_copy(out=picked_bytes[:].bitcast(I32), in_=zeros[:])
         warm = tile([P, 2], F32, "warm")
         nc.vector.memset(warm[:, 0:1], 0.0)
         nc.scalar.activation(out=warm[:, 1:2], in_=warm[:, 0:1], func=ACT.Relu)
         loads = ctx.enter_context(tc.tile_pool(name="loads", bufs=1))
         x_codes = loads.tile([P, T], U32, name="x_codes")
         w1_raw = [loads.tile([P, PACK, H // 2], F32, name=f"w1_raw{a}") for a in range(2)]
-        w_raw = loads.tile([P, 2, N], U32, name="w_raw")
         z = [loads.tile([P, U], F32, name=f"z{t}", align_bytes=64) for t in range(PACK - 1)]
         z.append(z[2])
 
         nc.sync.dma_start(offs_sb[:], offs)
         nc.sync.dma_start(skip_sb[:], skip)
         nc.sync.dma_start(where_sb[:], where)
-        load_scale_rows((nc.sync,), x_bytes, 0, x_scales)
+        nc.sync.dma_start(out=x_bytes[0:P:8, :].bitcast(I32), in_=x_scales[0].bitcast(I32))
         nc.sync.dma_start(out=x_codes[:].bitcast(I32), in_=words_view(x_words))
         for a in range(2):
             cols = slice(a * H // 2, (a + 1) * H // 2)
             nc.sync.dma_start(out=w1_raw[a][:], in_=w1.rearrange("(p j) h -> p j h", j=PACK)[:, :, cols])
+
+        def place_rows(dst, src):
+            for q in range(4):
+                nc.sync.dma_start(
+                    out=dst[32 * q : 32 * q + 4, :].bitcast(I32), in_=src[32 * q : 32 * q + 32 : 8, :].bitcast(I32)
+                )
+
+        last = U - QUARTER
+        skip_bytes = tile([P, U], U8, "skip_bytes")
+        nc.vector.memset(skip_bytes[:].bitcast(I32), 0)
+        picked_spread = tile([P, S], U8, "picked_spread", "w_raw")
+        skip_spread = tile([P, U], U8, "skip_spread")
+        picked_codes = tile([P, S], U32, "picked_codes")
+        nc.vector.tensor_copy(out=picked_spread[:], in_=x_bytes[:].indirect(offs_sb[:]))
+        place_rows(picked_bytes, picked_spread)
+        nc.vector.tensor_copy(out=skip_spread[:], in_=x_bytes[:].indirect(skip_sb[:]))
+        place_rows(skip_bytes, skip_spread)
+        w_raw = tile([P, 2, N], U32, "w_raw")
         nc.sync.dma_start(out=w_raw[:, 0, :].bitcast(I32), in_=words_view(w2_words))
         nc.sync.dma_start(out=w_raw[:, 1, :].bitcast(I32), in_=words_view(w3_words))
+        w_bytes_raw = tile([P, N], U8, "w_bytes_raw", "skip_spread")
+        nc.gpsimd.memset(w_bytes_raw[:].bitcast(I32), 0)
         load_scale_rows((nc.sync,), w_bytes_raw, W3_ROW, w3_scales)
         load_scale_rows((nc.sync,), w_bytes_raw, 0, w2_scales)
-
-        picked_bytes = tile([P, S], U8, "picked_bytes")
-        last = U - QUARTER
-        skip_bytes = tile([P, last], U8, "skip_bytes")
-        picked_codes = tile([P, S], U32, "picked_codes")
-        nc.vector.tensor_copy(out=picked_bytes[:], in_=x_bytes[:].indirect(offs_sb[:]))
-        nc.vector.tensor_copy(out=skip_bytes[:], in_=x_bytes[:].indirect(skip_sb[:, : last // 16]))
         nc.vector.tensor_copy(out=picked_codes[:], in_=x_codes[:].indirect(offs_sb[:]))
 
         def gather_skip_codes(first, count, tag):
@@ -103,7 +115,7 @@ def tile_picked_segunpool_relu_po_kernel(
             return codes
 
         skip_codes = [None, gather_skip_codes(QUARTER, HALF, None), None]
-        skip_scales = [skip_bytes[:, :QUARTER], skip_bytes[:, QUARTER:], None]
+        skip_scales = [skip_bytes[:, :QUARTER], skip_bytes[:, QUARTER:last], skip_bytes[:, last:]]
 
         w1_codes, w1_bytes = {}, {}
         for u in (1, 0):
@@ -207,9 +219,6 @@ def tile_picked_segunpool_relu_po_kernel(
         last_codes = loads.tile([P, QUARTER], U32, name="last_codes", tag="z1", align_bytes=64)
         nc.vector.tensor_copy(out=last_codes[:], in_=x_codes[:].indirect(skip_sb[:, last // 16 :]))
         skip_codes[2] = last_codes
-        last_bytes = loads.tile([P, QUARTER], U8, name="last_bytes", tag="z2", align_bytes=64)
-        nc.vector.tensor_copy(out=last_bytes[:], in_=x_bytes[:].indirect(skip_sb[:, last // 16 :]))
-        skip_scales[2] = last_bytes[:]
         quantize_z(2)
 
         def close_bank(i, t, bank):

@@ -20,7 +20,7 @@ HALF = U // 2
 W3_ROW = 4
 QUARTER = U // 4
 SCALAR_CELLS = 128
-PIECE = 64
+ROWS_AT = 112
 
 
 def words_view(dram):
@@ -60,11 +60,11 @@ def tile_picked_segunpool_relu_po_kernel(
         x_bytes = tile([P, T], U8, "x_bytes")
         picked_bytes = tile([P, S], U8, "picked_bytes")
 
-        nc.gpsimd.memset(x_bytes[:].bitcast(I32), 0)
-        with tc.tile_pool(name="early", bufs=1) as early:
-            zeros = early.tile([P, N // 4], I32, name="zeros")
-            nc.vector.memset(zeros[:], 0)
-            nc.vector.tensor_copy(out=picked_bytes[:].bitcast(I32), in_=zeros[:])
+        skip_bytes = tile([P, U], U8, "skip_bytes")
+        nc.gpsimd.memset(x_bytes[:96, :].bitcast(I32), 0)
+        nc.gpsimd.memset(x_bytes[96:ROWS_AT, :].bitcast(I32), 0)
+        nc.gpsimd.memset(picked_bytes[:].bitcast(I32), 0)
+        nc.gpsimd.memset(skip_bytes[:].bitcast(I32), 0)
         warm = tile([P, 2], F32, "warm")
         nc.vector.memset(warm[:, 0:1], 0.0)
         nc.scalar.activation(out=warm[:, 1:2], in_=warm[:, 0:1], func=ACT.Relu)
@@ -75,23 +75,21 @@ def tile_picked_segunpool_relu_po_kernel(
         z.append(z[2])
 
         nc.sync.dma_start(offs_sb[:], offs)
+        nc.sync.dma_start(out=x_bytes[ROWS_AT:, :].bitcast(I32), in_=x_scales[0].bitcast(I32))
         nc.sync.dma_start(skip_sb[:], skip)
-        nc.sync.dma_start(where_sb[:], where)
-        nc.sync.dma_start(out=x_bytes[0:P:8, :].bitcast(I32), in_=x_scales[0].bitcast(I32))
         nc.sync.dma_start(out=x_codes[:].bitcast(I32), in_=words_view(x_words))
         for a in range(2):
             cols = slice(a * H // 2, (a + 1) * H // 2)
             nc.sync.dma_start(out=w1_raw[a][:], in_=w1.rearrange("(p j) h -> p j h", j=PACK)[:, :, cols])
+        nc.sync.dma_start(where_sb[:], where)
 
         def place_rows(dst, src):
             for q in range(4):
                 nc.sync.dma_start(
-                    out=dst[32 * q : 32 * q + 4, :].bitcast(I32), in_=src[32 * q : 32 * q + 32 : 8, :].bitcast(I32)
+                    out=dst[32 * q : 32 * q + 4, :].bitcast(I32), in_=src[ROWS_AT + 4 * q : ROWS_AT + 4 * q + 4, :].bitcast(I32)
                 )
 
         last = U - QUARTER
-        skip_bytes = tile([P, U], U8, "skip_bytes")
-        nc.vector.memset(skip_bytes[:].bitcast(I32), 0)
         picked_spread = tile([P, S], U8, "picked_spread", "w_raw")
         skip_spread = tile([P, U], U8, "skip_spread")
         picked_codes = tile([P, S], U32, "picked_codes")

@@ -61,8 +61,7 @@ def tile_picked_segunpool_relu_po_kernel(
         picked_bytes = tile([P, S], U8, "picked_bytes")
 
         skip_bytes = tile([P, U], U8, "skip_bytes")
-        nc.gpsimd.memset(x_bytes[:96, :].bitcast(I32), 0)
-        nc.gpsimd.memset(x_bytes[96:ROWS_AT, :].bitcast(I32), 0)
+        nc.gpsimd.memset(x_bytes[:ROWS_AT, :].bitcast(I32), 0)
         nc.gpsimd.memset(picked_bytes[:].bitcast(I32), 0)
         nc.gpsimd.memset(skip_bytes[:].bitcast(I32), 0)
         warm = tile([P, 2], F32, "warm")
@@ -83,9 +82,9 @@ def tile_picked_segunpool_relu_po_kernel(
             nc.sync.dma_start(out=w1_raw[a][:], in_=w1.rearrange("(p j) h -> p j h", j=PACK)[:, :, cols])
         nc.sync.dma_start(where_sb[:], where)
 
-        def place_rows(dst, src):
+        def place_rows(queue, dst, src):
             for q in range(4):
-                nc.sync.dma_start(
+                queue.dma_start(
                     out=dst[32 * q : 32 * q + 4, :].bitcast(I32), in_=src[ROWS_AT + 4 * q : ROWS_AT + 4 * q + 4, :].bitcast(I32)
                 )
 
@@ -94,9 +93,9 @@ def tile_picked_segunpool_relu_po_kernel(
         skip_spread = tile([P, U], U8, "skip_spread")
         picked_codes = tile([P, S], U32, "picked_codes")
         nc.vector.tensor_copy(out=picked_spread[:], in_=x_bytes[:].indirect(offs_sb[:]))
-        place_rows(picked_bytes, picked_spread)
+        place_rows(nc.scalar, picked_bytes, picked_spread)
         nc.vector.tensor_copy(out=skip_spread[:], in_=x_bytes[:].indirect(skip_sb[:]))
-        place_rows(skip_bytes, skip_spread)
+        place_rows(nc.sync, skip_bytes, skip_spread)
         w_raw = tile([P, 2, N], U32, "w_raw")
         nc.sync.dma_start(out=w_raw[:, 0, :].bitcast(I32), in_=words_view(w2_words))
         nc.sync.dma_start(out=w_raw[:, 1, :].bitcast(I32), in_=words_view(w3_words))

@@ -69,17 +69,17 @@ def tile_picked_segunpool_relu_po_kernel(
         nc.scalar.activation(out=warm[:, 1:2], in_=warm[:, 0:1], func=ACT.Relu)
         loads = ctx.enter_context(tc.tile_pool(name="loads", bufs=1))
         x_codes = loads.tile([P, T], U32, name="x_codes")
-        w1_raw = [loads.tile([P, PACK, H // 2], F32, name=f"w1_raw{a}") for a in range(2)]
+        w1_raw = [loads.tile([P, 2, H], F32, name=f"w1_raw{a}") for a in range(2)]
         z = [loads.tile([P, U], F32, name=f"z{t}", align_bytes=64) for t in range(PACK - 1)]
         z.append(z[2])
 
         nc.sync.dma_start(offs_sb[:], offs)
         nc.sync.dma_start(out=x_bytes[ROWS_AT:, :].bitcast(I32), in_=x_scales[0].bitcast(I32))
         nc.sync.dma_start(skip_sb[:], skip)
-        nc.sync.dma_start(out=x_codes[:].bitcast(I32), in_=words_view(x_words))
         for a in range(2):
-            cols = slice(a * H // 2, (a + 1) * H // 2)
-            nc.sync.dma_start(out=w1_raw[a][:], in_=w1.rearrange("(p j) h -> p j h", j=PACK)[:, :, cols])
+            if a == 1:
+                nc.sync.dma_start(out=x_codes[:].bitcast(I32), in_=words_view(x_words))
+            nc.sync.dma_start(out=w1_raw[a][:], in_=w1.rearrange("(p j) h -> p j h", j=PACK)[:, 2 * a : 2 * a + 2, :])
         nc.sync.dma_start(where_sb[:], where)
 
         def place_rows(queue, dst, src):
@@ -111,7 +111,7 @@ def tile_picked_segunpool_relu_po_kernel(
             nc.vector.tensor_copy(out=codes[:], in_=x_codes[:].indirect(skip_sb[:, cols]))
             return codes
 
-        skip_codes = [None, gather_skip_codes(QUARTER, HALF, None), None]
+        skip_codes = [gather_skip_codes(0, QUARTER, None), None, None]
         skip_scales = [skip_bytes[:, :QUARTER], skip_bytes[:, QUARTER:last], skip_bytes[:, last:]]
 
         w1_codes, w1_bytes = {}, {}
@@ -119,7 +119,7 @@ def tile_picked_segunpool_relu_po_kernel(
             grouped = tile([P, 2, P, PACK], BF16, f"w1_grouped{u}")
             for a in range(2):
                 nc.scalar.activation(
-                    out=grouped[:, :, a * P // 2 : (a + 1) * P // 2, :].rearrange("p t m j -> p m j t"),
+                    out=grouped[:, :, :, 2 * a : 2 * a + 2].rearrange("p t m j -> p m j t"),
                     in_=w1_raw[a][:].rearrange("p j (m t) -> p m j t", t=PACK)[:, :, :, 2 * u : 2 * u + 2],
                     func=ACT.Copy,
                 )
@@ -131,7 +131,7 @@ def tile_picked_segunpool_relu_po_kernel(
             w1_codes[u] = codes
             w1_bytes[u] = scale
             if u == 1:
-                skip_codes[0] = gather_skip_codes(0, QUARTER, "w1_grouped1")
+                skip_codes[1] = gather_skip_codes(QUARTER, HALF, "w1_grouped1")
 
         for t in (2, 0, 1):
             nc.gpsimd.memset(z[t][:], 0.0)
@@ -231,7 +231,7 @@ def tile_picked_segunpool_relu_po_kernel(
             )
 
         out_rows = out_0.rearrange("(p t) w -> p t w", t=PACK)
-        out_bytes = tile([P, U], U8, "out_bytes")
+        out_bytes = tile([P, QUARTER], U8, "out_bytes")
         out_codes = tile([P, U], U32, "out_codes")
         result = [tile([P, PACK, width], F32, f"result{i}") for i, (first, width) in enumerate(pieces)]
         grouped = [tile([P, QUARTER, PACK], BF16, f"out_grouped{c}") for c in range(4)]
@@ -256,7 +256,7 @@ def tile_picked_segunpool_relu_po_kernel(
             cells = slice(c * QUARTER, (c + 1) * QUARTER)
             nc.vector.quantize_mx(
                 out=out_codes[:, cells].bitcast(FP8X4),
-                scales=out_bytes[:, cells],
+                scales=out_bytes[4 * c : P, :],
                 in_=grouped[c][:].rearrange("p c t -> p (c t)"),
             )
 
@@ -280,5 +280,6 @@ def tile_picked_segunpool_relu_po_kernel(
         nc.scalar.dma_start(out=words_view(out_1)[:, last:], in_=out_codes[:, last:].bitcast(I32))
         for q in range(4):
             (nc.sync if q < 3 else nc.scalar).dma_start(
-                out=out_2[0, 4 * q : 4 * q + 4, :].bitcast(I32), in_=out_bytes[32 * q : 32 * q + 4, :].bitcast(I32)
+                out=out_2[0, 4 * q : 4 * q + 4, :].bitcast(I32).rearrange("r (c w) -> c r w", c=4),
+                in_=out_bytes[32 * q : 32 * q + 16, :].bitcast(I32),
             )

@@ -21,6 +21,7 @@ W3_ROW = 4
 QUARTER = U // 4
 SCALAR_CELLS = 128
 ROWS_AT = 112
+W1_PIECES = ((0, 256), (256, 384), (384, 512))
 
 
 def words_view(dram):
@@ -69,17 +70,17 @@ def tile_picked_segunpool_relu_po_kernel(
         nc.scalar.activation(out=warm[:, 1:2], in_=warm[:, 0:1], func=ACT.Relu)
         loads = ctx.enter_context(tc.tile_pool(name="loads", bufs=1))
         x_codes = loads.tile([P, T], U32, name="x_codes")
-        w1_raw = [loads.tile([P, 2, H], F32, name=f"w1_raw{a}") for a in range(2)]
+        w1_raw = [loads.tile([P, PACK, hi - lo], F32, name=f"w1_raw{lo}") for lo, hi in W1_PIECES]
         z = [loads.tile([P, U], F32, name=f"z{t}", align_bytes=64) for t in range(PACK - 1)]
         z.append(z[2])
 
         nc.sync.dma_start(offs_sb[:], offs)
         nc.sync.dma_start(out=x_bytes[ROWS_AT:, :].bitcast(I32), in_=x_scales[0].bitcast(I32))
         nc.sync.dma_start(skip_sb[:], skip)
-        for a in range(2):
+        for a, (lo, hi) in enumerate(W1_PIECES):
             if a == 1:
                 nc.sync.dma_start(out=x_codes[:].bitcast(I32), in_=words_view(x_words))
-            nc.sync.dma_start(out=w1_raw[a][:], in_=w1.rearrange("(p j) h -> p j h", j=PACK)[:, 2 * a : 2 * a + 2, :])
+            nc.sync.dma_start(out=w1_raw[a][:], in_=w1.rearrange("(p j) h -> p j h", j=PACK)[:, :, lo:hi])
         nc.sync.dma_start(where_sb[:], where)
 
         def place_rows(queue, dst, src):
@@ -111,15 +112,14 @@ def tile_picked_segunpool_relu_po_kernel(
             nc.vector.tensor_copy(out=codes[:], in_=x_codes[:].indirect(skip_sb[:, cols]))
             return codes
 
-        skip_codes = [gather_skip_codes(0, QUARTER, None), None, None]
-        skip_scales = [skip_bytes[:, :QUARTER], skip_bytes[:, QUARTER:last], skip_bytes[:, last:]]
+        skip_codes = {}
 
         w1_codes, w1_bytes = {}, {}
         for u in (1, 0):
             grouped = tile([P, 2, P, PACK], BF16, f"w1_grouped{u}")
-            for a in range(2):
+            for a, (lo, hi) in enumerate(W1_PIECES):
                 nc.scalar.activation(
-                    out=grouped[:, :, :, 2 * a : 2 * a + 2].rearrange("p t m j -> p m j t"),
+                    out=grouped[:, :, lo // PACK : hi // PACK, :].rearrange("p t m j -> p m j t"),
                     in_=w1_raw[a][:].rearrange("p j (m t) -> p m j t", t=PACK)[:, :, :, 2 * u : 2 * u + 2],
                     func=ACT.Copy,
                 )
@@ -131,7 +131,7 @@ def tile_picked_segunpool_relu_po_kernel(
             w1_codes[u] = codes
             w1_bytes[u] = scale
             if u == 1:
-                skip_codes[1] = gather_skip_codes(QUARTER, HALF, "w1_grouped1")
+                skip_codes[0] = gather_skip_codes(0, QUARTER, "w1_grouped1")[:]
 
         for t in (2, 0, 1):
             nc.gpsimd.memset(z[t][:], 0.0)
@@ -173,113 +173,112 @@ def tile_picked_segunpool_relu_po_kernel(
             if t < 3:
                 nc.scalar.copy(out=z_grouped[:, :, t], in_=z[t][:])
 
-        pieces = [(0, QUARTER), (QUARTER, HALF), (U - QUARTER, QUARTER)]
+        def quarter(c):
+            return slice(c * QUARTER, (c + 1) * QUARTER)
 
-        def open_bank(i, t):
-            first, width = pieces[i]
-            acc = psum.tile([P, width], F32, name=f"acc{i}{t}", tag=f"bank{PACK * (i % 2) + t}")
+        def open_bank(c, t):
+            bank = psum.tile([P, QUARTER], F32, name=f"acc{c}{t}", tag=f"bank{PACK * (c % 2) + t}")
             cols = slice(t * P, (t + 1) * P)
             nc.tensor.matmul_mx(
-                out=acc[:],
+                out=bank[:],
                 lhsT=w_codes[:, 1, cols].bitcast(FP8X4),
                 lhsT_scale=w_bytes[W3_ROW:P, cols],
-                rhs=skip_codes[i][:].bitcast(FP8X4),
-                rhs_scale=skip_scales[i],
+                rhs=skip_codes[c].bitcast(FP8X4),
+                rhs_scale=skip_bytes[:, quarter(c)],
                 start=True,
                 stop=False,
             )
-            return acc
+            return bank
 
-        acc = [[open_bank(i, t) for t in range(PACK)] for i in range(2)]
+        opened = [open_bank(0, t) for t in range(PACK)]
 
-        z_codes = [tile([P, width], U32, f"z_codes{i}") for i, (first, width) in enumerate(pieces)]
-        z_bytes = [tile([P, width], U8, f"z_bytes{i}") for i, (first, width) in enumerate(pieces)]
+        z_codes = tile([P, U], U32, "z_codes")
+        z_bytes = tile([P, U], U8, "z_bytes")
 
-        def regroup(copy, lo, hi):
-            cells = slice(lo, hi)
-            copy(out=z_grouped[:, cells, 3], in_=z[3][:, cells])
+        def regroup(copy, c):
+            copy(out=z_grouped[:, quarter(c), 3], in_=z[3][:, quarter(c)])
 
-        def quantize_z(i):
-            first, width = pieces[i]
+        def quantize_z(cells):
             nc.vector.quantize_mx(
-                out=z_codes[i][:].bitcast(FP8X4),
-                scales=z_bytes[i][:],
-                in_=z_grouped[:, first : first + width, :].rearrange("p c t -> p (c t)"),
+                out=z_codes[:, cells].bitcast(FP8X4),
+                scales=z_bytes[:, cells],
+                in_=z_grouped[:, cells, :].rearrange("p c t -> p (c t)"),
             )
 
-        regroup(nc.vector.tensor_copy, 0, QUARTER)
-        regroup(nc.scalar.copy, QUARTER, HALF)
-        regroup(nc.vector.tensor_copy, HALF, last)
-        regroup(nc.scalar.copy, last, U)
-        quantize_z(0)
-        quantize_z(1)
-        last_codes = loads.tile([P, QUARTER], U32, name="last_codes", tag="z1", align_bytes=64)
-        nc.vector.tensor_copy(out=last_codes[:], in_=x_codes[:].indirect(skip_sb[:, last // 16 :]))
-        skip_codes[2] = last_codes
-        quantize_z(2)
+        def gather_late(first, count, tag):
+            codes = loads.tile([P, count], U32, name=f"late_codes{first}", tag=tag, align_bytes=64)
+            nc.vector.tensor_copy(out=codes[:], in_=x_codes[:].indirect(skip_sb[:, first // 16 : (first + count) // 16]))
+            return codes
 
-        def close_bank(i, t, bank):
+        on_s, on_v = nc.scalar.copy, nc.vector.tensor_copy
+        regroup(on_v, 0)
+        regroup(on_s, 1)
+        regroup(on_v, 2)
+        regroup(on_s, 3)
+        quantize_z(quarter(0))
+        middle = gather_late(QUARTER, HALF, "z1")
+        skip_codes[1], skip_codes[2] = middle[:, :QUARTER], middle[:, QUARTER:]
+        quantize_z(quarter(1))
+        skip_codes[3] = gather_late(last, QUARTER, "z2")[:]
+        quantize_z(slice(HALF, U))
+
+        def close_bank(c, t, bank):
             cols = slice(t * P, (t + 1) * P)
             nc.tensor.matmul_mx(
                 out=bank[:],
                 lhsT=w_codes[:, 0, cols].bitcast(FP8X4),
                 lhsT_scale=w_bytes[:, cols],
-                rhs=z_codes[i][:].bitcast(FP8X4),
-                rhs_scale=z_bytes[i][:],
+                rhs=z_codes[:, quarter(c)].bitcast(FP8X4),
+                rhs_scale=z_bytes[:, quarter(c)],
                 start=False,
                 stop=True,
             )
 
         out_rows = out_0.rearrange("(p t) w -> p t w", t=PACK)
-        out_bytes = tile([P, QUARTER], U8, "out_bytes")
+        out_bytes = tile([P, HALF], U8, "out_bytes")
         out_codes = tile([P, U], U32, "out_codes")
-        result = [tile([P, PACK, width], F32, f"result{i}") for i, (first, width) in enumerate(pieces)]
-        grouped = [tile([P, QUARTER, PACK], BF16, f"out_grouped{c}") for c in range(4)]
+        result = [tile([P, PACK, QUARTER], F32, f"result{c}") for c in range(4)]
+        grouped = tile([P, U, PACK], BF16, "out_grouped")
 
-        def empty(i, t, copy):
-            first, width = pieces[i]
-            cells = slice(first, first + width)
-            bank = acc[i][t] if i < 2 else open_bank(i, t)
-            close_bank(i, t, bank)
-            copy(out=result[i][:, t, :], in_=bank[:])
-            if i < 2:
-                nc.sync.dma_start(out=out_rows[:, t, cells], in_=result[i][:, t, :])
-            elif t % 2 == 1:
-                nc.sync.dma_start(out=out_rows[:, t - 1 : t + 1, cells], in_=result[i][:, t - 1 : t + 1, :])
+        def empty(c):
+            for t in range(PACK):
+                bank = opened[t] if c == 0 else open_bank(c, t)
+                close_bank(c, t, bank)
+                on_s(out=result[c][:, t, :], in_=bank[:])
+                if c == 0:
+                    nc.sync.dma_start(out=out_rows[:, t, quarter(c)], in_=result[c][:, t, :])
+                elif t % 2 == 1:
+                    nc.sync.dma_start(out=out_rows[:, t - 1 : t + 1, quarter(c)], in_=result[c][:, t - 1 : t + 1, :])
 
-        def interleave(c, i, at, copy, lo, hi):
-            src = result[i][:, :, at + lo : at + hi].rearrange("p t (c i) -> p c t i", i=4)
-            dst = grouped[c][:, lo:hi, :].rearrange("p (c i) t -> p c t i", i=4)
+        def interleave(c, copy, lo, hi):
+            src = result[c][:, :, lo:hi].rearrange("p t (c i) -> p c t i", i=4)
+            dst = grouped[:, c * QUARTER + lo : c * QUARTER + hi, :].rearrange("p (c i) t -> p c t i", i=4)
             copy(out=dst, in_=src)
 
-        def quantize_out(c):
-            cells = slice(c * QUARTER, (c + 1) * QUARTER)
+        def quantize_out(lo, hi):
+            half = lo // HALF
             nc.vector.quantize_mx(
-                out=out_codes[:, cells].bitcast(FP8X4),
-                scales=out_bytes[4 * c : P, :],
-                in_=grouped[c][:].rearrange("p c t -> p (c t)"),
+                out=out_codes[:, lo:hi].bitcast(FP8X4),
+                scales=out_bytes[4 * half : P, lo - half * HALF : hi - half * HALF],
+                in_=grouped[:, lo:hi, :].rearrange("p c t -> p (c t)"),
             )
 
-        on_s, on_v = nc.scalar.copy, nc.vector.tensor_copy
-        for t in range(PACK):
-            empty(0, t, on_s)
-        interleave(0, 0, 0, on_v, 0, QUARTER)
-        for t in range(PACK):
-            empty(1, t, on_v if t == 1 else on_s)
-        quantize_out(0)
-        interleave(1, 1, 0, on_v, 0, QUARTER)
-        interleave(2, 1, QUARTER, on_v, 0, QUARTER)
-        quantize_out(1)
-        for t in range(PACK):
-            empty(2, t, on_s)
-        interleave(3, 2, 0, on_s, 0, SCALAR_CELLS)
-        interleave(3, 2, 0, on_v, SCALAR_CELLS, QUARTER)
-        quantize_out(2)
-        quantize_out(3)
+        empty(0)
+        interleave(0, on_v, 0, QUARTER)
+        empty(1)
+        interleave(1, on_v, 0, QUARTER)
+        empty(2)
+        interleave(2, on_v, 0, QUARTER)
+        quantize_out(0, HALF)
+        empty(3)
+        interleave(3, on_s, 0, SCALAR_CELLS)
+        interleave(3, on_v, SCALAR_CELLS, QUARTER)
+        quantize_out(HALF, last)
+        quantize_out(last, U)
         nc.sync.dma_start(out=words_view(out_1)[:, :last], in_=out_codes[:, :last].bitcast(I32))
         nc.scalar.dma_start(out=words_view(out_1)[:, last:], in_=out_codes[:, last:].bitcast(I32))
         for q in range(4):
             (nc.sync if q < 3 else nc.scalar).dma_start(
-                out=out_2[0, 4 * q : 4 * q + 4, :].bitcast(I32).rearrange("r (c w) -> c r w", c=4),
-                in_=out_bytes[32 * q : 32 * q + 16, :].bitcast(I32),
+                out=out_2[0, 4 * q : 4 * q + 4, :].bitcast(I32).rearrange("r (c w) -> c r w", c=2),
+                in_=out_bytes[32 * q : 32 * q + 8, :].bitcast(I32),
             )

@@ -13,6 +13,7 @@ U16 = mybir.dt.uint16
 U8 = mybir.dt.uint8
 FP8X4 = mybir.dt.float8_e4m3fn_x4
 ACT = mybir.ActivationFunctionType
+ALU = mybir.AluOpType
 
 P = 128
 PACK = 4
@@ -21,7 +22,10 @@ W3_ROW = 4
 QUARTER = U // 4
 SCALAR_CELLS = 128
 ROWS_AT = 112
-W1_PIECES = ((0, 256), (256, 384), (384, 512))
+GPSIMD_CELLS = 384
+SKIP_FIRST = ((0, 0), (0, 1), (1, 0), (1, 1), (3, 0), (3, 1))
+FIRST = 128
+W1_PIECES = ((0, 256), (256, 512))
 
 
 def words_view(dram):
@@ -55,6 +59,11 @@ def tile_picked_segunpool_relu_po_kernel(
         def tile(shape, dtype, name, tag=None):
             return sb.tile(shape, dtype, name=name, tag=tag or name, align_bytes=64)
 
+        placed = ctx.enter_context(tc.tile_pool(name="placed", bufs=1))
+
+        def place(shape, dtype, name, offset):
+            return placed.tile(shape, dtype, name=name, offset=offset, align_bytes=64)
+
         offs_sb = lists.tile([P, S // 16], U16, name="offs_sb")
         skip_sb = lists.tile([P, U // 16], U16, name="skip_sb")
         where_sb = lists.tile([P, S // 16], U16, name="where_sb")
@@ -76,11 +85,11 @@ def tile_picked_segunpool_relu_po_kernel(
 
         nc.sync.dma_start(offs_sb[:], offs)
         nc.sync.dma_start(out=x_bytes[ROWS_AT:, :].bitcast(I32), in_=x_scales[0].bitcast(I32))
-        nc.sync.dma_start(skip_sb[:], skip)
         for a, (lo, hi) in enumerate(W1_PIECES):
-            if a == 1:
-                nc.sync.dma_start(out=x_codes[:].bitcast(I32), in_=words_view(x_words))
             nc.sync.dma_start(out=w1_raw[a][:], in_=w1.rearrange("(p j) h -> p j h", j=PACK)[:, :, lo:hi])
+            if a == 0:
+                nc.sync.dma_start(skip_sb[:], skip)
+        nc.sync.dma_start(out=x_codes[:].bitcast(I32), in_=words_view(x_words))
         nc.sync.dma_start(where_sb[:], where)
 
         def place_rows(queue, dst, src):
@@ -91,7 +100,7 @@ def tile_picked_segunpool_relu_po_kernel(
 
         last = U - QUARTER
         picked_spread = tile([P, S], U8, "picked_spread", "w_raw")
-        skip_spread = tile([P, U], U8, "skip_spread")
+        skip_spread = place([P, U], U8, "skip_spread", 1792)
         picked_codes = tile([P, S], U32, "picked_codes")
         nc.vector.tensor_copy(out=picked_spread[:], in_=x_bytes[:].indirect(offs_sb[:]))
         place_rows(nc.scalar, picked_bytes, picked_spread)
@@ -100,11 +109,12 @@ def tile_picked_segunpool_relu_po_kernel(
         w_raw = tile([P, 2, N], U32, "w_raw")
         nc.sync.dma_start(out=w_raw[:, 0, :].bitcast(I32), in_=words_view(w2_words))
         nc.sync.dma_start(out=w_raw[:, 1, :].bitcast(I32), in_=words_view(w3_words))
-        w_bytes_raw = tile([P, N], U8, "w_bytes_raw", "skip_spread")
+        w_bytes_raw = place([P, N], U8, "w_bytes_raw", 1792)
         nc.gpsimd.memset(w_bytes_raw[:].bitcast(I32), 0)
         load_scale_rows((nc.sync,), w_bytes_raw, W3_ROW, w3_scales)
         load_scale_rows((nc.sync,), w_bytes_raw, 0, w2_scales)
-        nc.vector.tensor_copy(out=picked_codes[:], in_=x_codes[:].indirect(offs_sb[:]))
+        nc.vector.tensor_copy(out=picked_codes[:, : S // 2], in_=x_codes[:].indirect(offs_sb[:, : S // 32]))
+        nc.vector.tensor_copy(out=picked_codes[:, S // 2 :], in_=x_codes[:].indirect(offs_sb[:, S // 32 :]))
 
         def gather_skip_codes(first, count, tag):
             codes = tile([P, count], U32, f"skip_codes{first}", tag)
@@ -112,16 +122,15 @@ def tile_picked_segunpool_relu_po_kernel(
             nc.vector.tensor_copy(out=codes[:], in_=x_codes[:].indirect(skip_sb[:, cols]))
             return codes
 
-        skip_codes = {}
+        skip_codes = {0: gather_skip_codes(0, QUARTER, None)[:]}
 
         w1_codes, w1_bytes = {}, {}
         for u in (1, 0):
             grouped = tile([P, 2, P, PACK], BF16, f"w1_grouped{u}")
             for a, (lo, hi) in enumerate(W1_PIECES):
-                nc.scalar.activation(
+                (nc.vector.tensor_copy if (u, a) == (0, 1) else nc.scalar.copy)(
                     out=grouped[:, :, lo // PACK : hi // PACK, :].rearrange("p t m j -> p m j t"),
                     in_=w1_raw[a][:].rearrange("p j (m t) -> p m j t", t=PACK)[:, :, :, 2 * u : 2 * u + 2],
-                    func=ACT.Copy,
                 )
             codes = tile([P, 2 * P], U32, f"w1_codes{u}")
             scale = tile([P, 2 * P], U8, f"w1_bytes{u}")
@@ -130,73 +139,96 @@ def tile_picked_segunpool_relu_po_kernel(
             )
             w1_codes[u] = codes
             w1_bytes[u] = scale
-            if u == 1:
-                skip_codes[0] = gather_skip_codes(0, QUARTER, "w1_grouped1")[:]
 
         for t in (2, 0, 1):
             nc.gpsimd.memset(z[t][:], 0.0)
 
-        def project(t, part, bank, name):
+        def project(t, parts, bank, name):
             cols = slice((t % 2) * P, (t % 2 + 1) * P)
-            width = part.stop - part.start
-            acc = psum.tile([P, width], F32, name=f"acc_{name}", tag=f"bank{bank}")
-            nc.tensor.matmul_mx(
-                out=acc[:],
-                lhsT=w1_codes[t // 2][:, cols].bitcast(FP8X4),
-                lhsT_scale=w1_bytes[t // 2][:, cols],
-                rhs=picked_codes[:, part].bitcast(FP8X4),
-                rhs_scale=picked_bytes[:, part],
-                start=True,
-                stop=True,
-            )
-            values = tile([P, width], F32, name)
-            nc.scalar.activation(out=values[:], in_=acc[:], func=ACT.Relu)
+            first = parts[0][0]
+            acc = psum.tile([P, parts[-1][1] - first], F32, name=f"acc_{name}", tag=f"bank{bank}")
+            for lo, hi in parts:
+                nc.tensor.matmul_mx(
+                    out=acc[:, lo - first : hi - first],
+                    lhsT=w1_codes[t // 2][:, cols].bitcast(FP8X4),
+                    lhsT_scale=w1_bytes[t // 2][:, cols],
+                    rhs=picked_codes[:, lo:hi].bitcast(FP8X4),
+                    rhs_scale=picked_bytes[:, lo:hi],
+                    start=True,
+                    stop=True,
+                )
+            return acc
+
+        def relu(out, acc):
+            nc.scalar.activation(out=out, in_=acc[:], func=ACT.Relu)
+
+        def activate(t, parts, bank, name):
+            values = tile([P, parts[-1][1] - parts[0][0]], F32, name)
+            relu(values[:], project(t, parts, bank, name))
             return values
 
-        y_first = project(2, slice(0, S // 2), 0, "y_first")
-        y = {2: project(2, slice(S // 2, S), PACK + 2, "y2")}
+        y_first = activate(2, [(0, FIRST)], 0, "y_first")
+        y = {2: activate(2, [(FIRST, S // 2), (S // 2, S)], PACK + 2, "y2")}
         for t in (0, 1, 3):
-            y[t] = project(t, slice(0, S), PACK + t, f"y{t}")
+            y[t] = activate(t, [(0, S)], PACK + t, f"y{t}")
 
-        z_grouped = tile([P, U, PACK], BF16, "z_grouped")
+        w2_codes = tile([P, 1, N], U32, "w2_codes")
+        deal(nc.gpsimd, w2_codes[:], w_raw[:, 0:1, :], 4)
+        w_bytes = tile([P, N], U8, "w_bytes")
+        deal(nc.gpsimd, w_bytes[:].unsqueeze(1), w_bytes_raw[:].unsqueeze(1), 16)
+        z_grouped = place([P, U, PACK], BF16, "z_grouped", 2048)
+        w3_codes = place([P, 1, N], U32, "w3_codes", 0)
+
+        def on_g(out, in_):
+            nc.gpsimd.tensor_scalar(out=out, in0=in_, scalar1=1.0, scalar2=0.0, op0=ALU.mult, op1=ALU.add)
+
+        on_s, on_v = nc.scalar.copy, nc.vector.tensor_copy
+
+        def regroup(copy, t, lo, hi):
+            copy(out=z_grouped[:, lo:hi, t], in_=z[t][:, lo:hi])
+
         for t in (2, 0, 1, 3):
             if t == 2:
-                nc.vector.tensor_copy(out=z[t][:].indirect(where_sb[:, : S // 32]), in_=y_first[:])
-                nc.vector.tensor_copy(out=z[t][:].indirect(where_sb[:, S // 32 :]), in_=y[t][:])
-                w_codes = tile([P, 2, N], U32, "w_codes", "y2")
-                deal(nc.gpsimd, w_codes[:], w_raw[:], 4)
+                nc.vector.tensor_copy(out=z[t][:].indirect(where_sb[:, : FIRST // 16]), in_=y_first[:])
+                nc.vector.tensor_copy(out=z[t][:].indirect(where_sb[:, FIRST // 16 :]), in_=y[t][:])
             else:
                 nc.vector.tensor_copy(out=z[t][:].indirect(where_sb[:]), in_=y[t][:])
-            if t == 1:
-                w_bytes = tile([P, N], U8, "w_bytes", "y1")
-                deal(nc.gpsimd, w_bytes[:].unsqueeze(1), w_bytes_raw[:].unsqueeze(1), 16)
             if t < 3:
-                nc.scalar.copy(out=z_grouped[:, :, t], in_=z[t][:])
+                regroup(on_g, t, 0, GPSIMD_CELLS)
+                regroup(on_s, t, GPSIMD_CELLS, U)
+            if t == 1:
+                deal(nc.gpsimd, w3_codes[:], w_raw[:, 1:2, :], 4)
+        regroup(on_s, 3, 0, QUARTER)
+        regroup(on_s, 3, QUARTER, HALF)
+        regroup(on_g, 3, HALF, HALF + GPSIMD_CELLS)
+        regroup(on_s, 3, HALF + GPSIMD_CELLS, U)
 
         def quarter(c):
             return slice(c * QUARTER, (c + 1) * QUARTER)
 
-        def open_bank(c, t):
-            bank = psum.tile([P, QUARTER], F32, name=f"acc{c}{t}", tag=f"bank{PACK * (c % 2) + t}")
-            cols = slice(t * P, (t + 1) * P)
-            nc.tensor.matmul_mx(
-                out=bank[:],
-                lhsT=w_codes[:, 1, cols].bitcast(FP8X4),
-                lhsT_scale=w_bytes[W3_ROW:P, cols],
-                rhs=skip_codes[c].bitcast(FP8X4),
-                rhs_scale=skip_bytes[:, quarter(c)],
-                start=True,
-                stop=False,
-            )
-            return bank
+        banks = {}
 
-        opened = [open_bank(0, t) for t in range(PACK)]
+        def add_product(c, h, skip_side):
+            opens = (c, h) not in banks
+            if opens:
+                banks[c, h] = psum.tile([P, 2, QUARTER], F32, name=f"acc{c}{h}", tag=f"bank{2 * c + h}")
+            for e in range(2):
+                cols = slice((2 * h + e) * P, (2 * h + e + 1) * P)
+                nc.tensor.matmul_mx(
+                    out=banks[c, h][:, e, :],
+                    lhsT=(w3_codes if skip_side else w2_codes)[:, 0, cols].bitcast(FP8X4),
+                    lhsT_scale=w_bytes[W3_ROW if skip_side else 0 : P, cols],
+                    rhs=(skip_codes[c] if skip_side else z_codes[:, quarter(c)]).bitcast(FP8X4),
+                    rhs_scale=(skip_bytes if skip_side else z_bytes)[:, quarter(c)],
+                    start=opens and e == 0,
+                    stop=not opens and e == 1,
+                )
+
+        add_product(0, 0, True)
+        add_product(0, 1, True)
 
         z_codes = tile([P, U], U32, "z_codes")
         z_bytes = tile([P, U], U8, "z_bytes")
-
-        def regroup(copy, c):
-            copy(out=z_grouped[:, quarter(c), 3], in_=z[3][:, quarter(c)])
 
         def quantize_z(cells):
             nc.vector.quantize_mx(
@@ -205,34 +237,18 @@ def tile_picked_segunpool_relu_po_kernel(
                 in_=z_grouped[:, cells, :].rearrange("p c t -> p (c t)"),
             )
 
-        def gather_late(first, count, tag):
-            codes = loads.tile([P, count], U32, name=f"late_codes{first}", tag=tag, align_bytes=64)
+        def gather_late(pool, tag, first, count):
+            codes = pool.tile([P, count], U32, name=f"late_codes{first}", tag=tag, align_bytes=64)
             nc.vector.tensor_copy(out=codes[:], in_=x_codes[:].indirect(skip_sb[:, first // 16 : (first + count) // 16]))
             return codes
 
-        on_s, on_v = nc.scalar.copy, nc.vector.tensor_copy
-        regroup(on_v, 0)
-        regroup(on_s, 1)
-        regroup(on_v, 2)
-        regroup(on_s, 3)
-        quantize_z(quarter(0))
-        middle = gather_late(QUARTER, HALF, "z1")
+        middle = gather_late(sb, "y3", QUARTER, HALF)
         skip_codes[1], skip_codes[2] = middle[:, :QUARTER], middle[:, QUARTER:]
+        quantize_z(quarter(0))
         quantize_z(quarter(1))
-        skip_codes[3] = gather_late(last, QUARTER, "z2")[:]
-        quantize_z(slice(HALF, U))
-
-        def close_bank(c, t, bank):
-            cols = slice(t * P, (t + 1) * P)
-            nc.tensor.matmul_mx(
-                out=bank[:],
-                lhsT=w_codes[:, 0, cols].bitcast(FP8X4),
-                lhsT_scale=w_bytes[:, cols],
-                rhs=z_codes[:, quarter(c)].bitcast(FP8X4),
-                rhs_scale=z_bytes[:, quarter(c)],
-                start=False,
-                stop=True,
-            )
+        quantize_z(quarter(2))
+        skip_codes[3] = gather_late(loads, "z2", last, QUARTER)[:]
+        quantize_z(quarter(3))
 
         out_rows = out_0.rearrange("(p t) w -> p t w", t=PACK)
         out_bytes = tile([P, HALF], U8, "out_bytes")
@@ -241,14 +257,16 @@ def tile_picked_segunpool_relu_po_kernel(
         grouped = tile([P, U, PACK], BF16, "out_grouped")
 
         def empty(c):
-            for t in range(PACK):
-                bank = opened[t] if c == 0 else open_bank(c, t)
-                close_bank(c, t, bank)
-                on_s(out=result[c][:, t, :], in_=bank[:])
-                if c == 0:
-                    nc.sync.dma_start(out=out_rows[:, t, quarter(c)], in_=result[c][:, t, :])
-                elif t % 2 == 1:
-                    nc.sync.dma_start(out=out_rows[:, t - 1 : t + 1, quarter(c)], in_=result[c][:, t - 1 : t + 1, :])
+            for h in range(2):
+                skip_first = (c, h) in SKIP_FIRST
+                if c > 0:
+                    add_product(c, h, skip_first)
+                add_product(c, h, not skip_first)
+                runs = ((0, 1), (1, 2)) if (c, h) == (0, 0) else ((0, 2),)
+                for lo, hi in runs:
+                    planes = slice(2 * h + lo, 2 * h + hi)
+                    (on_v if (c, h) == (1, 1) else on_s)(out=result[c][:, planes, :], in_=banks[c, h][:, lo:hi, :])
+                    nc.sync.dma_start(out=out_rows[:, planes, quarter(c)], in_=result[c][:, planes, :])
 
         def interleave(c, copy, lo, hi):
             src = result[c][:, :, lo:hi].rearrange("p t (c i) -> p c t i", i=4)

@@ -22,6 +22,8 @@ W3_ROW = 4
 QUARTER = U // 4
 SCALAR_CELLS = 128
 ROWS_AT = 112
+AHEAD_OF_DEAL = 64
+WARM_PASSES = 3
 GPSIMD_CELLS = 384
 SKIP_FIRST = ((0, 0), (0, 1), (1, 0), (1, 1), (3, 0), (3, 1))
 FIRST = 128
@@ -193,11 +195,14 @@ def tile_picked_segunpool_relu_po_kernel(
                 nc.vector.tensor_copy(out=z[t][:].indirect(where_sb[:, FIRST // 16 :]), in_=y[t][:])
             else:
                 nc.vector.tensor_copy(out=z[t][:].indirect(where_sb[:]), in_=y[t][:])
-            if t < 3:
-                regroup(on_g, t, 0, GPSIMD_CELLS)
-                regroup(on_s, t, GPSIMD_CELLS, U)
             if t == 1:
+                regroup(on_g, t, 0, AHEAD_OF_DEAL)
                 deal(nc.gpsimd, w3_codes[:], w_raw[:, 1:2, :], 4)
+                regroup(on_g, t, AHEAD_OF_DEAL, GPSIMD_CELLS)
+            elif t < 3:
+                regroup(on_g, t, 0, GPSIMD_CELLS)
+            if t < 3:
+                regroup(on_s, t, GPSIMD_CELLS, U)
         regroup(on_s, 3, 0, QUARTER)
         regroup(on_s, 3, QUARTER, HALF)
         regroup(on_g, 3, HALF, HALF + GPSIMD_CELLS)
@@ -226,6 +231,17 @@ def tile_picked_segunpool_relu_po_kernel(
 
         add_product(0, 0, True)
         add_product(0, 1, True)
+        unread = psum.tile([P, S], F32, name="unread", tag="bank7")
+        for repeat in range(WARM_PASSES):
+            nc.tensor.matmul_mx(
+                out=unread[:],
+                lhsT=w3_codes[:, 0, :P].bitcast(FP8X4),
+                lhsT_scale=w_bytes[W3_ROW:P, :P],
+                rhs=picked_codes[:].bitcast(FP8X4),
+                rhs_scale=picked_bytes[:],
+                start=True,
+                stop=True,
+            )
 
         z_codes = tile([P, U], U32, "z_codes")
         z_bytes = tile([P, U], U8, "z_bytes")

@@ -24,7 +24,6 @@ SCALAR_CELLS = 128
 ROWS_AT = 112
 AHEAD_OF_DEAL = 64
 WARM_PASSES = 3
-GPSIMD_CELLS = 384
 SKIP_FIRST = ((0, 0), (0, 1), (1, 0), (1, 1), (3, 0), (3, 1))
 FIRST = 128
 W1_PIECES = ((0, 256), (256, 512))
@@ -178,7 +177,9 @@ def tile_picked_segunpool_relu_po_kernel(
         deal(nc.gpsimd, w2_codes[:], w_raw[:, 0:1, :], 4)
         w_bytes = tile([P, N], U8, "w_bytes")
         deal(nc.gpsimd, w_bytes[:].unsqueeze(1), w_bytes_raw[:].unsqueeze(1), 16)
-        z_grouped = place([P, U, PACK], BF16, "z_grouped", 2048)
+        first_grouped = place([P, QUARTER, PACK], BF16, "first_grouped", 4096)
+        middle_grouped = tile([P, HALF, PACK], BF16, "middle_grouped")
+        last_grouped = place([P, QUARTER, PACK], BF16, "last_grouped", 2048)
         w3_codes = place([P, 1, N], U32, "w3_codes", 0)
 
         def on_g(out, in_):
@@ -186,8 +187,15 @@ def tile_picked_segunpool_relu_po_kernel(
 
         on_s, on_v = nc.scalar.copy, nc.vector.tensor_copy
 
+        def z_grouped(lo, hi):
+            if hi <= QUARTER:
+                return first_grouped[:, lo:hi, :]
+            if hi <= last:
+                return middle_grouped[:, lo - QUARTER : hi - QUARTER, :]
+            return last_grouped[:, lo - last : hi - last, :]
+
         def regroup(copy, t, lo, hi):
-            copy(out=z_grouped[:, lo:hi, t], in_=z[t][:, lo:hi])
+            copy(out=z_grouped(lo, hi)[:, :, t], in_=z[t][:, lo:hi])
 
         for t in (2, 0, 1, 3):
             if t == 2:
@@ -196,17 +204,18 @@ def tile_picked_segunpool_relu_po_kernel(
             else:
                 nc.vector.tensor_copy(out=z[t][:].indirect(where_sb[:]), in_=y[t][:])
             if t == 1:
-                regroup(on_g, t, 0, AHEAD_OF_DEAL)
+                regroup(on_g, t, last, last + AHEAD_OF_DEAL)
                 deal(nc.gpsimd, w3_codes[:], w_raw[:, 1:2, :], 4)
-                regroup(on_g, t, AHEAD_OF_DEAL, GPSIMD_CELLS)
+                regroup(on_g, t, last + AHEAD_OF_DEAL, U)
             elif t < 3:
-                regroup(on_g, t, 0, GPSIMD_CELLS)
+                regroup(on_g, t, last, U)
             if t < 3:
-                regroup(on_s, t, GPSIMD_CELLS, U)
-        regroup(on_s, 3, 0, QUARTER)
+                regroup(on_s, t, 0, QUARTER)
+                regroup(on_s, t, QUARTER, last)
+        regroup(on_v, 3, 0, QUARTER)
         regroup(on_s, 3, QUARTER, HALF)
-        regroup(on_g, 3, HALF, HALF + GPSIMD_CELLS)
-        regroup(on_s, 3, HALF + GPSIMD_CELLS, U)
+        regroup(on_s, 3, HALF, last)
+        regroup(on_g, 3, last, U)
 
         def quarter(c):
             return slice(c * QUARTER, (c + 1) * QUARTER)
@@ -250,27 +259,28 @@ def tile_picked_segunpool_relu_po_kernel(
             nc.vector.quantize_mx(
                 out=z_codes[:, cells].bitcast(FP8X4),
                 scales=z_bytes[:, cells],
-                in_=z_grouped[:, cells, :].rearrange("p c t -> p (c t)"),
+                in_=z_grouped(cells.start, cells.stop).rearrange("p c t -> p (c t)"),
             )
 
-        def gather_late(pool, tag, first, count):
-            codes = pool.tile([P, count], U32, name=f"late_codes{first}", tag=tag, align_bytes=64)
+        def gather_late(codes, first, count):
             nc.vector.tensor_copy(out=codes[:], in_=x_codes[:].indirect(skip_sb[:, first // 16 : (first + count) // 16]))
             return codes
 
-        middle = gather_late(sb, "y3", QUARTER, HALF)
-        skip_codes[1], skip_codes[2] = middle[:, :QUARTER], middle[:, QUARTER:]
+        skip_codes[1] = gather_late(tile([P, QUARTER], U32, "late_codes1", "y3"), QUARTER, QUARTER)[:]
         quantize_z(quarter(0))
         quantize_z(quarter(1))
+        skip_codes[2] = gather_late(place([P, QUARTER], U32, "late_codes2", 4096), HALF, QUARTER)[:]
         quantize_z(quarter(2))
-        skip_codes[3] = gather_late(loads, "z2", last, QUARTER)[:]
+        skip_codes[3] = gather_late(loads.tile([P, QUARTER], U32, name="late_codes3", tag="z2", align_bytes=64), last, QUARTER)[:]
         quantize_z(quarter(3))
 
         out_rows = out_0.rearrange("(p t) w -> p t w", t=PACK)
         out_bytes = tile([P, HALF], U8, "out_bytes")
         out_codes = tile([P, U], U32, "out_codes")
         result = [tile([P, PACK, QUARTER], F32, f"result{c}") for c in range(4)]
-        grouped = tile([P, U, PACK], BF16, "out_grouped")
+        first_half = tile([P, HALF, PACK], BF16, "out_grouped01")
+        grouped = [first_half[:, :QUARTER, :], first_half[:, QUARTER:, :]]
+        grouped.extend(tile([P, QUARTER, PACK], BF16, f"out_grouped{c}")[:] for c in (2, 3))
 
         def empty(c):
             for h in range(2):
@@ -281,34 +291,33 @@ def tile_picked_segunpool_relu_po_kernel(
                 runs = ((0, 1), (1, 2)) if (c, h) == (0, 0) else ((0, 2),)
                 for lo, hi in runs:
                     planes = slice(2 * h + lo, 2 * h + hi)
-                    (on_v if (c, h) == (1, 1) else on_s)(out=result[c][:, planes, :], in_=banks[c, h][:, lo:hi, :])
+                    on_s(out=result[c][:, planes, :], in_=banks[c, h][:, lo:hi, :])
                     nc.sync.dma_start(out=out_rows[:, planes, quarter(c)], in_=result[c][:, planes, :])
 
         def interleave(c, copy, lo, hi):
             src = result[c][:, :, lo:hi].rearrange("p t (c i) -> p c t i", i=4)
-            dst = grouped[:, c * QUARTER + lo : c * QUARTER + hi, :].rearrange("p (c i) t -> p c t i", i=4)
+            dst = grouped[c][:, lo:hi, :].rearrange("p (c i) t -> p c t i", i=4)
             copy(out=dst, in_=src)
 
-        def quantize_out(lo, hi):
-            half = lo // HALF
+        def quantize_out(source, half, cells):
             nc.vector.quantize_mx(
-                out=out_codes[:, lo:hi].bitcast(FP8X4),
-                scales=out_bytes[4 * half : P, lo - half * HALF : hi - half * HALF],
-                in_=grouped[:, lo:hi, :].rearrange("p c t -> p (c t)"),
+                out=out_codes[:, half * HALF + cells.start : half * HALF + cells.stop].bitcast(FP8X4),
+                scales=out_bytes[4 * half : P, cells],
+                in_=source.rearrange("p c t -> p (c t)"),
             )
 
         empty(0)
         interleave(0, on_v, 0, QUARTER)
         empty(1)
         interleave(1, on_v, 0, QUARTER)
+        quantize_out(first_half[:], 0, slice(0, HALF))
         empty(2)
         interleave(2, on_v, 0, QUARTER)
-        quantize_out(0, HALF)
+        quantize_out(grouped[2], 1, quarter(0))
         empty(3)
         interleave(3, on_s, 0, SCALAR_CELLS)
         interleave(3, on_v, SCALAR_CELLS, QUARTER)
-        quantize_out(HALF, last)
-        quantize_out(last, U)
+        quantize_out(grouped[3], 1, quarter(1))
         nc.sync.dma_start(out=words_view(out_1)[:, :last], in_=out_codes[:, :last].bitcast(I32))
         nc.scalar.dma_start(out=words_view(out_1)[:, last:], in_=out_codes[:, last:].bitcast(I32))
         for q in range(4):

@@ -26,6 +26,7 @@ AHEAD_OF_DEAL = 64
 WARM_PASSES = 3
 SKIP_FIRST = ((0, 0), (0, 1), (1, 0), (1, 1), (3, 0), (3, 1))
 FIRST = 128
+GPSIMD_CELLS = 160
 W1_PIECES = ((0, 256), (256, 512))
 
 
@@ -215,7 +216,8 @@ def tile_picked_segunpool_relu_po_kernel(
         regroup(on_v, 3, 0, QUARTER)
         regroup(on_s, 3, QUARTER, HALF)
         regroup(on_s, 3, HALF, last)
-        regroup(on_g, 3, last, U)
+        regroup(on_g, 3, last, last + GPSIMD_CELLS)
+        regroup(on_s, 3, last + GPSIMD_CELLS, U)
 
         def quarter(c):
             return slice(c * QUARTER, (c + 1) * QUARTER)

@@ -18,34 +18,28 @@ ALU = mybir.AluOpType
 P = 128
 PACK = 4
 HALF = U // 2
-W3_ROW = 4
 QUARTER = U // 4
-SCALAR_CELLS = 128
+LAST = U - QUARTER
+W3_ROW = 4
 ROWS_AT = 112
-AHEAD_OF_DEAL = 64
-WARM_PASSES = 3
-SKIP_FIRST = ((0, 0), (0, 1), (1, 0), (1, 1), (3, 0), (3, 1))
 FIRST = 128
-GPSIMD_CELLS = 160
-W1_PIECES = ((0, 256), (256, 512))
+SCALAR_W1 = 76
+PLANES = (0, 2, 1, 3)
+AHEAD_OF_DEAL = 64
+GPSIMD_LAST = 160
+VECTOR_LAST = 256
+SCALAR_CELLS = 128
+WARM_PASSES = 2
 
 
 def words_view(dram):
     return dram[0].rearrange("p c r -> p (c r)").bitcast(I32)
 
 
-def load_scale_rows(queues, tile, first_row, dram):
-    for q in range(4):
-        queues[q % len(queues)].dma_start(
-            out=tile[32 * q + first_row : 32 * q + first_row + 4, :].bitcast(I32),
-            in_=dram[0, 4 * q : 4 * q + 4, :].bitcast(I32),
-        )
-
-
 def deal(engine, out, in_, run):
     engine.tensor_copy(
-        out=out.rearrange("p w (t b i) -> p w b t i", t=PACK, i=run),
-        in_=in_.rearrange("p w (b i t) -> p w b t i", t=PACK, i=run),
+        out=out.rearrange("p (t b i) -> p b t i", t=PACK, i=run),
+        in_=in_.rearrange("p (b i t) -> p b t i", t=PACK, i=run),
     )
 
 
@@ -56,41 +50,44 @@ def tile_picked_segunpool_relu_po_kernel(
     with ExitStack() as ctx:
         lists = ctx.enter_context(tc.tile_pool(name="lists", bufs=1))
         sb = ctx.enter_context(tc.tile_pool(name="sb", bufs=1))
+        placed = ctx.enter_context(tc.tile_pool(name="placed", bufs=1))
         psum = ctx.enter_context(tc.psum_pool(name="psum", bufs=1))
 
         def tile(shape, dtype, name, tag=None):
             return sb.tile(shape, dtype, name=name, tag=tag or name, align_bytes=64)
 
-        placed = ctx.enter_context(tc.tile_pool(name="placed", bufs=1))
-
         def place(shape, dtype, name, offset):
             return placed.tile(shape, dtype, name=name, offset=offset, align_bytes=64)
+
+        def bank(shape, number, name):
+            return psum.tile(shape, F32, name=name, tag=f"bank{number}")
+
+        def on_gpsimd(out, in_):
+            nc.gpsimd.tensor_scalar(out=out, in0=in_, scalar1=1.0, scalar2=0.0, op0=ALU.mult, op1=ALU.add)
+
+        on_scalar, on_vector = nc.scalar.copy, nc.vector.tensor_copy
 
         offs_sb = lists.tile([P, S // 16], U16, name="offs_sb")
         skip_sb = lists.tile([P, U // 16], U16, name="skip_sb")
         where_sb = lists.tile([P, S // 16], U16, name="where_sb")
         x_bytes = tile([P, T], U8, "x_bytes")
         picked_bytes = tile([P, S], U8, "picked_bytes")
+        x_codes = tile([P, T], U32, "x_codes")
+        w1_raw = place([P, PACK, H], F32, "w1_raw", 9472)
+        windows = [tile([P, U], F32, f"window{a}") for a in range(2)]
 
-        skip_bytes = tile([P, U], U8, "skip_bytes")
         nc.gpsimd.memset(x_bytes[:ROWS_AT, :].bitcast(I32), 0)
         nc.gpsimd.memset(picked_bytes[:].bitcast(I32), 0)
-        nc.gpsimd.memset(skip_bytes[:].bitcast(I32), 0)
+        for window in windows:
+            nc.gpsimd.memset(window[:], 0.0)
         warm = tile([P, 2], F32, "warm")
         nc.vector.memset(warm[:, 0:1], 0.0)
         nc.scalar.activation(out=warm[:, 1:2], in_=warm[:, 0:1], func=ACT.Relu)
-        loads = ctx.enter_context(tc.tile_pool(name="loads", bufs=1))
-        x_codes = loads.tile([P, T], U32, name="x_codes")
-        w1_raw = [loads.tile([P, PACK, hi - lo], F32, name=f"w1_raw{lo}") for lo, hi in W1_PIECES]
-        z = [loads.tile([P, U], F32, name=f"z{t}", align_bytes=64) for t in range(PACK - 1)]
-        z.append(z[2])
 
         nc.sync.dma_start(offs_sb[:], offs)
         nc.sync.dma_start(out=x_bytes[ROWS_AT:, :].bitcast(I32), in_=x_scales[0].bitcast(I32))
-        for a, (lo, hi) in enumerate(W1_PIECES):
-            nc.sync.dma_start(out=w1_raw[a][:], in_=w1.rearrange("(p j) h -> p j h", j=PACK)[:, :, lo:hi])
-            if a == 0:
-                nc.sync.dma_start(skip_sb[:], skip)
+        nc.sync.dma_start(skip_sb[:], skip)
+        nc.sync.dma_start(out=w1_raw[:], in_=w1.rearrange("(p j) h -> p j h", j=PACK))
         nc.sync.dma_start(out=x_codes[:].bitcast(I32), in_=words_view(x_words))
         nc.sync.dma_start(where_sb[:], where)
 
@@ -100,181 +97,173 @@ def tile_picked_segunpool_relu_po_kernel(
                     out=dst[32 * q : 32 * q + 4, :].bitcast(I32), in_=src[ROWS_AT + 4 * q : ROWS_AT + 4 * q + 4, :].bitcast(I32)
                 )
 
-        last = U - QUARTER
-        picked_spread = tile([P, S], U8, "picked_spread", "w_raw")
-        skip_spread = place([P, U], U8, "skip_spread", 1792)
-        picked_codes = tile([P, S], U32, "picked_codes")
+        picked_spread = place([P, S], U8, "picked_spread", 4352 + U - S // 2)
+        skip_spread = place([P, U], U8, "skip_spread", 0)
         nc.vector.tensor_copy(out=picked_spread[:], in_=x_bytes[:].indirect(offs_sb[:]))
         place_rows(nc.scalar, picked_bytes, picked_spread)
         nc.vector.tensor_copy(out=skip_spread[:], in_=x_bytes[:].indirect(skip_sb[:]))
+        skip_bytes = place([P, U], U8, "skip_bytes", 4352)
+        nc.gpsimd.memset(skip_bytes[:].bitcast(I32), 0)
         place_rows(nc.sync, skip_bytes, skip_spread)
-        w_raw = tile([P, 2, N], U32, "w_raw")
+
+        w_raw = place([P, 2, N], U32, "w_raw", 4352 + U)
         nc.sync.dma_start(out=w_raw[:, 0, :].bitcast(I32), in_=words_view(w2_words))
         nc.sync.dma_start(out=w_raw[:, 1, :].bitcast(I32), in_=words_view(w3_words))
-        w_bytes_raw = place([P, N], U8, "w_bytes_raw", 1792)
+        w_bytes_raw = place([P, N], U8, "w_bytes_raw", 0)
         nc.gpsimd.memset(w_bytes_raw[:].bitcast(I32), 0)
-        load_scale_rows((nc.sync,), w_bytes_raw, W3_ROW, w3_scales)
-        load_scale_rows((nc.sync,), w_bytes_raw, 0, w2_scales)
-        nc.vector.tensor_copy(out=picked_codes[:, : S // 2], in_=x_codes[:].indirect(offs_sb[:, : S // 32]))
-        nc.vector.tensor_copy(out=picked_codes[:, S // 2 :], in_=x_codes[:].indirect(offs_sb[:, S // 32 :]))
+        for first_row, scales in ((W3_ROW, w3_scales), (0, w2_scales)):
+            for q in range(4):
+                nc.sync.dma_start(
+                    out=w_bytes_raw[32 * q + first_row : 32 * q + first_row + 4, :].bitcast(I32),
+                    in_=scales[0, 4 * q : 4 * q + 4, :].bitcast(I32),
+                )
 
-        def gather_skip_codes(first, count, tag):
-            codes = tile([P, count], U32, f"skip_codes{first}", tag)
-            cols = slice(first // 16, (first + count) // 16)
-            nc.vector.tensor_copy(out=codes[:], in_=x_codes[:].indirect(skip_sb[:, cols]))
+        w1_grouped = tile([P, PACK, P, PACK], BF16, "w1_grouped")
+        for copy, lo, hi in ((on_scalar, 0, SCALAR_W1), (on_vector, SCALAR_W1, P)):
+            copy(
+                out=w1_grouped[:, :, lo:hi, :].rearrange("p t m j -> p m j t"),
+                in_=w1_raw[:].rearrange("p j (m t) -> p m j t", t=PACK)[:, lo:hi, :, :],
+            )
+        w1_codes = tile([P, H], U32, "w1_codes")
+        w1_bytes = tile([P, H], U8, "w1_bytes")
+        nc.vector.quantize_mx(out=w1_codes[:].bitcast(FP8X4), scales=w1_bytes[:], in_=w1_grouped[:].rearrange("p t m j -> p (t m j)"))
+
+        picked_codes = place([P, S], U32, "picked_codes", 9472)
+        for lo in (0, S // 2):
+            nc.vector.tensor_copy(out=picked_codes[:, lo : lo + S // 2], in_=x_codes[:].indirect(offs_sb[:, lo // 16 : (lo + S // 2) // 16]))
+
+        def gather_skip_codes(codes, c):
+            nc.vector.tensor_copy(out=codes[:], in_=x_codes[:].indirect(skip_sb[:, c * QUARTER // 16 : (c + 1) * QUARTER // 16]))
             return codes
 
-        skip_codes = {0: gather_skip_codes(0, QUARTER, None)[:]}
+        skip_codes = [gather_skip_codes(place([P, QUARTER], U32, "skip_codes0", 9472 + 4 * S), 0)]
 
-        w1_codes, w1_bytes = {}, {}
-        for u in (1, 0):
-            grouped = tile([P, 2, P, PACK], BF16, f"w1_grouped{u}")
-            for a, (lo, hi) in enumerate(W1_PIECES):
-                (nc.vector.tensor_copy if (u, a) == (0, 1) else nc.scalar.copy)(
-                    out=grouped[:, :, lo // PACK : hi // PACK, :].rearrange("p t m j -> p m j t"),
-                    in_=w1_raw[a][:].rearrange("p j (m t) -> p m j t", t=PACK)[:, :, :, 2 * u : 2 * u + 2],
-                )
-            codes = tile([P, 2 * P], U32, f"w1_codes{u}")
-            scale = tile([P, 2 * P], U8, f"w1_bytes{u}")
-            nc.vector.quantize_mx(
-                out=codes[:].bitcast(FP8X4), scales=scale[:], in_=grouped[:].rearrange("p t m j -> p (t m j)")
+        def activate(t, lo, hi, number, out):
+            cols = slice(t * P, (t + 1) * P)
+            acc = bank([P, hi - lo], number, f"acc_y{t}_{lo}")
+            nc.tensor.matmul_mx(
+                out=acc[:],
+                lhsT=w1_codes[:, cols].bitcast(FP8X4),
+                lhsT_scale=w1_bytes[:, cols],
+                rhs=picked_codes[:, lo:hi].bitcast(FP8X4),
+                rhs_scale=picked_bytes[:, lo:hi],
+                start=True,
+                stop=True,
             )
-            w1_codes[u] = codes
-            w1_bytes[u] = scale
-
-        for t in (2, 0, 1):
-            nc.gpsimd.memset(z[t][:], 0.0)
-
-        def project(t, parts, bank, name):
-            cols = slice((t % 2) * P, (t % 2 + 1) * P)
-            first = parts[0][0]
-            acc = psum.tile([P, parts[-1][1] - first], F32, name=f"acc_{name}", tag=f"bank{bank}")
-            for lo, hi in parts:
-                nc.tensor.matmul_mx(
-                    out=acc[:, lo - first : hi - first],
-                    lhsT=w1_codes[t // 2][:, cols].bitcast(FP8X4),
-                    lhsT_scale=w1_bytes[t // 2][:, cols],
-                    rhs=picked_codes[:, lo:hi].bitcast(FP8X4),
-                    rhs_scale=picked_bytes[:, lo:hi],
-                    start=True,
-                    stop=True,
-                )
-            return acc
-
-        def relu(out, acc):
             nc.scalar.activation(out=out, in_=acc[:], func=ACT.Relu)
 
-        def activate(t, parts, bank, name):
-            values = tile([P, parts[-1][1] - parts[0][0]], F32, name)
-            relu(values[:], project(t, parts, bank, name))
-            return values
+        first, second, third, fourth = PLANES
+        y_first = tile([P, FIRST], F32, "y_first")
+        y = {
+            first: tile([P, S - FIRST], F32, "y_rest"),
+            second: tile([P, S], F32, "y_second"),
+            third: tile([P, S], F32, "y_third"),
+            fourth: tile([P, S], F32, "y_fourth"),
+        }
+        activate(first, 0, FIRST, 0, y_first[:])
+        activate(first, FIRST, S // 2, 1, y[first][:, : S // 2 - FIRST])
+        activate(first, S // 2, S, 2, y[first][:, S // 2 - FIRST :])
+        for number, t in enumerate((second, third, fourth)):
+            activate(t, 0, S, 3 + number, y[t][:])
 
-        y_first = activate(2, [(0, FIRST)], 0, "y_first")
-        y = {2: activate(2, [(FIRST, S // 2), (S // 2, S)], PACK + 2, "y2")}
-        for t in (0, 1, 3):
-            y[t] = activate(t, [(0, S)], PACK + t, f"y{t}")
-
-        w2_codes = tile([P, 1, N], U32, "w2_codes")
-        deal(nc.gpsimd, w2_codes[:], w_raw[:, 0:1, :], 4)
+        w2_codes = tile([P, N], U32, "w2_codes")
+        deal(nc.gpsimd, w2_codes[:], w_raw[:, 0, :], 4)
         w_bytes = tile([P, N], U8, "w_bytes")
-        deal(nc.gpsimd, w_bytes[:].unsqueeze(1), w_bytes_raw[:].unsqueeze(1), 16)
-        first_grouped = place([P, QUARTER, PACK], BF16, "first_grouped", 4096)
+        deal(nc.gpsimd, w_bytes[:], w_bytes_raw[:], 16)
+
+        first_grouped = place([P, QUARTER, PACK], BF16, "first_grouped", 2304)
         middle_grouped = tile([P, HALF, PACK], BF16, "middle_grouped")
-        last_grouped = place([P, QUARTER, PACK], BF16, "last_grouped", 2048)
-        w3_codes = place([P, 1, N], U32, "w3_codes", 0)
-
-        def on_g(out, in_):
-            nc.gpsimd.tensor_scalar(out=out, in0=in_, scalar1=1.0, scalar2=0.0, op0=ALU.mult, op1=ALU.add)
-
-        on_s, on_v = nc.scalar.copy, nc.vector.tensor_copy
+        last_grouped = place([P, QUARTER, PACK], BF16, "last_grouped", 256)
 
         def z_grouped(lo, hi):
             if hi <= QUARTER:
                 return first_grouped[:, lo:hi, :]
-            if hi <= last:
+            if hi <= LAST:
                 return middle_grouped[:, lo - QUARTER : hi - QUARTER, :]
-            return last_grouped[:, lo - last : hi - last, :]
+            return last_grouped[:, lo - LAST : hi - LAST, :]
 
-        def regroup(copy, t, lo, hi):
-            copy(out=z_grouped(lo, hi)[:, :, t], in_=z[t][:, lo:hi])
+        def regroup(copy, step, lo, hi):
+            for start, stop in ((0, QUARTER), (QUARTER, LAST), (LAST, U)):
+                start, stop = max(start, lo), min(stop, hi)
+                if start < stop:
+                    copy(out=z_grouped(start, stop)[:, :, PLANES[step]], in_=windows[step % 2][:, start:stop])
 
-        for t in (2, 0, 1, 3):
-            if t == 2:
-                nc.vector.tensor_copy(out=z[t][:].indirect(where_sb[:, : FIRST // 16]), in_=y_first[:])
-                nc.vector.tensor_copy(out=z[t][:].indirect(where_sb[:, FIRST // 16 :]), in_=y[t][:])
+        def scatter(step, values, lo, hi):
+            nc.vector.tensor_copy(out=windows[step % 2][:].indirect(where_sb[:, lo // 16 : hi // 16]), in_=values)
+
+        scatter(0, y_first[:], 0, FIRST)
+        scatter(0, y[first][:], FIRST, S)
+        for step in range(3):
+            regroup(on_scalar, step, 0, LAST)
+            if step == 2:
+                regroup(on_gpsimd, step, LAST, LAST + AHEAD_OF_DEAL)
+                w3_codes = tile([P, N], U32, "w3_codes", "y_third")
+                deal(nc.gpsimd, w3_codes[:], w_raw[:, 1, :], 4)
+                regroup(on_gpsimd, step, LAST + AHEAD_OF_DEAL, U)
             else:
-                nc.vector.tensor_copy(out=z[t][:].indirect(where_sb[:]), in_=y[t][:])
-            if t == 1:
-                regroup(on_g, t, last, last + AHEAD_OF_DEAL)
-                deal(nc.gpsimd, w3_codes[:], w_raw[:, 1:2, :], 4)
-                regroup(on_g, t, last + AHEAD_OF_DEAL, U)
-            elif t < 3:
-                regroup(on_g, t, last, U)
-            if t < 3:
-                regroup(on_s, t, 0, QUARTER)
-                regroup(on_s, t, QUARTER, last)
-        regroup(on_v, 3, 0, QUARTER)
-        regroup(on_s, 3, QUARTER, HALF)
-        regroup(on_s, 3, HALF, last)
-        regroup(on_g, 3, last, last + GPSIMD_CELLS)
-        regroup(on_s, 3, last + GPSIMD_CELLS, U)
+                regroup(on_gpsimd, step, LAST, U)
+            scatter(step + 1, y[PLANES[step + 1]][:], 0, S)
 
         def quarter(c):
             return slice(c * QUARTER, (c + 1) * QUARTER)
 
-        banks = {}
+        z_codes = tile([P, U], U32, "z_codes")
+        z_bytes = tile([P, U], U8, "z_bytes")
 
-        def add_product(c, h, skip_side):
-            opens = (c, h) not in banks
-            if opens:
-                banks[c, h] = psum.tile([P, 2, QUARTER], F32, name=f"acc{c}{h}", tag=f"bank{2 * c + h}")
-            for e in range(2):
-                cols = slice((2 * h + e) * P, (2 * h + e + 1) * P)
+        def add_product(acc, c, planes, skip_side):
+            for e, t in enumerate(planes):
+                cols = slice(t * P, (t + 1) * P)
                 nc.tensor.matmul_mx(
-                    out=banks[c, h][:, e, :],
-                    lhsT=(w3_codes if skip_side else w2_codes)[:, 0, cols].bitcast(FP8X4),
+                    out=acc[:, e, :],
+                    lhsT=(w3_codes if skip_side else w2_codes)[:, cols].bitcast(FP8X4),
                     lhsT_scale=w_bytes[W3_ROW if skip_side else 0 : P, cols],
-                    rhs=(skip_codes[c] if skip_side else z_codes[:, quarter(c)]).bitcast(FP8X4),
+                    rhs=(skip_codes[c][:] if skip_side else z_codes[:, quarter(c)]).bitcast(FP8X4),
                     rhs_scale=(skip_bytes if skip_side else z_bytes)[:, quarter(c)],
-                    start=opens and e == 0,
-                    stop=not opens and e == 1,
+                    start=skip_side and e == 0,
+                    stop=not skip_side and e == len(planes) - 1,
                 )
 
-        add_product(0, 0, True)
-        add_product(0, 1, True)
-        unread = psum.tile([P, S], F32, name="unread", tag="bank7")
+        opened = []
+
+        def open_groups(c):
+            for planes in ((0,), (1,), (2, 3)) if c == 0 else ((0, 1), (2, 3)):
+                acc = bank([P, len(planes), QUARTER], len(opened) % 8, f"acc{c}_{planes[0]}")
+                opened.append((c, planes, acc))
+                add_product(acc, c, planes, True)
+
+        open_groups(0)
+        unread = bank([P, N], 7, "unread")
         for repeat in range(WARM_PASSES):
             nc.tensor.matmul_mx(
                 out=unread[:],
-                lhsT=w3_codes[:, 0, :P].bitcast(FP8X4),
+                lhsT=w3_codes[:, :P].bitcast(FP8X4),
                 lhsT_scale=w_bytes[W3_ROW:P, :P],
-                rhs=picked_codes[:].bitcast(FP8X4),
-                rhs_scale=picked_bytes[:],
+                rhs=w2_codes[:].bitcast(FP8X4),
+                rhs_scale=w_bytes[:],
                 start=True,
                 stop=True,
             )
 
-        z_codes = tile([P, U], U32, "z_codes")
-        z_bytes = tile([P, U], U8, "z_bytes")
+        regroup(on_vector, 3, 0, VECTOR_LAST)
+        regroup(on_gpsimd, 3, LAST, LAST + GPSIMD_LAST)
+        regroup(on_scalar, 3, VECTOR_LAST, HALF)
+        regroup(on_scalar, 3, HALF, LAST)
+        regroup(on_scalar, 3, LAST + GPSIMD_LAST, U)
 
-        def quantize_z(cells):
+        def quantize_z(c):
             nc.vector.quantize_mx(
-                out=z_codes[:, cells].bitcast(FP8X4),
-                scales=z_bytes[:, cells],
-                in_=z_grouped(cells.start, cells.stop).rearrange("p c t -> p (c t)"),
+                out=z_codes[:, quarter(c)].bitcast(FP8X4),
+                scales=z_bytes[:, quarter(c)],
+                in_=z_grouped(c * QUARTER, (c + 1) * QUARTER).rearrange("p c t -> p (c t)"),
             )
 
-        def gather_late(codes, first, count):
-            nc.vector.tensor_copy(out=codes[:], in_=x_codes[:].indirect(skip_sb[:, first // 16 : (first + count) // 16]))
-            return codes
-
-        skip_codes[1] = gather_late(tile([P, QUARTER], U32, "late_codes1", "y3"), QUARTER, QUARTER)[:]
-        quantize_z(quarter(0))
-        quantize_z(quarter(1))
-        skip_codes[2] = gather_late(place([P, QUARTER], U32, "late_codes2", 4096), HALF, QUARTER)[:]
-        quantize_z(quarter(2))
-        skip_codes[3] = gather_late(loads.tile([P, QUARTER], U32, name="late_codes3", tag="z2", align_bytes=64), last, QUARTER)[:]
-        quantize_z(quarter(3))
+        skip_codes.append(gather_skip_codes(tile([P, QUARTER], U32, "skip_codes1", "y_fourth"), 1))
+        quantize_z(0)
+        quantize_z(1)
+        skip_codes.append(gather_skip_codes(place([P, QUARTER], U32, "skip_codes2", 2304), 2))
+        quantize_z(2)
+        skip_codes.append(gather_skip_codes(tile([P, QUARTER], U32, "skip_codes3", "window1"), 3))
+        quantize_z(3)
 
         out_rows = out_0.rearrange("(p t) w -> p t w", t=PACK)
         out_bytes = tile([P, HALF], U8, "out_bytes")
@@ -284,17 +273,12 @@ def tile_picked_segunpool_relu_po_kernel(
         grouped = [first_half[:, :QUARTER, :], first_half[:, QUARTER:, :]]
         grouped.extend(tile([P, QUARTER, PACK], BF16, f"out_grouped{c}")[:] for c in (2, 3))
 
-        def empty(c):
-            for h in range(2):
-                skip_first = (c, h) in SKIP_FIRST
-                if c > 0:
-                    add_product(c, h, skip_first)
-                add_product(c, h, not skip_first)
-                runs = ((0, 1), (1, 2)) if (c, h) == (0, 0) else ((0, 2),)
-                for lo, hi in runs:
-                    planes = slice(2 * h + lo, 2 * h + hi)
-                    on_s(out=result[c][:, planes, :], in_=banks[c, h][:, lo:hi, :])
-                    nc.sync.dma_start(out=out_rows[:, planes, quarter(c)], in_=result[c][:, planes, :])
+        def close_groups(c):
+            for planes, acc in [(planes, acc) for quarter_of, planes, acc in opened if quarter_of == c]:
+                add_product(acc, c, planes, False)
+                rows = slice(planes[0], planes[-1] + 1)
+                on_scalar(out=result[c][:, rows, :], in_=acc[:])
+                nc.sync.dma_start(out=out_rows[:, rows, quarter(c)], in_=result[c][:, rows, :])
 
         def interleave(c, copy, lo, hi):
             src = result[c][:, :, lo:hi].rearrange("p t (c i) -> p c t i", i=4)
@@ -308,20 +292,23 @@ def tile_picked_segunpool_relu_po_kernel(
                 in_=source.rearrange("p c t -> p (c t)"),
             )
 
-        empty(0)
-        interleave(0, on_v, 0, QUARTER)
-        empty(1)
-        interleave(1, on_v, 0, QUARTER)
+        close_groups(0)
+        interleave(0, on_vector, 0, QUARTER)
+        open_groups(1)
+        close_groups(1)
+        interleave(1, on_vector, 0, QUARTER)
         quantize_out(first_half[:], 0, slice(0, HALF))
-        empty(2)
-        interleave(2, on_v, 0, QUARTER)
+        open_groups(2)
+        close_groups(2)
+        interleave(2, on_vector, 0, QUARTER)
         quantize_out(grouped[2], 1, quarter(0))
-        empty(3)
-        interleave(3, on_s, 0, SCALAR_CELLS)
-        interleave(3, on_v, SCALAR_CELLS, QUARTER)
+        open_groups(3)
+        close_groups(3)
+        interleave(3, on_scalar, 0, SCALAR_CELLS)
+        interleave(3, on_vector, SCALAR_CELLS, QUARTER)
         quantize_out(grouped[3], 1, quarter(1))
-        nc.sync.dma_start(out=words_view(out_1)[:, :last], in_=out_codes[:, :last].bitcast(I32))
-        nc.scalar.dma_start(out=words_view(out_1)[:, last:], in_=out_codes[:, last:].bitcast(I32))
+        nc.sync.dma_start(out=words_view(out_1)[:, :LAST], in_=out_codes[:, :LAST].bitcast(I32))
+        nc.scalar.dma_start(out=words_view(out_1)[:, LAST:], in_=out_codes[:, LAST:].bitcast(I32))
         for q in range(4):
             (nc.sync if q < 3 else nc.scalar).dma_start(
                 out=out_2[0, 4 * q : 4 * q + 4, :].bitcast(I32).rearrange("r (c w) -> c r w", c=2),

@@ -23,7 +23,8 @@ LAST = U - QUARTER
 W3_ROW = 4
 ROWS_AT = 112
 FIRST = 128
-SCALAR_W1 = 76
+SCALAR_W1 = 68
+GPSIMD_W1 = 36
 PLANES = (0, 2, 1, 3)
 AHEAD_OF_DEAL = 64
 GPSIMD_LAST = 160
@@ -119,10 +120,14 @@ def tile_picked_segunpool_relu_po_kernel(
                 )
 
         w1_grouped = tile([P, PACK, P, PACK], BF16, "w1_grouped")
-        for copy, lo, hi in ((on_scalar, 0, SCALAR_W1), (on_vector, SCALAR_W1, P)):
+        for copy, order, lo, hi in (
+            (on_scalar, "p m j t", 0, SCALAR_W1),
+            (on_gpsimd, "p m t j", SCALAR_W1, SCALAR_W1 + GPSIMD_W1),
+            (on_vector, "p m j t", SCALAR_W1 + GPSIMD_W1, P),
+        ):
             copy(
-                out=w1_grouped[:, :, lo:hi, :].rearrange("p t m j -> p m j t"),
-                in_=w1_raw[:].rearrange("p j (m t) -> p m j t", t=PACK)[:, lo:hi, :, :],
+                out=w1_grouped[:, :, lo:hi, :].rearrange("p t m j -> " + order),
+                in_=w1_raw[:].rearrange("p j (m t) -> p j m t", t=PACK)[:, :, lo:hi, :].rearrange("p j m t -> " + order),
             )
         w1_codes = tile([P, H], U32, "w1_codes")
         w1_bytes = tile([P, H], U8, "w1_bytes")

@@ -19,17 +19,15 @@ P = 128
 PACK = 4
 HALF = U // 2
 QUARTER = U // 4
+EIGHTH = U // 8
 LAST = U - QUARTER
 W3_ROW = 4
 ROWS_AT = 112
 FIRST = 128
-SCALAR_W1 = 68
-GPSIMD_W1 = 36
+SCALAR_W1 = 72
 PLANES = (0, 2, 1, 3)
-AHEAD_OF_DEAL = 64
-GPSIMD_LAST = 160
-VECTOR_LAST = 256
-SCALAR_CELLS = 128
+AHEAD_OF_DEAL = 176
+SCALAR_CELLS = 144
 WARM_PASSES = 2
 
 
@@ -120,14 +118,10 @@ def tile_picked_segunpool_relu_po_kernel(
                 )
 
         w1_grouped = tile([P, PACK, P, PACK], BF16, "w1_grouped")
-        for copy, order, lo, hi in (
-            (on_scalar, "p m j t", 0, SCALAR_W1),
-            (on_gpsimd, "p m t j", SCALAR_W1, SCALAR_W1 + GPSIMD_W1),
-            (on_vector, "p m j t", SCALAR_W1 + GPSIMD_W1, P),
-        ):
+        for copy, lo, hi in ((on_scalar, 0, SCALAR_W1), (on_vector, SCALAR_W1, P)):
             copy(
-                out=w1_grouped[:, :, lo:hi, :].rearrange("p t m j -> " + order),
-                in_=w1_raw[:].rearrange("p j (m t) -> p j m t", t=PACK)[:, :, lo:hi, :].rearrange("p j m t -> " + order),
+                out=w1_grouped[:, :, lo:hi, :].rearrange("p t m j -> p m j t"),
+                in_=w1_raw[:].rearrange("p j (m t) -> p m j t", t=PACK)[:, lo:hi, :, :],
             )
         w1_codes = tile([P, H], U32, "w1_codes")
         w1_bytes = tile([P, H], U8, "w1_bytes")
@@ -176,22 +170,18 @@ def tile_picked_segunpool_relu_po_kernel(
         w_bytes = tile([P, N], U8, "w_bytes")
         deal(nc.gpsimd, w_bytes[:], w_bytes_raw[:], 16)
 
-        first_grouped = place([P, QUARTER, PACK], BF16, "first_grouped", 2304)
-        middle_grouped = tile([P, HALF, PACK], BF16, "middle_grouped")
-        last_grouped = place([P, QUARTER, PACK], BF16, "last_grouped", 256)
-
-        def z_grouped(lo, hi):
-            if hi <= QUARTER:
-                return first_grouped[:, lo:hi, :]
-            if hi <= LAST:
-                return middle_grouped[:, lo - QUARTER : hi - QUARTER, :]
-            return last_grouped[:, lo - LAST : hi - LAST, :]
+        z_grouped = [
+            place([P, QUARTER, PACK], BF16, f"z_grouped{c}", offset) for c, offset in enumerate((2304, 17664, 19712, 256))
+        ]
 
         def regroup(copy, step, lo, hi):
-            for start, stop in ((0, QUARTER), (QUARTER, LAST), (LAST, U)):
-                start, stop = max(start, lo), min(stop, hi)
+            for c in range(4):
+                start, stop = max(c * QUARTER, lo), min((c + 1) * QUARTER, hi)
                 if start < stop:
-                    copy(out=z_grouped(start, stop)[:, :, PLANES[step]], in_=windows[step % 2][:, start:stop])
+                    copy(
+                        out=z_grouped[c][:, start - c * QUARTER : stop - c * QUARTER, PLANES[step]],
+                        in_=windows[step % 2][:, start:stop],
+                    )
 
         def scatter(step, values, lo, hi):
             nc.vector.tensor_copy(out=windows[step % 2][:].indirect(where_sb[:, lo // 16 : hi // 16]), in_=values)
@@ -215,7 +205,8 @@ def tile_picked_segunpool_relu_po_kernel(
         z_codes = tile([P, U], U32, "z_codes")
         z_bytes = tile([P, U], U8, "z_bytes")
 
-        def add_product(acc, c, planes, skip_side):
+        def add_product(acc, c, planes, opens):
+            skip_side = opens == (c % 2 == 0)
             for e, t in enumerate(planes):
                 cols = slice(t * P, (t + 1) * P)
                 nc.tensor.matmul_mx(
@@ -224,19 +215,19 @@ def tile_picked_segunpool_relu_po_kernel(
                     lhsT_scale=w_bytes[W3_ROW if skip_side else 0 : P, cols],
                     rhs=(skip_codes[c][:] if skip_side else z_codes[:, quarter(c)]).bitcast(FP8X4),
                     rhs_scale=(skip_bytes if skip_side else z_bytes)[:, quarter(c)],
-                    start=skip_side and e == 0,
-                    stop=not skip_side and e == len(planes) - 1,
+                    start=opens and e == 0,
+                    stop=not opens and e == len(planes) - 1,
                 )
 
-        opened = []
+        groups = [(c, planes) for c in range(4) for planes in (((0,), (1,), (2, 3)) if c == 0 else ((0, 1), (2, 3)))]
+        accs = {}
 
-        def open_groups(c):
-            for planes in ((0,), (1,), (2, 3)) if c == 0 else ((0, 1), (2, 3)):
-                acc = bank([P, len(planes), QUARTER], len(opened) % 8, f"acc{c}_{planes[0]}")
-                opened.append((c, planes, acc))
-                add_product(acc, c, planes, True)
+        def open_group(c, planes):
+            accs[c, planes] = bank([P, len(planes), QUARTER], len(accs) % 8, f"acc{c}_{planes[0]}")
+            add_product(accs[c, planes], c, planes, True)
 
-        open_groups(0)
+        for c, planes in groups[:3]:
+            open_group(c, planes)
         unread = bank([P, N], 7, "unread")
         for repeat in range(WARM_PASSES):
             nc.tensor.matmul_mx(
@@ -249,69 +240,70 @@ def tile_picked_segunpool_relu_po_kernel(
                 stop=True,
             )
 
-        regroup(on_vector, 3, 0, VECTOR_LAST)
-        regroup(on_gpsimd, 3, LAST, LAST + GPSIMD_LAST)
-        regroup(on_scalar, 3, VECTOR_LAST, HALF)
-        regroup(on_scalar, 3, HALF, LAST)
-        regroup(on_scalar, 3, LAST + GPSIMD_LAST, U)
+        regroup(on_vector, 3, 0, HALF)
+        regroup(on_scalar, 3, HALF, U)
 
         def quantize_z(c):
             nc.vector.quantize_mx(
                 out=z_codes[:, quarter(c)].bitcast(FP8X4),
                 scales=z_bytes[:, quarter(c)],
-                in_=z_grouped(c * QUARTER, (c + 1) * QUARTER).rearrange("p c t -> p (c t)"),
+                in_=z_grouped[c][:].rearrange("p c t -> p (c t)"),
             )
 
-        skip_codes.append(gather_skip_codes(tile([P, QUARTER], U32, "skip_codes1", "y_fourth"), 1))
         quantize_z(0)
         quantize_z(1)
-        skip_codes.append(gather_skip_codes(place([P, QUARTER], U32, "skip_codes2", 2304), 2))
+        skip_codes.append(gather_skip_codes(place([P, QUARTER], U32, "skip_codes1", 2304), 1))
+        skip_codes.append(gather_skip_codes(place([P, QUARTER], U32, "skip_codes2", 17664), 2))
         quantize_z(2)
-        skip_codes.append(gather_skip_codes(tile([P, QUARTER], U32, "skip_codes3", "window1"), 3))
         quantize_z(3)
+        skip_codes.append(gather_skip_codes(place([P, QUARTER], U32, "skip_codes3", 19712), 3))
 
         out_rows = out_0.rearrange("(p t) w -> p t w", t=PACK)
         out_bytes = tile([P, HALF], U8, "out_bytes")
         out_codes = tile([P, U], U32, "out_codes")
         result = [tile([P, PACK, QUARTER], F32, f"result{c}") for c in range(4)]
-        first_half = tile([P, HALF, PACK], BF16, "out_grouped01")
-        grouped = [first_half[:, :QUARTER, :], first_half[:, QUARTER:, :]]
-        grouped.extend(tile([P, QUARTER, PACK], BF16, f"out_grouped{c}")[:] for c in (2, 3))
+        early_grouped = tile([P, LAST, PACK], BF16, "early_grouped")
+        late_grouped = tile([P, QUARTER, PACK], BF16, "late_grouped")
 
-        def close_groups(c):
-            for planes, acc in [(planes, acc) for quarter_of, planes, acc in opened if quarter_of == c]:
-                add_product(acc, c, planes, False)
-                rows = slice(planes[0], planes[-1] + 1)
-                on_scalar(out=result[c][:, rows, :], in_=acc[:])
-                nc.sync.dma_start(out=out_rows[:, rows, quarter(c)], in_=result[c][:, rows, :])
+        def out_grouped(lo, hi):
+            return early_grouped[:, lo:hi, :] if hi <= LAST else late_grouped[:, lo - LAST : hi - LAST, :]
 
-        def interleave(c, copy, lo, hi):
-            src = result[c][:, :, lo:hi].rearrange("p t (c i) -> p c t i", i=4)
-            dst = grouped[c][:, lo:hi, :].rearrange("p (c i) t -> p c t i", i=4)
-            copy(out=dst, in_=src)
+        def close_groups(quarter_number):
+            for c, planes in groups:
+                if c == quarter_number:
+                    if c > 0:
+                        open_group(c, planes)
+                    add_product(accs[c, planes], c, planes, False)
+                    rows = slice(planes[0], planes[-1] + 1)
+                    on_scalar(out=result[c][:, rows, :], in_=accs[c, planes][:])
+                    nc.sync.dma_start(out=out_rows[:, rows, quarter(c)], in_=result[c][:, rows, :])
 
-        def quantize_out(source, half, cells):
+        def interleave(copy, lo, hi):
+            c = lo // QUARTER
+            src = result[c][:, :, lo - c * QUARTER : hi - c * QUARTER].rearrange("p t (c i) -> p c t i", i=4)
+            copy(out=out_grouped(lo, hi).rearrange("p (c i) t -> p c t i", i=4), in_=src)
+
+        def quantize_out(lo, hi):
+            half = lo // HALF
             nc.vector.quantize_mx(
-                out=out_codes[:, half * HALF + cells.start : half * HALF + cells.stop].bitcast(FP8X4),
-                scales=out_bytes[4 * half : P, cells],
-                in_=source.rearrange("p c t -> p (c t)"),
+                out=out_codes[:, lo:hi].bitcast(FP8X4),
+                scales=out_bytes[4 * half : P, lo - half * HALF : hi - half * HALF],
+                in_=out_grouped(lo, hi).rearrange("p c t -> p (c t)"),
             )
 
         close_groups(0)
-        interleave(0, on_vector, 0, QUARTER)
-        open_groups(1)
-        close_groups(1)
-        interleave(1, on_vector, 0, QUARTER)
-        quantize_out(first_half[:], 0, slice(0, HALF))
-        open_groups(2)
-        close_groups(2)
-        interleave(2, on_vector, 0, QUARTER)
-        quantize_out(grouped[2], 1, quarter(0))
-        open_groups(3)
+        interleave(on_vector, 0, QUARTER)
+        for c, start in ((1, 0), (2, HALF)):
+            middle = c * QUARTER + EIGHTH
+            close_groups(c)
+            interleave(on_vector, c * QUARTER, middle)
+            interleave(on_vector, middle, middle + EIGHTH)
+            quantize_out(start, middle)
+            quantize_out(middle, middle + EIGHTH)
         close_groups(3)
-        interleave(3, on_scalar, 0, SCALAR_CELLS)
-        interleave(3, on_vector, SCALAR_CELLS, QUARTER)
-        quantize_out(grouped[3], 1, quarter(1))
+        interleave(on_scalar, LAST, LAST + SCALAR_CELLS)
+        interleave(on_vector, LAST + SCALAR_CELLS, U)
+        quantize_out(LAST, U)
         nc.sync.dma_start(out=words_view(out_1)[:, :LAST], in_=out_codes[:, :LAST].bitcast(I32))
         nc.scalar.dma_start(out=words_view(out_1)[:, LAST:], in_=out_codes[:, LAST:].bitcast(I32))
         for q in range(4):

@@ -24,9 +24,9 @@ LAST = U - QUARTER
 W3_ROW = 4
 ROWS_AT = 112
 FIRST = 128
-SCALAR_W1 = 72
 PLANES = (0, 2, 1, 3)
 AHEAD_OF_DEAL = 176
+GPSIMD_LAST = 160
 SCALAR_CELLS = 144
 WARM_PASSES = 2
 
@@ -71,12 +71,14 @@ def tile_picked_segunpool_relu_po_kernel(
         where_sb = lists.tile([P, S // 16], U16, name="where_sb")
         x_bytes = tile([P, T], U8, "x_bytes")
         picked_bytes = tile([P, S], U8, "picked_bytes")
+        skip_bytes = tile([P, U], U8, "skip_bytes")
         x_codes = tile([P, T], U32, "x_codes")
-        w1_raw = place([P, PACK, H], F32, "w1_raw", 9472)
+        w1_raw = [tile([P, PACK, H // 2], F32, "w1_raw0"), place([P, PACK, H // 2], F32, "w1_raw1", 9472)]
         windows = [tile([P, U], F32, f"window{a}") for a in range(2)]
 
         nc.gpsimd.memset(x_bytes[:ROWS_AT, :].bitcast(I32), 0)
         nc.gpsimd.memset(picked_bytes[:].bitcast(I32), 0)
+        nc.gpsimd.memset(skip_bytes[:].bitcast(I32), 0)
         for window in windows:
             nc.gpsimd.memset(window[:], 0.0)
         warm = tile([P, 2], F32, "warm")
@@ -85,8 +87,10 @@ def tile_picked_segunpool_relu_po_kernel(
 
         nc.sync.dma_start(offs_sb[:], offs)
         nc.sync.dma_start(out=x_bytes[ROWS_AT:, :].bitcast(I32), in_=x_scales[0].bitcast(I32))
+        w1_rows = w1.rearrange("(p j) h -> p j h", j=PACK)
+        nc.sync.dma_start(out=w1_raw[0][:], in_=w1_rows[:, :, : H // 2])
         nc.sync.dma_start(skip_sb[:], skip)
-        nc.sync.dma_start(out=w1_raw[:], in_=w1.rearrange("(p j) h -> p j h", j=PACK))
+        nc.sync.dma_start(out=w1_raw[1][:], in_=w1_rows[:, :, H // 2 :])
         nc.sync.dma_start(out=x_codes[:].bitcast(I32), in_=words_view(x_words))
         nc.sync.dma_start(where_sb[:], where)
 
@@ -101,8 +105,6 @@ def tile_picked_segunpool_relu_po_kernel(
         nc.vector.tensor_copy(out=picked_spread[:], in_=x_bytes[:].indirect(offs_sb[:]))
         place_rows(nc.scalar, picked_bytes, picked_spread)
         nc.vector.tensor_copy(out=skip_spread[:], in_=x_bytes[:].indirect(skip_sb[:]))
-        skip_bytes = place([P, U], U8, "skip_bytes", 4352)
-        nc.gpsimd.memset(skip_bytes[:].bitcast(I32), 0)
         place_rows(nc.sync, skip_bytes, skip_spread)
 
         w_raw = place([P, 2, N], U32, "w_raw", 4352 + U)
@@ -117,15 +119,19 @@ def tile_picked_segunpool_relu_po_kernel(
                     in_=scales[0, 4 * q : 4 * q + 4, :].bitcast(I32),
                 )
 
-        w1_grouped = tile([P, PACK, P, PACK], BF16, "w1_grouped")
-        for copy, lo, hi in ((on_scalar, 0, SCALAR_W1), (on_vector, SCALAR_W1, P)):
-            copy(
-                out=w1_grouped[:, :, lo:hi, :].rearrange("p t m j -> p m j t"),
-                in_=w1_raw[:].rearrange("p j (m t) -> p m j t", t=PACK)[:, lo:hi, :, :],
-            )
         w1_codes = tile([P, H], U32, "w1_codes")
         w1_bytes = tile([P, H], U8, "w1_bytes")
-        nc.vector.quantize_mx(out=w1_codes[:].bitcast(FP8X4), scales=w1_bytes[:], in_=w1_grouped[:].rearrange("p t m j -> p (t m j)"))
+        for u in range(2):
+            w1_grouped = tile([P, 2, P, PACK], BF16, f"w1_grouped{u}")
+            for a in range(2):
+                (on_vector if (u, a) == (1, 1) else on_scalar)(
+                    out=w1_grouped[:, :, a * P // 2 : (a + 1) * P // 2, :].rearrange("p t m j -> p m j t"),
+                    in_=w1_raw[a][:].rearrange("p j (m t) -> p m j t", t=PACK)[:, :, :, 2 * u : 2 * u + 2],
+                )
+            cols = slice(2 * u * P, 2 * (u + 1) * P)
+            nc.vector.quantize_mx(
+                out=w1_codes[:, cols].bitcast(FP8X4), scales=w1_bytes[:, cols], in_=w1_grouped[:].rearrange("p t m j -> p (t m j)")
+            )
 
         picked_codes = place([P, S], U32, "picked_codes", 9472)
         for lo in (0, S // 2):
@@ -165,15 +171,6 @@ def tile_picked_segunpool_relu_po_kernel(
         for number, t in enumerate((second, third, fourth)):
             activate(t, 0, S, 3 + number, y[t][:])
 
-        w2_codes = tile([P, N], U32, "w2_codes")
-        deal(nc.gpsimd, w2_codes[:], w_raw[:, 0, :], 4)
-        w_bytes = tile([P, N], U8, "w_bytes")
-        deal(nc.gpsimd, w_bytes[:], w_bytes_raw[:], 16)
-
-        z_grouped = [
-            place([P, QUARTER, PACK], BF16, f"z_grouped{c}", offset) for c, offset in enumerate((2304, 17664, 19712, 256))
-        ]
-
         def regroup(copy, step, lo, hi):
             for c in range(4):
                 start, stop = max(c * QUARTER, lo), min((c + 1) * QUARTER, hi)
@@ -188,6 +185,16 @@ def tile_picked_segunpool_relu_po_kernel(
 
         scatter(0, y_first[:], 0, FIRST)
         scatter(0, y[first][:], FIRST, S)
+
+        w2_codes = tile([P, N], U32, "w2_codes", "y_first")
+        deal(nc.gpsimd, w2_codes[:], w_raw[:, 0, :], 4)
+        w_bytes = tile([P, N], U8, "w_bytes")
+        deal(nc.gpsimd, w_bytes[:], w_bytes_raw[:], 16)
+
+        z_grouped = [
+            place([P, QUARTER, PACK], BF16, f"z_grouped{c}", offset) for c, offset in enumerate((2304, 17664, 19712, 256))
+        ]
+
         for step in range(3):
             regroup(on_scalar, step, 0, LAST)
             if step == 2:
@@ -205,8 +212,7 @@ def tile_picked_segunpool_relu_po_kernel(
         z_codes = tile([P, U], U32, "z_codes")
         z_bytes = tile([P, U], U8, "z_bytes")
 
-        def add_product(acc, c, planes, opens):
-            skip_side = opens == (c % 2 == 0)
+        def add_product(acc, c, planes, skip_side):
             for e, t in enumerate(planes):
                 cols = slice(t * P, (t + 1) * P)
                 nc.tensor.matmul_mx(
@@ -215,8 +221,8 @@ def tile_picked_segunpool_relu_po_kernel(
                     lhsT_scale=w_bytes[W3_ROW if skip_side else 0 : P, cols],
                     rhs=(skip_codes[c][:] if skip_side else z_codes[:, quarter(c)]).bitcast(FP8X4),
                     rhs_scale=(skip_bytes if skip_side else z_bytes)[:, quarter(c)],
-                    start=opens and e == 0,
-                    stop=not opens and e == len(planes) - 1,
+                    start=skip_side and e == 0,
+                    stop=not skip_side and e == len(planes) - 1,
                 )
 
         groups = [(c, planes) for c in range(4) for planes in (((0,), (1,), (2, 3)) if c == 0 else ((0, 1), (2, 3)))]
@@ -240,8 +246,10 @@ def tile_picked_segunpool_relu_po_kernel(
                 stop=True,
             )
 
-        regroup(on_vector, 3, 0, HALF)
-        regroup(on_scalar, 3, HALF, U)
+        regroup(on_vector, 3, 0, QUARTER)
+        regroup(on_gpsimd, 3, LAST, LAST + GPSIMD_LAST)
+        regroup(on_scalar, 3, QUARTER, LAST)
+        regroup(on_scalar, 3, LAST + GPSIMD_LAST, U)
 
         def quantize_z(c):
             nc.vector.quantize_mx(
@@ -250,13 +258,13 @@ def tile_picked_segunpool_relu_po_kernel(
                 in_=z_grouped[c][:].rearrange("p c t -> p (c t)"),
             )
 
+        skip_codes.append(gather_skip_codes(tile([P, QUARTER], U32, "skip_codes1", "y_fourth"), 1))
         quantize_z(0)
         quantize_z(1)
-        skip_codes.append(gather_skip_codes(place([P, QUARTER], U32, "skip_codes1", 2304), 1))
-        skip_codes.append(gather_skip_codes(place([P, QUARTER], U32, "skip_codes2", 17664), 2))
+        skip_codes.append(gather_skip_codes(place([P, QUARTER], U32, "skip_codes2", 2304), 2))
         quantize_z(2)
+        skip_codes.append(gather_skip_codes(place([P, QUARTER], U32, "skip_codes3", 17664), 3))
         quantize_z(3)
-        skip_codes.append(gather_skip_codes(place([P, QUARTER], U32, "skip_codes3", 19712), 3))
 
         out_rows = out_0.rearrange("(p t) w -> p t w", t=PACK)
         out_bytes = tile([P, HALF], U8, "out_bytes")

@@ -24,7 +24,7 @@ LAST = U - QUARTER
 W3_ROW = 4
 ROWS_AT = 112
 FIRST = 128
-PLANES = (0, 2, 1, 3)
+PLANES = (2, 0, 1, 3)
 AHEAD_OF_DEAL = 176
 GPSIMD_LAST = 160
 SCALAR_CELLS = 144
@@ -74,7 +74,7 @@ def tile_picked_segunpool_relu_po_kernel(
         skip_bytes = tile([P, U], U8, "skip_bytes")
         x_codes = tile([P, T], U32, "x_codes")
         w1_raw = [tile([P, PACK, H // 2], F32, "w1_raw0"), place([P, PACK, H // 2], F32, "w1_raw1", 9472)]
-        windows = [tile([P, U], F32, f"window{a}") for a in range(2)]
+        windows = [tile([P, U], F32, f"window{a}") for a in range(3)]
 
         nc.gpsimd.memset(x_bytes[:ROWS_AT, :].bitcast(I32), 0)
         nc.gpsimd.memset(picked_bytes[:].bitcast(I32), 0)
@@ -101,7 +101,7 @@ def tile_picked_segunpool_relu_po_kernel(
                 )
 
         picked_spread = place([P, S], U8, "picked_spread", 4352 + U - S // 2)
-        skip_spread = place([P, U], U8, "skip_spread", 0)
+        skip_spread = place([P, U], U8, "skip_spread", 2048)
         nc.vector.tensor_copy(out=picked_spread[:], in_=x_bytes[:].indirect(offs_sb[:]))
         place_rows(nc.scalar, picked_bytes, picked_spread)
         nc.vector.tensor_copy(out=skip_spread[:], in_=x_bytes[:].indirect(skip_sb[:]))
@@ -110,7 +110,7 @@ def tile_picked_segunpool_relu_po_kernel(
         w_raw = place([P, 2, N], U32, "w_raw", 4352 + U)
         nc.sync.dma_start(out=w_raw[:, 0, :].bitcast(I32), in_=words_view(w2_words))
         nc.sync.dma_start(out=w_raw[:, 1, :].bitcast(I32), in_=words_view(w3_words))
-        w_bytes_raw = place([P, N], U8, "w_bytes_raw", 0)
+        w_bytes_raw = place([P, N], U8, "w_bytes_raw", 2048)
         nc.gpsimd.memset(w_bytes_raw[:].bitcast(I32), 0)
         for first_row, scales in ((W3_ROW, w3_scales), (0, w2_scales)):
             for q in range(4):
@@ -121,10 +121,10 @@ def tile_picked_segunpool_relu_po_kernel(
 
         w1_codes = tile([P, H], U32, "w1_codes")
         w1_bytes = tile([P, H], U8, "w1_bytes")
-        for u in range(2):
+        for u in (1, 0):
             w1_grouped = tile([P, 2, P, PACK], BF16, f"w1_grouped{u}")
             for a in range(2):
-                (on_vector if (u, a) == (1, 1) else on_scalar)(
+                (on_vector if (u, a) == (0, 1) else on_scalar)(
                     out=w1_grouped[:, :, a * P // 2 : (a + 1) * P // 2, :].rearrange("p t m j -> p m j t"),
                     in_=w1_raw[a][:].rearrange("p j (m t) -> p m j t", t=PACK)[:, :, :, 2 * u : 2 * u + 2],
                 )
@@ -162,7 +162,7 @@ def tile_picked_segunpool_relu_po_kernel(
         y = {
             first: tile([P, S - FIRST], F32, "y_rest"),
             second: tile([P, S], F32, "y_second"),
-            third: tile([P, S], F32, "y_third"),
+            third: place([P, S], F32, "y_third", 0),
             fourth: tile([P, S], F32, "y_fourth"),
         }
         activate(first, 0, FIRST, 0, y_first[:])
@@ -177,29 +177,29 @@ def tile_picked_segunpool_relu_po_kernel(
                 if start < stop:
                     copy(
                         out=z_grouped[c][:, start - c * QUARTER : stop - c * QUARTER, PLANES[step]],
-                        in_=windows[step % 2][:, start:stop],
+                        in_=windows[step % 3][:, start:stop],
                     )
 
         def scatter(step, values, lo, hi):
-            nc.vector.tensor_copy(out=windows[step % 2][:].indirect(where_sb[:, lo // 16 : hi // 16]), in_=values)
+            nc.vector.tensor_copy(out=windows[step % 3][:].indirect(where_sb[:, lo // 16 : hi // 16]), in_=values)
 
         scatter(0, y_first[:], 0, FIRST)
         scatter(0, y[first][:], FIRST, S)
 
-        w2_codes = tile([P, N], U32, "w2_codes", "y_first")
+        w2_codes = tile([P, N], U32, "w2_codes")
         deal(nc.gpsimd, w2_codes[:], w_raw[:, 0, :], 4)
         w_bytes = tile([P, N], U8, "w_bytes")
         deal(nc.gpsimd, w_bytes[:], w_bytes_raw[:], 16)
 
         z_grouped = [
-            place([P, QUARTER, PACK], BF16, f"z_grouped{c}", offset) for c, offset in enumerate((2304, 17664, 19712, 256))
+            place([P, QUARTER, PACK], BF16, f"z_grouped{c}", offset) for c, offset in enumerate((21760, 17664, 19712, 2304))
         ]
 
         for step in range(3):
             regroup(on_scalar, step, 0, LAST)
             if step == 2:
                 regroup(on_gpsimd, step, LAST, LAST + AHEAD_OF_DEAL)
-                w3_codes = tile([P, N], U32, "w3_codes", "y_third")
+                w3_codes = place([P, N], U32, "w3_codes", 256)
                 deal(nc.gpsimd, w3_codes[:], w_raw[:, 1, :], 4)
                 regroup(on_gpsimd, step, LAST + AHEAD_OF_DEAL, U)
             else:
@@ -261,7 +261,7 @@ def tile_picked_segunpool_relu_po_kernel(
         skip_codes.append(gather_skip_codes(tile([P, QUARTER], U32, "skip_codes1", "y_fourth"), 1))
         quantize_z(0)
         quantize_z(1)
-        skip_codes.append(gather_skip_codes(place([P, QUARTER], U32, "skip_codes2", 2304), 2))
+        skip_codes.append(gather_skip_codes(place([P, QUARTER], U32, "skip_codes2", 21760), 2))
         quantize_z(2)
         skip_codes.append(gather_skip_codes(place([P, QUARTER], U32, "skip_codes3", 17664), 3))
         quantize_z(3)

@@ -25,9 +25,9 @@ W3_ROW = 4
 ROWS_AT = 112
 FIRST = 128
 PLANES = (2, 0, 1, 3)
-AHEAD_OF_DEAL = 176
-GPSIMD_LAST = 160
+FINAL = U - EIGHTH
 SCALAR_CELLS = 144
+CUTS = (0, QUARTER, HALF, LAST, FINAL, U)
 WARM_PASSES = 2
 
 
@@ -172,11 +172,11 @@ def tile_picked_segunpool_relu_po_kernel(
             activate(t, 0, S, 3 + number, y[t][:])
 
         def regroup(copy, step, lo, hi):
-            for c in range(4):
-                start, stop = max(c * QUARTER, lo), min((c + 1) * QUARTER, hi)
+            for grouped, first_cell, end_cell in zip(z_grouped, CUTS, CUTS[1:]):
+                start, stop = max(first_cell, lo), min(end_cell, hi)
                 if start < stop:
                     copy(
-                        out=z_grouped[c][:, start - c * QUARTER : stop - c * QUARTER, PLANES[step]],
+                        out=grouped[:, start - first_cell : stop - first_cell, PLANES[step]],
                         in_=windows[step % 3][:, start:stop],
                     )
 
@@ -192,18 +192,16 @@ def tile_picked_segunpool_relu_po_kernel(
         deal(nc.gpsimd, w_bytes[:], w_bytes_raw[:], 16)
 
         z_grouped = [
-            place([P, QUARTER, PACK], BF16, f"z_grouped{c}", offset) for c, offset in enumerate((21760, 17664, 19712, 2304))
+            place([P, hi - lo, PACK], BF16, f"z_grouped{lo}", offset)
+            for lo, hi, offset in zip(CUTS, CUTS[1:], (21760, 17664, 19712, 23808, 2304))
         ]
 
         for step in range(3):
-            regroup(on_scalar, step, 0, LAST)
+            regroup(on_scalar, step, 0, FINAL)
+            regroup(on_gpsimd, step, FINAL, U)
             if step == 2:
-                regroup(on_gpsimd, step, LAST, LAST + AHEAD_OF_DEAL)
                 w3_codes = place([P, N], U32, "w3_codes", 256)
                 deal(nc.gpsimd, w3_codes[:], w_raw[:, 1, :], 4)
-                regroup(on_gpsimd, step, LAST + AHEAD_OF_DEAL, U)
-            else:
-                regroup(on_gpsimd, step, LAST, U)
             scatter(step + 1, y[PLANES[step + 1]][:], 0, S)
 
         def quarter(c):
@@ -247,14 +245,13 @@ def tile_picked_segunpool_relu_po_kernel(
             )
 
         regroup(on_vector, 3, 0, QUARTER)
-        regroup(on_gpsimd, 3, LAST, LAST + GPSIMD_LAST)
-        regroup(on_scalar, 3, QUARTER, LAST)
-        regroup(on_scalar, 3, LAST + GPSIMD_LAST, U)
+        regroup(on_gpsimd, 3, FINAL, U)
+        regroup(on_scalar, 3, QUARTER, FINAL)
 
         def quantize_z(c):
             nc.vector.quantize_mx(
-                out=z_codes[:, quarter(c)].bitcast(FP8X4),
-                scales=z_bytes[:, quarter(c)],
+                out=z_codes[:, CUTS[c] : CUTS[c + 1]].bitcast(FP8X4),
+                scales=z_bytes[:, CUTS[c] : CUTS[c + 1]],
                 in_=z_grouped[c][:].rearrange("p c t -> p (c t)"),
             )
 
@@ -265,6 +262,7 @@ def tile_picked_segunpool_relu_po_kernel(
         quantize_z(2)
         skip_codes.append(gather_skip_codes(place([P, QUARTER], U32, "skip_codes3", 17664), 3))
         quantize_z(3)
+        quantize_z(4)
 
         out_rows = out_0.rearrange("(p t) w -> p t w", t=PACK)
         out_bytes = tile([P, HALF], U8, "out_bytes")

@@ -27,7 +27,8 @@ FIRST = 128
 PLANES = (2, 0, 1, 3)
 FINAL = U - EIGHTH
 SCALAR_CELLS = 144
-CUTS = (0, QUARTER, HALF, LAST, FINAL, U)
+CUTS = (0, EIGHTH, QUARTER, HALF, LAST, FINAL, U)
+FILL = 64
 WARM_PASSES = 2
 
 
@@ -134,8 +135,8 @@ def tile_picked_segunpool_relu_po_kernel(
             )
 
         picked_codes = place([P, S], U32, "picked_codes", 9472)
-        for lo in (0, S // 2):
-            nc.vector.tensor_copy(out=picked_codes[:, lo : lo + S // 2], in_=x_codes[:].indirect(offs_sb[:, lo // 16 : (lo + S // 2) // 16]))
+        for lo, hi in ((0, FIRST), (FIRST, S // 2), (S // 2, S)):
+            nc.vector.tensor_copy(out=picked_codes[:, lo:hi], in_=x_codes[:].indirect(offs_sb[:, lo // 16 : hi // 16]))
 
         def gather_skip_codes(codes, c):
             nc.vector.tensor_copy(out=codes[:], in_=x_codes[:].indirect(skip_sb[:, c * QUARTER // 16 : (c + 1) * QUARTER // 16]))
@@ -193,15 +194,18 @@ def tile_picked_segunpool_relu_po_kernel(
 
         z_grouped = [
             place([P, hi - lo, PACK], BF16, f"z_grouped{lo}", offset)
-            for lo, hi, offset in zip(CUTS, CUTS[1:], (21760, 17664, 19712, 23808, 2304))
+            for lo, hi, offset in zip(CUTS, CUTS[1:], (21760, 22784, 17664, 19712, 23808, 2304))
         ]
 
         for step in range(3):
             regroup(on_scalar, step, 0, FINAL)
-            regroup(on_gpsimd, step, FINAL, U)
             if step == 2:
+                regroup(on_gpsimd, step, FINAL, FINAL + FILL)
                 w3_codes = place([P, N], U32, "w3_codes", 256)
                 deal(nc.gpsimd, w3_codes[:], w_raw[:, 1, :], 4)
+                regroup(on_gpsimd, step, FINAL + FILL, U)
+            else:
+                regroup(on_gpsimd, step, FINAL, U)
             scatter(step + 1, y[PLANES[step + 1]][:], 0, S)
 
         def quarter(c):
@@ -245,8 +249,8 @@ def tile_picked_segunpool_relu_po_kernel(
             )
 
         regroup(on_vector, 3, 0, QUARTER)
-        regroup(on_gpsimd, 3, FINAL, U)
-        regroup(on_scalar, 3, QUARTER, FINAL)
+        regroup(on_scalar, 3, QUARTER, HALF)
+        regroup(on_scalar, 3, LAST, U)
 
         def quantize_z(c):
             nc.vector.quantize_mx(
@@ -255,14 +259,18 @@ def tile_picked_segunpool_relu_po_kernel(
                 in_=z_grouped[c][:].rearrange("p c t -> p (c t)"),
             )
 
-        skip_codes.append(gather_skip_codes(tile([P, QUARTER], U32, "skip_codes1", "y_fourth"), 1))
         quantize_z(0)
         quantize_z(1)
-        skip_codes.append(gather_skip_codes(place([P, QUARTER], U32, "skip_codes2", 21760), 2))
+        skip_codes.append(gather_skip_codes(place([P, QUARTER], U32, "skip_codes1", 21760), 1))
         quantize_z(2)
-        skip_codes.append(gather_skip_codes(place([P, QUARTER], U32, "skip_codes3", 17664), 3))
+        for lo in range(HALF, HALF + 2 * FILL, FILL):
+            regroup(on_vector, 3, lo, lo + FILL)
+        regroup(on_vector, 3, HALF + 2 * FILL, LAST)
+        skip_codes.append(gather_skip_codes(place([P, QUARTER], U32, "skip_codes2", 22784), 2))
         quantize_z(3)
+        skip_codes.append(gather_skip_codes(place([P, QUARTER], U32, "skip_codes3", 17664), 3))
         quantize_z(4)
+        quantize_z(5)
 
         out_rows = out_0.rearrange("(p t) w -> p t w", t=PACK)
         out_bytes = tile([P, HALF], U8, "out_bytes")

@@ -26,7 +26,6 @@ ROWS_AT = 112
 FIRST = 128
 PLANES = (2, 0, 1, 3)
 FINAL = U - EIGHTH
-SCALAR_CELLS = 144
 CUTS = (0, EIGHTH, QUARTER, HALF, LAST, FINAL, U)
 FILL = 64
 WARM_PASSES = 2
@@ -82,12 +81,11 @@ def tile_picked_segunpool_relu_po_kernel(
         nc.gpsimd.memset(skip_bytes[:].bitcast(I32), 0)
         for window in windows:
             nc.gpsimd.memset(window[:], 0.0)
+        nc.sync.dma_start(offs_sb[:], offs)
+        nc.scalar.dma_start(out=x_bytes[ROWS_AT:, :].bitcast(I32), in_=x_scales[0].bitcast(I32))
         warm = tile([P, 2], F32, "warm")
         nc.vector.memset(warm[:, 0:1], 0.0)
         nc.scalar.activation(out=warm[:, 1:2], in_=warm[:, 0:1], func=ACT.Relu)
-
-        nc.sync.dma_start(offs_sb[:], offs)
-        nc.sync.dma_start(out=x_bytes[ROWS_AT:, :].bitcast(I32), in_=x_scales[0].bitcast(I32))
         w1_rows = w1.rearrange("(p j) h -> p j h", j=PACK)
         nc.sync.dma_start(out=w1_raw[0][:], in_=w1_rows[:, :, : H // 2])
         nc.sync.dma_start(skip_sb[:], skip)
@@ -227,7 +225,7 @@ def tile_picked_segunpool_relu_po_kernel(
                     stop=not skip_side and e == len(planes) - 1,
                 )
 
-        groups = [(c, planes) for c in range(4) for planes in (((0,), (1,), (2, 3)) if c == 0 else ((0, 1), (2, 3)))]
+        groups = [(c, planes) for c in range(3) for planes in (((0,), (1,), (2, 3)) if c == 0 else ((0, 1), (2, 3)))]
         accs = {}
 
         def open_group(c, planes):
@@ -276,11 +274,11 @@ def tile_picked_segunpool_relu_po_kernel(
         out_bytes = tile([P, HALF], U8, "out_bytes")
         out_codes = tile([P, U], U32, "out_codes")
         result = [tile([P, PACK, QUARTER], F32, f"result{c}") for c in range(4)]
-        early_grouped = tile([P, LAST, PACK], BF16, "early_grouped")
-        late_grouped = tile([P, QUARTER, PACK], BF16, "late_grouped")
+        early_grouped = tile([P, FINAL, PACK], BF16, "early_grouped")
+        late_grouped = tile([P, EIGHTH, PACK], BF16, "late_grouped")
 
         def out_grouped(lo, hi):
-            return early_grouped[:, lo:hi, :] if hi <= LAST else late_grouped[:, lo - LAST : hi - LAST, :]
+            return early_grouped[:, lo:hi, :] if hi <= FINAL else late_grouped[:, lo - FINAL : hi - FINAL, :]
 
         def close_groups(quarter_number):
             for c, planes in groups:
@@ -314,10 +312,27 @@ def tile_picked_segunpool_relu_po_kernel(
             interleave(on_vector, middle, middle + EIGHTH)
             quantize_out(start, middle)
             quantize_out(middle, middle + EIGHTH)
-        close_groups(3)
-        interleave(on_scalar, LAST, LAST + SCALAR_CELLS)
-        interleave(on_vector, LAST + SCALAR_CELLS, U)
-        quantize_out(LAST, U)
+        for a in range(2):
+            lo, hi = LAST + a * EIGHTH, LAST + (a + 1) * EIGHTH
+            acc = bank([P, PACK, EIGHTH], (7 + a) % 8, f"acc_last{a}")
+            for skip_side in (True, False):
+                for t in range(PACK):
+                    cols = slice(t * P, (t + 1) * P)
+                    nc.tensor.matmul_mx(
+                        out=acc[:, t, :],
+                        lhsT=(w3_codes if skip_side else w2_codes)[:, cols].bitcast(FP8X4),
+                        lhsT_scale=w_bytes[W3_ROW if skip_side else 0 : P, cols],
+                        rhs=(skip_codes[3][:, lo - LAST : hi - LAST] if skip_side else z_codes[:, lo:hi]).bitcast(FP8X4),
+                        rhs_scale=(skip_bytes if skip_side else z_bytes)[:, lo:hi],
+                        start=skip_side and t == 0,
+                        stop=not skip_side and t == PACK - 1,
+                    )
+            on_scalar(out=result[3][:, :, lo - LAST : hi - LAST], in_=acc[:])
+            nc.sync.dma_start(out=out_rows[:, :, lo:hi], in_=result[3][:, :, lo - LAST : hi - LAST])
+        interleave(on_vector, LAST, FINAL)
+        interleave(on_scalar, FINAL, U)
+        quantize_out(LAST, FINAL)
+        quantize_out(FINAL, U)
         nc.sync.dma_start(out=words_view(out_1)[:, :LAST], in_=out_codes[:, :LAST].bitcast(I32))
         nc.scalar.dma_start(out=words_view(out_1)[:, LAST:], in_=out_codes[:, LAST:].bitcast(I32))
         for q in range(4):

@@ -19,16 +19,12 @@ P = 128
 PACK = 4
 HALF = U // 2
 QUARTER = U // 4
-EIGHTH = U // 8
-LAST = U - QUARTER
-W3_ROW = 4
+PIECE = U // 8
+PIECES = 8
 ROWS_AT = 112
+W3_ROW = 4
 FIRST = 128
-PLANES = (2, 0, 1, 3)
-FINAL = U - EIGHTH
-CUTS = (0, EIGHTH, QUARTER, HALF, LAST, FINAL, U)
-FILL = 64
-WARM_PASSES = 2
+KB = 1024
 
 
 def words_view(dram):
@@ -52,11 +48,11 @@ def tile_picked_segunpool_relu_po_kernel(
         placed = ctx.enter_context(tc.tile_pool(name="placed", bufs=1))
         psum = ctx.enter_context(tc.psum_pool(name="psum", bufs=1))
 
-        def tile(shape, dtype, name, tag=None):
-            return sb.tile(shape, dtype, name=name, tag=tag or name, align_bytes=64)
+        def tile(shape, dtype, name):
+            return sb.tile(shape, dtype, name=name, tag=name, align_bytes=256)
 
         def place(shape, dtype, name, offset):
-            return placed.tile(shape, dtype, name=name, offset=offset, align_bytes=64)
+            return placed.tile(shape, dtype, name=name, offset=offset, align_bytes=256)
 
         def bank(shape, number, name):
             return psum.tile(shape, F32, name=name, tag=f"bank{number}")
@@ -72,20 +68,23 @@ def tile_picked_segunpool_relu_po_kernel(
         x_bytes = tile([P, T], U8, "x_bytes")
         picked_bytes = tile([P, S], U8, "picked_bytes")
         skip_bytes = tile([P, U], U8, "skip_bytes")
-        x_codes = tile([P, T], U32, "x_codes")
-        w1_raw = [tile([P, PACK, H // 2], F32, "w1_raw0"), place([P, PACK, H // 2], F32, "w1_raw1", 9472)]
-        windows = [tile([P, U], F32, f"window{a}") for a in range(3)]
+        x_codes = place([P, T], U32, "x_codes", 16 * KB)
+        w1_raw = [tile([P, PACK, H // 2], F32, "w1_raw0"), place([P, PACK, H // 2], F32, "w1_raw1", 10 * KB)]
+        windows = {t: tile([P, U], F32, f"window{t}") for t in (3, 0, 1)}
+        windows[2] = place([P, U], F32, "window2", 24 * KB)
 
         nc.gpsimd.memset(x_bytes[:ROWS_AT, :].bitcast(I32), 0)
         nc.gpsimd.memset(picked_bytes[:].bitcast(I32), 0)
         nc.gpsimd.memset(skip_bytes[:].bitcast(I32), 0)
-        for window in windows:
-            nc.gpsimd.memset(window[:], 0.0)
+        for t in (0, 1):
+            nc.gpsimd.memset(windows[t][:], 0.0)
         nc.sync.dma_start(offs_sb[:], offs)
         nc.scalar.dma_start(out=x_bytes[ROWS_AT:, :].bitcast(I32), in_=x_scales[0].bitcast(I32))
         warm = tile([P, 2], F32, "warm")
         nc.vector.memset(warm[:, 0:1], 0.0)
         nc.scalar.activation(out=warm[:, 1:2], in_=warm[:, 0:1], func=ACT.Relu)
+        for t in (2, 3):
+            nc.vector.memset(windows[t][:], 0.0)
         w1_rows = w1.rearrange("(p j) h -> p j h", j=PACK)
         nc.sync.dma_start(out=w1_raw[0][:], in_=w1_rows[:, :, : H // 2])
         nc.sync.dma_start(skip_sb[:], skip)
@@ -99,17 +98,18 @@ def tile_picked_segunpool_relu_po_kernel(
                     out=dst[32 * q : 32 * q + 4, :].bitcast(I32), in_=src[ROWS_AT + 4 * q : ROWS_AT + 4 * q + 4, :].bitcast(I32)
                 )
 
-        picked_spread = place([P, S], U8, "picked_spread", 4352 + U - S // 2)
-        skip_spread = place([P, U], U8, "skip_spread", 2048)
+        picked_spread = place([P, S], U8, "picked_spread", 8 * KB - S // 2)
+        skip_spread = place([P, U], U8, "skip_spread", 0)
         nc.vector.tensor_copy(out=picked_spread[:], in_=x_bytes[:].indirect(offs_sb[:]))
         place_rows(nc.scalar, picked_bytes, picked_spread)
         nc.vector.tensor_copy(out=skip_spread[:], in_=x_bytes[:].indirect(skip_sb[:]))
         place_rows(nc.sync, skip_bytes, skip_spread)
 
-        w_raw = place([P, 2, N], U32, "w_raw", 4352 + U)
-        nc.sync.dma_start(out=w_raw[:, 0, :].bitcast(I32), in_=words_view(w2_words))
-        nc.sync.dma_start(out=w_raw[:, 1, :].bitcast(I32), in_=words_view(w3_words))
-        w_bytes_raw = place([P, N], U8, "w_bytes_raw", 2048)
+        w2_raw = place([P, N], U32, "w2_raw", 6 * KB)
+        w3_raw = place([P, N], U32, "w3_raw", 8 * KB)
+        nc.sync.dma_start(out=w2_raw[:].bitcast(I32), in_=words_view(w2_words))
+        nc.sync.dma_start(out=w3_raw[:].bitcast(I32), in_=words_view(w3_words))
+        w_bytes_raw = place([P, N], U8, "w_bytes_raw", 0)
         nc.gpsimd.memset(w_bytes_raw[:].bitcast(I32), 0)
         for first_row, scales in ((W3_ROW, w3_scales), (0, w2_scales)):
             for q in range(4):
@@ -132,15 +132,11 @@ def tile_picked_segunpool_relu_po_kernel(
                 out=w1_codes[:, cols].bitcast(FP8X4), scales=w1_bytes[:, cols], in_=w1_grouped[:].rearrange("p t m j -> p (t m j)")
             )
 
-        picked_codes = place([P, S], U32, "picked_codes", 9472)
+        picked_codes = place([P, S], U32, "picked_codes", 10 * KB)
         for lo, hi in ((0, FIRST), (FIRST, S // 2), (S // 2, S)):
             nc.vector.tensor_copy(out=picked_codes[:, lo:hi], in_=x_codes[:].indirect(offs_sb[:, lo // 16 : hi // 16]))
-
-        def gather_skip_codes(codes, c):
-            nc.vector.tensor_copy(out=codes[:], in_=x_codes[:].indirect(skip_sb[:, c * QUARTER // 16 : (c + 1) * QUARTER // 16]))
-            return codes
-
-        skip_codes = [gather_skip_codes(place([P, QUARTER], U32, "skip_codes0", 9472 + 4 * S), 0)]
+        skip_codes = place([P, U], U32, "skip_codes", 12 * KB)
+        nc.vector.tensor_copy(out=skip_codes[:], in_=x_codes[:].indirect(skip_sb[:]))
 
         def activate(t, lo, hi, number, out):
             cols = slice(t * P, (t + 1) * P)
@@ -156,185 +152,134 @@ def tile_picked_segunpool_relu_po_kernel(
             )
             nc.scalar.activation(out=out, in_=acc[:], func=ACT.Relu)
 
-        first, second, third, fourth = PLANES
-        y_first = tile([P, FIRST], F32, "y_first")
-        y = {
-            first: tile([P, S - FIRST], F32, "y_rest"),
-            second: tile([P, S], F32, "y_second"),
-            third: place([P, S], F32, "y_third", 0),
-            fourth: tile([P, S], F32, "y_fourth"),
-        }
-        activate(first, 0, FIRST, 0, y_first[:])
-        activate(first, FIRST, S // 2, 1, y[first][:, : S // 2 - FIRST])
-        activate(first, S // 2, S, 2, y[first][:, S // 2 - FIRST :])
-        for number, t in enumerate((second, third, fourth)):
-            activate(t, 0, S, 3 + number, y[t][:])
-
-        def regroup(copy, step, lo, hi):
-            for grouped, first_cell, end_cell in zip(z_grouped, CUTS, CUTS[1:]):
-                start, stop = max(first_cell, lo), min(end_cell, hi)
-                if start < stop:
-                    copy(
-                        out=grouped[:, start - first_cell : stop - first_cell, PLANES[step]],
-                        in_=windows[step % 3][:, start:stop],
-                    )
-
-        def scatter(step, values, lo, hi):
-            nc.vector.tensor_copy(out=windows[step % 3][:].indirect(where_sb[:, lo // 16 : hi // 16]), in_=values)
-
-        scatter(0, y_first[:], 0, FIRST)
-        scatter(0, y[first][:], FIRST, S)
-
-        w2_codes = tile([P, N], U32, "w2_codes")
-        deal(nc.gpsimd, w2_codes[:], w_raw[:, 0, :], 4)
-        w_bytes = tile([P, N], U8, "w_bytes")
-        deal(nc.gpsimd, w_bytes[:], w_bytes_raw[:], 16)
-
-        z_grouped = [
-            place([P, hi - lo, PACK], BF16, f"z_grouped{lo}", offset)
-            for lo, hi, offset in zip(CUTS, CUTS[1:], (21760, 22784, 17664, 19712, 23808, 2304))
-        ]
-
-        for step in range(3):
-            regroup(on_scalar, step, 0, FINAL)
-            if step == 2:
-                regroup(on_gpsimd, step, FINAL, FINAL + FILL)
-                w3_codes = place([P, N], U32, "w3_codes", 256)
-                deal(nc.gpsimd, w3_codes[:], w_raw[:, 1, :], 4)
-                regroup(on_gpsimd, step, FINAL + FILL, U)
+        def scatter(t, values, lo, hi):
+            target = windows[t][:].indirect(where_sb[:, lo // 16 : hi // 16])
+            if t in (2, 1):
+                nc.scalar.activation(out=target, in_=values, func=ACT.Copy)
             else:
-                regroup(on_gpsimd, step, FINAL, U)
-            scatter(step + 1, y[PLANES[step + 1]][:], 0, S)
+                nc.vector.tensor_copy(out=target, in_=values)
 
-        def quarter(c):
-            return slice(c * QUARTER, (c + 1) * QUARTER)
+        y_first = tile([P, FIRST], F32, "y_first")
+        y = {t: tile([P, S - FIRST if t == 2 else S], F32, f"y{t}") for t in range(PACK)}
+        activate(2, 0, FIRST, 0, y_first[:])
+        activate(2, FIRST, S // 2, 1, y[2][:, : S // 2 - FIRST])
+        scatter(2, y_first[:], 0, FIRST)
+        activate(2, S // 2, S, 2, y[2][:, S // 2 - FIRST :])
+        activate(3, 0, S, 3, y[3][:])
+        scatter(2, y[2][:], FIRST, S)
+        scatter(3, y[3][:], 0, S)
+        activate(1, 0, S, 4, y[1][:])
+        activate(0, 0, S, 5, y[0][:])
+        scatter(1, y[1][:], 0, S)
+        scatter(0, y[0][:], 0, S)
+
+        w_bytes = place([P, N], U8, "w_bytes", 18 * KB)
+        deal(nc.gpsimd, w_bytes[:], w_bytes_raw[:], 16)
+        w2_codes = place([P, N], U32, "w2_codes", 16 * KB)
+        deal(nc.gpsimd, w2_codes[:], w2_raw[:], 4)
+
+        z_pairs = place([P, PIECES, 2, PIECE, 2], BF16, "z_pairs", 0)
+
+        def pair_up(copy, t, first, end):
+            copy(
+                out=z_pairs[:, first:end, t // 2, :, t % 2],
+                in_=windows[t][:, first * PIECE : end * PIECE].rearrange("p (a c) -> p a c", c=PIECE),
+            )
+
+        pair_up(on_gpsimd, 2, 0, PIECES)
+        pair_up(on_gpsimd, 3, 0, PIECES // 2)
+        w3_codes = place([P, N], U32, "w3_codes", 24 * KB)
+        deal(nc.gpsimd, w3_codes[:], w3_raw[:], 4)
+        pair_up(on_gpsimd, 3, PIECES // 2, PIECES)
 
         z_codes = tile([P, U], U32, "z_codes")
         z_bytes = tile([P, U], U8, "z_bytes")
 
-        def add_product(acc, c, planes, skip_side):
-            for e, t in enumerate(planes):
+        def cells(first, end):
+            return slice(first * PIECE, end * PIECE)
+
+        def add_product(acc, piece, skip_side):
+            for t in range(PACK):
                 cols = slice(t * P, (t + 1) * P)
                 nc.tensor.matmul_mx(
-                    out=acc[:, e, :],
+                    out=acc[:, t, :],
                     lhsT=(w3_codes if skip_side else w2_codes)[:, cols].bitcast(FP8X4),
                     lhsT_scale=w_bytes[W3_ROW if skip_side else 0 : P, cols],
-                    rhs=(skip_codes[c][:] if skip_side else z_codes[:, quarter(c)]).bitcast(FP8X4),
-                    rhs_scale=(skip_bytes if skip_side else z_bytes)[:, quarter(c)],
-                    start=skip_side and e == 0,
-                    stop=not skip_side and e == len(planes) - 1,
+                    rhs=(skip_codes if skip_side else z_codes)[:, cells(piece, piece + 1)].bitcast(FP8X4),
+                    rhs_scale=(skip_bytes if skip_side else z_bytes)[:, cells(piece, piece + 1)],
+                    start=skip_side and t == 0,
+                    stop=not skip_side and t == PACK - 1,
                 )
 
-        groups = [(c, planes) for c in range(3) for planes in (((0,), (1,), (2, 3)) if c == 0 else ((0, 1), (2, 3)))]
-        accs = {}
+        accs = [bank([P, PACK, PIECE], piece, f"acc{piece}") for piece in range(PIECES)]
+        for piece in range(PIECES):
+            add_product(accs[piece], piece, True)
 
-        def open_group(c, planes):
-            accs[c, planes] = bank([P, len(planes), QUARTER], len(accs) % 8, f"acc{c}_{planes[0]}")
-            add_product(accs[c, planes], c, planes, True)
+        z_grouped = {}
 
-        for c, planes in groups[:3]:
-            open_group(c, planes)
-        unread = bank([P, N], 7, "unread")
-        for repeat in range(WARM_PASSES):
-            nc.tensor.matmul_mx(
-                out=unread[:],
-                lhsT=w3_codes[:, :P].bitcast(FP8X4),
-                lhsT_scale=w_bytes[W3_ROW:P, :P],
-                rhs=w2_codes[:].bitcast(FP8X4),
-                rhs_scale=w_bytes[:],
-                start=True,
-                stop=True,
+        def weave(first, end):
+            grouped = tile([P, (end - first) * PIECE, PACK], BF16, f"z_grouped{first}")
+            z_grouped[first] = grouped
+            nc.vector.tensor_copy(
+                out=grouped[:].rearrange("p c t -> p (c t)").bitcast(I32).rearrange("p (a c u) -> p a c u", c=PIECE, u=2),
+                in_=z_pairs[:, first:end].rearrange("p a u c e -> p (a u c e)").bitcast(I32).rearrange("p (a u c) -> p a c u", c=PIECE, u=2),
             )
 
-        regroup(on_vector, 3, 0, QUARTER)
-        regroup(on_scalar, 3, QUARTER, HALF)
-        regroup(on_scalar, 3, LAST, U)
-
-        def quantize_z(c):
+        def quantize_z(first, end):
             nc.vector.quantize_mx(
-                out=z_codes[:, CUTS[c] : CUTS[c + 1]].bitcast(FP8X4),
-                scales=z_bytes[:, CUTS[c] : CUTS[c + 1]],
-                in_=z_grouped[c][:].rearrange("p c t -> p (c t)"),
+                out=z_codes[:, cells(first, end)].bitcast(FP8X4),
+                scales=z_bytes[:, cells(first, end)],
+                in_=z_grouped[first][:].rearrange("p c t -> p (c t)"),
             )
 
-        quantize_z(0)
-        quantize_z(1)
-        skip_codes.append(gather_skip_codes(place([P, QUARTER], U32, "skip_codes1", 21760), 1))
-        quantize_z(2)
-        for lo in range(HALF, HALF + 2 * FILL, FILL):
-            regroup(on_vector, 3, lo, lo + FILL)
-        regroup(on_vector, 3, HALF + 2 * FILL, LAST)
-        skip_codes.append(gather_skip_codes(place([P, QUARTER], U32, "skip_codes2", 22784), 2))
-        quantize_z(3)
-        skip_codes.append(gather_skip_codes(place([P, QUARTER], U32, "skip_codes3", 17664), 3))
-        quantize_z(4)
-        quantize_z(5)
+        pair_up(on_vector, 0, 0, 2)
+        pair_up(on_vector, 1, 0, 1)
+        pair_up(on_vector, 1, 1, 2)
+        for first in (2, 4):
+            pair_up(on_scalar, 0, first, first + 2)
+            pair_up(on_scalar, 1, first, first + 2)
+        weave(0, 1)
+        weave(1, 2)
+        quantize_z(0, 1)
+        quantize_z(1, 2)
+        weave(2, 4)
+        pair_up(on_vector, 0, 6, 8)
+        quantize_z(2, 4)
+        pair_up(on_vector, 1, 6, 8)
+        weave(4, 6)
+        weave(6, 8)
+        quantize_z(4, 6)
+        quantize_z(6, 8)
 
         out_rows = out_0.rearrange("(p t) w -> p t w", t=PACK)
         out_bytes = tile([P, HALF], U8, "out_bytes")
         out_codes = tile([P, U], U32, "out_codes")
-        result = [tile([P, PACK, QUARTER], F32, f"result{c}") for c in range(4)]
-        early_grouped = tile([P, FINAL, PACK], BF16, "early_grouped")
-        late_grouped = tile([P, EIGHTH, PACK], BF16, "late_grouped")
+        result = [tile([P, PACK, PIECE], F32, f"result{piece}") for piece in range(PIECES)]
+        out_grouped = [tile([P, PIECE, PACK], BF16, f"out_grouped{piece}") for piece in range(PIECES)]
 
-        def out_grouped(lo, hi):
-            return early_grouped[:, lo:hi, :] if hi <= FINAL else late_grouped[:, lo - FINAL : hi - FINAL, :]
-
-        def close_groups(quarter_number):
-            for c, planes in groups:
-                if c == quarter_number:
-                    if c > 0:
-                        open_group(c, planes)
-                    add_product(accs[c, planes], c, planes, False)
-                    rows = slice(planes[0], planes[-1] + 1)
-                    on_scalar(out=result[c][:, rows, :], in_=accs[c, planes][:])
-                    nc.sync.dma_start(out=out_rows[:, rows, quarter(c)], in_=result[c][:, rows, :])
-
-        def interleave(copy, lo, hi):
-            c = lo // QUARTER
-            src = result[c][:, :, lo - c * QUARTER : hi - c * QUARTER].rearrange("p t (c i) -> p c t i", i=4)
-            copy(out=out_grouped(lo, hi).rearrange("p (c i) t -> p c t i", i=4), in_=src)
-
-        def quantize_out(lo, hi):
-            half = lo // HALF
+        def quantize_out(piece):
+            half, at = divmod(piece * PIECE, HALF)
             nc.vector.quantize_mx(
-                out=out_codes[:, lo:hi].bitcast(FP8X4),
-                scales=out_bytes[4 * half : P, lo - half * HALF : hi - half * HALF],
-                in_=out_grouped(lo, hi).rearrange("p c t -> p (c t)"),
+                out=out_codes[:, cells(piece, piece + 1)].bitcast(FP8X4),
+                scales=out_bytes[4 * half : P, at : at + PIECE],
+                in_=out_grouped[piece][:].rearrange("p c t -> p (c t)"),
             )
 
-        close_groups(0)
-        interleave(on_vector, 0, QUARTER)
-        for c, start in ((1, 0), (2, HALF)):
-            middle = c * QUARTER + EIGHTH
-            close_groups(c)
-            interleave(on_vector, c * QUARTER, middle)
-            interleave(on_vector, middle, middle + EIGHTH)
-            quantize_out(start, middle)
-            quantize_out(middle, middle + EIGHTH)
-        for a in range(2):
-            lo, hi = LAST + a * EIGHTH, LAST + (a + 1) * EIGHTH
-            acc = bank([P, PACK, EIGHTH], (7 + a) % 8, f"acc_last{a}")
-            for skip_side in (True, False):
-                for t in range(PACK):
-                    cols = slice(t * P, (t + 1) * P)
-                    nc.tensor.matmul_mx(
-                        out=acc[:, t, :],
-                        lhsT=(w3_codes if skip_side else w2_codes)[:, cols].bitcast(FP8X4),
-                        lhsT_scale=w_bytes[W3_ROW if skip_side else 0 : P, cols],
-                        rhs=(skip_codes[3][:, lo - LAST : hi - LAST] if skip_side else z_codes[:, lo:hi]).bitcast(FP8X4),
-                        rhs_scale=(skip_bytes if skip_side else z_bytes)[:, lo:hi],
-                        start=skip_side and t == 0,
-                        stop=not skip_side and t == PACK - 1,
-                    )
-            on_scalar(out=result[3][:, :, lo - LAST : hi - LAST], in_=acc[:])
-            nc.sync.dma_start(out=out_rows[:, :, lo:hi], in_=result[3][:, :, lo - LAST : hi - LAST])
-        interleave(on_vector, LAST, FINAL)
-        interleave(on_scalar, FINAL, U)
-        quantize_out(LAST, FINAL)
-        quantize_out(FINAL, U)
-        nc.sync.dma_start(out=words_view(out_1)[:, :LAST], in_=out_codes[:, :LAST].bitcast(I32))
-        nc.scalar.dma_start(out=words_view(out_1)[:, LAST:], in_=out_codes[:, LAST:].bitcast(I32))
+        for piece in range(PIECES):
+            add_product(accs[piece], piece, False)
+            on_scalar(out=result[piece][:], in_=accs[piece][:])
+            nc.sync.dma_start(out=out_rows[:, :, cells(piece, piece + 1)], in_=result[piece][:])
+            last = piece == PIECES - 1
+            (on_scalar if last else on_vector)(
+                out=out_grouped[piece][:].rearrange("p (c i) t -> p c t i", i=4),
+                in_=result[piece][:].rearrange("p t (c i) -> p c t i", i=4),
+            )
+            if piece > 0:
+                quantize_out(piece - 1)
+        quantize_out(PIECES - 1)
+        split = U - QUARTER
+        nc.sync.dma_start(out=words_view(out_1)[:, :split], in_=out_codes[:, :split].bitcast(I32))
+        nc.scalar.dma_start(out=words_view(out_1)[:, split:], in_=out_codes[:, split:].bitcast(I32))
         for q in range(4):
             (nc.sync if q < 3 else nc.scalar).dma_start(
                 out=out_2[0, 4 * q : 4 * q + 4, :].bitcast(I32).rearrange("r (c w) -> c r w", c=2),

@@ -24,6 +24,8 @@ PIECES = 8
 ROWS_AT = 112
 W3_ROW = 4
 FIRST = 128
+SHARE = 256
+W2_ROWS_AT = 96
 KB = 1024
 
 
@@ -68,14 +70,15 @@ def tile_picked_segunpool_relu_po_kernel(
         x_bytes = tile([P, T], U8, "x_bytes")
         picked_bytes = tile([P, S], U8, "picked_bytes")
         skip_bytes = tile([P, U], U8, "skip_bytes")
-        x_codes = place([P, T], U32, "x_codes", 16 * KB)
-        w1_raw = [tile([P, PACK, H // 2], F32, "w1_raw0"), place([P, PACK, H // 2], F32, "w1_raw1", 10 * KB)]
-        windows = {t: tile([P, U], F32, f"window{t}") for t in (3, 0, 1)}
-        windows[2] = place([P, U], F32, "window2", 24 * KB)
+        x_codes = place([P, T], U32, "x_codes", 44 * KB)
+        w1_raw = [place([P, PACK, H // 2], F32, "w1_raw0", 30 * KB), place([P, PACK, H // 2], F32, "w1_raw1", 20 * KB)]
+        w_bytes = tile([P, N], U8, "w_bytes")
+        windows = [place([P, U], F32, f"window{t}", offset * KB) for t, offset in enumerate((80, 40, 124, 120))]
 
         nc.gpsimd.memset(x_bytes[:ROWS_AT, :].bitcast(I32), 0)
         nc.gpsimd.memset(picked_bytes[:].bitcast(I32), 0)
         nc.gpsimd.memset(skip_bytes[:].bitcast(I32), 0)
+        nc.gpsimd.memset(w_bytes[:].bitcast(I32), 0)
         for t in (0, 1):
             nc.gpsimd.memset(windows[t][:], 0.0)
         nc.sync.dma_start(offs_sb[:], offs)
@@ -92,31 +95,28 @@ def tile_picked_segunpool_relu_po_kernel(
         nc.sync.dma_start(out=x_codes[:].bitcast(I32), in_=words_view(x_words))
         nc.sync.dma_start(where_sb[:], where)
 
-        def place_rows(queue, dst, src):
+        def place_rows(queue, dst, src, rows_at=ROWS_AT, first_row=0):
             for q in range(4):
                 queue.dma_start(
-                    out=dst[32 * q : 32 * q + 4, :].bitcast(I32), in_=src[ROWS_AT + 4 * q : ROWS_AT + 4 * q + 4, :].bitcast(I32)
+                    out=dst[32 * q + first_row : 32 * q + first_row + 4, :].bitcast(I32),
+                    in_=src[rows_at + 4 * q : rows_at + 4 * q + 4, :].bitcast(I32),
                 )
 
-        picked_spread = place([P, S], U8, "picked_spread", 8 * KB - S // 2)
+        picked_spread = place([P, S], U8, "picked_spread", 10 * KB)
         skip_spread = place([P, U], U8, "skip_spread", 0)
         nc.vector.tensor_copy(out=picked_spread[:], in_=x_bytes[:].indirect(offs_sb[:]))
         place_rows(nc.scalar, picked_bytes, picked_spread)
         nc.vector.tensor_copy(out=skip_spread[:], in_=x_bytes[:].indirect(skip_sb[:]))
         place_rows(nc.sync, skip_bytes, skip_spread)
 
-        w2_raw = place([P, N], U32, "w2_raw", 6 * KB)
-        w3_raw = place([P, N], U32, "w3_raw", 8 * KB)
+        w2_raw = place([P, N], U32, "w2_raw", 10 * KB + S // 2)
+        w3_raw = place([P, N], U32, "w3_raw", 30 * KB)
         nc.sync.dma_start(out=w2_raw[:].bitcast(I32), in_=words_view(w2_words))
+        w_bytes_raw = place([P, N], U8, "w_bytes_raw", 10 * KB - S // 2)
+        nc.gpsimd.memset(w_bytes_raw[:W2_ROWS_AT, :].bitcast(I32), 0)
+        nc.sync.dma_start(out=w_bytes_raw[W2_ROWS_AT:ROWS_AT, :].bitcast(I32), in_=w2_scales[0].bitcast(I32))
+        nc.sync.dma_start(out=w_bytes_raw[ROWS_AT:, :].bitcast(I32), in_=w3_scales[0].bitcast(I32))
         nc.sync.dma_start(out=w3_raw[:].bitcast(I32), in_=words_view(w3_words))
-        w_bytes_raw = place([P, N], U8, "w_bytes_raw", 0)
-        nc.gpsimd.memset(w_bytes_raw[:].bitcast(I32), 0)
-        for first_row, scales in ((W3_ROW, w3_scales), (0, w2_scales)):
-            for q in range(4):
-                nc.sync.dma_start(
-                    out=w_bytes_raw[32 * q + first_row : 32 * q + first_row + 4, :].bitcast(I32),
-                    in_=scales[0, 4 * q : 4 * q + 4, :].bitcast(I32),
-                )
 
         w1_codes = tile([P, H], U32, "w1_codes")
         w1_bytes = tile([P, H], U8, "w1_bytes")
@@ -132,13 +132,19 @@ def tile_picked_segunpool_relu_po_kernel(
                 out=w1_codes[:, cols].bitcast(FP8X4), scales=w1_bytes[:, cols], in_=w1_grouped[:].rearrange("p t m j -> p (t m j)")
             )
 
-        picked_codes = place([P, S], U32, "picked_codes", 10 * KB)
+        picked_codes = place([P, S], U32, "picked_codes", 20 * KB)
         for lo, hi in ((0, FIRST), (FIRST, S // 2), (S // 2, S)):
             nc.vector.tensor_copy(out=picked_codes[:, lo:hi], in_=x_codes[:].indirect(offs_sb[:, lo // 16 : hi // 16]))
-        skip_codes = place([P, U], U32, "skip_codes", 12 * KB)
+        skip_codes = place([P, U], U32, "skip_codes", 22 * KB)
         nc.vector.tensor_copy(out=skip_codes[:], in_=x_codes[:].indirect(skip_sb[:]))
 
-        def activate(t, lo, hi, number, out):
+        def relu_on_scalar(out, in_):
+            nc.scalar.activation(out=out, in_=in_, func=ACT.Relu)
+
+        def relu_on_vector(out, in_):
+            nc.vector.tensor_scalar_max(out, in_, 0.0)
+
+        def activate(relu, t, lo, hi, number, out):
             cols = slice(t * P, (t + 1) * P)
             acc = bank([P, hi - lo], number, f"acc_y{t}_{lo}")
             nc.tensor.matmul_mx(
@@ -150,35 +156,47 @@ def tile_picked_segunpool_relu_po_kernel(
                 start=True,
                 stop=True,
             )
-            nc.scalar.activation(out=out, in_=acc[:], func=ACT.Relu)
+            relu(out, acc[:])
 
-        def scatter(t, values, lo, hi):
+        def scatter(by_scalar, t, values, lo, hi):
             target = windows[t][:].indirect(where_sb[:, lo // 16 : hi // 16])
-            if t in (2, 1):
+            if by_scalar:
                 nc.scalar.activation(out=target, in_=values, func=ACT.Copy)
             else:
                 nc.vector.tensor_copy(out=target, in_=values)
 
-        y_first = tile([P, FIRST], F32, "y_first")
-        y = {t: tile([P, S - FIRST if t == 2 else S], F32, f"y{t}") for t in range(PACK)}
-        activate(2, 0, FIRST, 0, y_first[:])
-        activate(2, FIRST, S // 2, 1, y[2][:, : S // 2 - FIRST])
-        scatter(2, y_first[:], 0, FIRST)
-        activate(2, S // 2, S, 2, y[2][:, S // 2 - FIRST :])
-        activate(3, 0, S, 3, y[3][:])
-        scatter(2, y[2][:], FIRST, S)
-        scatter(3, y[3][:], 0, S)
-        activate(1, 0, S, 4, y[1][:])
-        activate(0, 0, S, 5, y[0][:])
-        scatter(1, y[1][:], 0, S)
-        scatter(0, y[0][:], 0, S)
+        y_first = place([P, FIRST], F32, "y_first", 36 * KB)
+        y_second = tile([P, FIRST], F32, "y_second")
+        y_rest = place([P, S // 2], F32, "y_rest", 35 * KB + 2 * FIRST)
+        y_early = place([P, S], F32, "y_early", 36 * KB + 2 * FIRST)
+        y_late = place([P, 2, S], F32, "y_late", 12 * KB)
+        y = {3: y_early[:], 0: y_late[:, 0, :], 1: y_late[:, 1, :]}
+        activate(relu_on_scalar, 2, 0, FIRST, 0, y_first[:])
+        activate(relu_on_scalar, 2, FIRST, S // 2, 1, y_second[:])
+        scatter(True, 2, y_first[:], 0, FIRST)
+        scatter(True, 2, y_second[:], FIRST, S // 2)
+        activate(relu_on_scalar, 2, S // 2, S, 2, y_rest[:])
+        scatter(True, 2, y_rest[:], S // 2, S)
+        for number, t in enumerate((3, 0, 1)):
+            activate(relu_on_vector, t, 0, S, 3 + number, y[t])
+        scatter(True, 3, y[3], 0, S)
+        scatter(False, 0, y[0][:, :SHARE], 0, SHARE)
+        scatter(False, 1, y[1], 0, S)
+        scatter(True, 0, y[0][:, SHARE:], SHARE, S)
 
-        w_bytes = place([P, N], U8, "w_bytes", 18 * KB)
-        deal(nc.gpsimd, w_bytes[:], w_bytes_raw[:], 16)
-        w2_codes = place([P, N], U32, "w2_codes", 16 * KB)
+        w2_codes = tile([P, N], U32, "w2_codes")
         deal(nc.gpsimd, w2_codes[:], w2_raw[:], 4)
+        w_bytes_spread = tile([P, N], U8, "w_bytes_spread")
+        deal(nc.gpsimd, w_bytes_spread[:], w_bytes_raw[:], 16)
+        w3_codes = tile([P, N], U32, "w3_codes")
+        deal(nc.gpsimd, w3_codes[:], w3_raw[:], 4)
+        place_rows(nc.sync, w_bytes, w_bytes_spread, ROWS_AT, W3_ROW)
+        place_rows(nc.sync, w_bytes, w_bytes_spread, W2_ROWS_AT)
 
-        z_pairs = place([P, PIECES, 2, PIECE, 2], BF16, "z_pairs", 0)
+        z_pairs = place([P, PIECES, 2, PIECE, 2], BF16, "z_pairs", 3 * KB)
+
+        def cells(first, end):
+            return slice(first * PIECE, end * PIECE)
 
         def pair_up(copy, t, first, end):
             copy(
@@ -188,32 +206,32 @@ def tile_picked_segunpool_relu_po_kernel(
 
         pair_up(on_gpsimd, 2, 0, PIECES)
         pair_up(on_gpsimd, 3, 0, PIECES // 2)
-        w3_codes = place([P, N], U32, "w3_codes", 24 * KB)
-        deal(nc.gpsimd, w3_codes[:], w3_raw[:], 4)
         pair_up(on_gpsimd, 3, PIECES // 2, PIECES)
 
         z_codes = tile([P, U], U32, "z_codes")
         z_bytes = tile([P, U], U8, "z_bytes")
 
-        def cells(first, end):
-            return slice(first * PIECE, end * PIECE)
+        groups = [(0, 1, 0, 4), (1, 2, 0, 4), (2, 4, 0, 2), (2, 4, 2, 4), (4, 6, 0, 2), (4, 6, 2, 4), (6, 7, 0, 4), (7, 8, 0, 4)]
 
-        def add_product(acc, piece, skip_side):
-            for t in range(PACK):
+        def add_product(acc, group, skip_side):
+            first, end, first_plane, end_plane = group
+            for t in range(first_plane, end_plane):
                 cols = slice(t * P, (t + 1) * P)
                 nc.tensor.matmul_mx(
-                    out=acc[:, t, :],
+                    out=acc[:, t - first_plane, :],
                     lhsT=(w3_codes if skip_side else w2_codes)[:, cols].bitcast(FP8X4),
                     lhsT_scale=w_bytes[W3_ROW if skip_side else 0 : P, cols],
-                    rhs=(skip_codes if skip_side else z_codes)[:, cells(piece, piece + 1)].bitcast(FP8X4),
-                    rhs_scale=(skip_bytes if skip_side else z_bytes)[:, cells(piece, piece + 1)],
-                    start=skip_side and t == 0,
-                    stop=not skip_side and t == PACK - 1,
+                    rhs=(skip_codes if skip_side else z_codes)[:, cells(first, end)].bitcast(FP8X4),
+                    rhs_scale=(skip_bytes if skip_side else z_bytes)[:, cells(first, end)],
+                    start=skip_side and t == first_plane,
+                    stop=not skip_side and t == end_plane - 1,
                 )
 
-        accs = [bank([P, PACK, PIECE], piece, f"acc{piece}") for piece in range(PIECES)]
-        for piece in range(PIECES):
-            add_product(accs[piece], piece, True)
+        accs = {}
+        for number, group in enumerate(groups):
+            first, end, first_plane, end_plane = group
+            accs[group] = bank([P, end_plane - first_plane, (end - first) * PIECE], number, f"acc{number}")
+            add_product(accs[group], group, True)
 
         z_grouped = {}
 
@@ -232,21 +250,19 @@ def tile_picked_segunpool_relu_po_kernel(
                 in_=z_grouped[first][:].rearrange("p c t -> p (c t)"),
             )
 
-        pair_up(on_vector, 0, 0, 2)
-        pair_up(on_vector, 1, 0, 1)
-        pair_up(on_vector, 1, 1, 2)
-        for first in (2, 4):
-            pair_up(on_scalar, 0, first, first + 2)
+        pair_up(on_vector, 1, 0, 4)
+        pair_up(on_vector, 0, 0, 1)
+        pair_up(on_vector, 0, 1, 4)
+        for first in (4, 6):
             pair_up(on_scalar, 1, first, first + 2)
+            pair_up(on_scalar, 0, first, first + 2)
         weave(0, 1)
         weave(1, 2)
         quantize_z(0, 1)
         quantize_z(1, 2)
         weave(2, 4)
-        pair_up(on_vector, 0, 6, 8)
-        quantize_z(2, 4)
-        pair_up(on_vector, 1, 6, 8)
         weave(4, 6)
+        quantize_z(2, 4)
         weave(6, 8)
         quantize_z(4, 6)
         quantize_z(6, 8)
@@ -254,29 +270,43 @@ def tile_picked_segunpool_relu_po_kernel(
         out_rows = out_0.rearrange("(p t) w -> p t w", t=PACK)
         out_bytes = tile([P, HALF], U8, "out_bytes")
         out_codes = tile([P, U], U32, "out_codes")
-        result = [tile([P, PACK, PIECE], F32, f"result{piece}") for piece in range(PIECES)]
-        out_grouped = [tile([P, PIECE, PACK], BF16, f"out_grouped{piece}") for piece in range(PIECES)]
+        result = [tile([P, PACK, QUARTER], F32, f"result{c}") for c in range(4)]
+        spans = ((0, 2), (2, 4), (4, 6), (6, 8))
 
-        def quantize_out(piece):
-            half, at = divmod(piece * PIECE, HALF)
+        def result_cells(first, end, first_plane, end_plane):
+            at = first % 2 * PIECE
+            return result[first // 2][:, first_plane:end_plane, at : at + (end - first) * PIECE]
+
+        def quantize_out(grouped, first, end):
+            half, at = divmod(first * PIECE, HALF)
             nc.vector.quantize_mx(
-                out=out_codes[:, cells(piece, piece + 1)].bitcast(FP8X4),
-                scales=out_bytes[4 * half : P, at : at + PIECE],
-                in_=out_grouped[piece][:].rearrange("p c t -> p (c t)"),
+                out=out_codes[:, cells(first, end)].bitcast(FP8X4),
+                scales=out_bytes[4 * half : P, at : at + (end - first) * PIECE],
+                in_=grouped[:].rearrange("p c t -> p (c t)"),
             )
 
-        for piece in range(PIECES):
-            add_product(accs[piece], piece, False)
-            on_scalar(out=result[piece][:], in_=accs[piece][:])
-            nc.sync.dma_start(out=out_rows[:, :, cells(piece, piece + 1)], in_=result[piece][:])
-            last = piece == PIECES - 1
-            (on_scalar if last else on_vector)(
-                out=out_grouped[piece][:].rearrange("p (c i) t -> p c t i", i=4),
-                in_=result[piece][:].rearrange("p t (c i) -> p c t i", i=4),
+        waiting = None
+        for first, end in spans:
+            grouped = tile([P, (end - first) * PIECE, PACK], BF16, f"out_grouped{first}")
+            for group in groups:
+                if first <= group[0] < end:
+                    add_product(accs[group], group, False)
+                    if group == groups[-1]:
+                        on_vector(
+                            out=grouped[:, PIECE:, :].rearrange("p (c i) t -> p c t i", i=4),
+                            in_=accs[group][:].rearrange("p t (c i) -> p c t i", i=4),
+                        )
+                    on_scalar(out=result_cells(*group), in_=accs[group][:])
+                    nc.sync.dma_start(out=out_rows[:, group[2] : group[3], cells(*group[:2])], in_=result_cells(*group))
+            copied = min(end, PIECES - 1)
+            on_vector(
+                out=grouped[:, : (copied - first) * PIECE, :].rearrange("p (c i) t -> p c t i", i=4),
+                in_=result_cells(first, copied, 0, PACK).rearrange("p t (c i) -> p c t i", i=4),
             )
-            if piece > 0:
-                quantize_out(piece - 1)
-        quantize_out(PIECES - 1)
+            if waiting:
+                quantize_out(*waiting)
+            waiting = (grouped, first, end)
+        quantize_out(*waiting)
         split = U - QUARTER
         nc.sync.dma_start(out=words_view(out_1)[:, :split], in_=out_codes[:, :split].bitcast(I32))
         nc.scalar.dma_start(out=words_view(out_1)[:, split:], in_=out_codes[:, split:].bitcast(I32))

@@ -24,7 +24,7 @@ PIECES = 8
 ROWS_AT = 112
 W3_ROW = 4
 FIRST = 128
-SHARE = 256
+SHARE = 192
 W2_ROWS_AT = 96
 KB = 1024
 
@@ -33,10 +33,10 @@ def words_view(dram):
     return dram[0].rearrange("p c r -> p (c r)").bitcast(I32)
 
 
-def deal(engine, out, in_, run):
+def deal(engine, out, in_, run, first_plane=0, end_plane=PACK):
     engine.tensor_copy(
-        out=out.rearrange("p (t b i) -> p b t i", t=PACK, i=run),
-        in_=in_.rearrange("p (b i t) -> p b t i", t=PACK, i=run),
+        out=out.rearrange("p (t b i) -> p b t i", t=end_plane - first_plane, i=run),
+        in_=in_.rearrange("p (b i t) -> p b t i", t=PACK, i=run)[:, :, first_plane:end_plane, :],
     )
 
 
@@ -70,10 +70,11 @@ def tile_picked_segunpool_relu_po_kernel(
         x_bytes = tile([P, T], U8, "x_bytes")
         picked_bytes = tile([P, S], U8, "picked_bytes")
         skip_bytes = tile([P, U], U8, "skip_bytes")
-        x_codes = place([P, T], U32, "x_codes", 44 * KB)
-        w1_raw = [place([P, PACK, H // 2], F32, "w1_raw0", 30 * KB), place([P, PACK, H // 2], F32, "w1_raw1", 20 * KB)]
+        x_codes = tile([P, T], U32, "x_codes")
+        w1_raw = [place([P, PACK, H // 2], F32, "w1_raw0", 16 * KB), place([P, PACK, H // 2], F32, "w1_raw1", 20 * KB)]
         w_bytes = tile([P, N], U8, "w_bytes")
-        windows = [place([P, U], F32, f"window{t}", offset * KB) for t, offset in enumerate((80, 40, 124, 120))]
+        windows = {t: tile([P, U], F32, f"window{t}") for t in (0, 1, 3)}
+        windows[2] = place([P, U], F32, "window2", 32 * KB)
 
         nc.gpsimd.memset(x_bytes[:ROWS_AT, :].bitcast(I32), 0)
         nc.gpsimd.memset(picked_bytes[:].bitcast(I32), 0)
@@ -102,23 +103,23 @@ def tile_picked_segunpool_relu_po_kernel(
                     in_=src[rows_at + 4 * q : rows_at + 4 * q + 4, :].bitcast(I32),
                 )
 
-        picked_spread = place([P, S], U8, "picked_spread", 10 * KB)
+        picked_spread = place([P, S], U8, "picked_spread", 8 * KB)
         skip_spread = place([P, U], U8, "skip_spread", 0)
         nc.vector.tensor_copy(out=picked_spread[:], in_=x_bytes[:].indirect(offs_sb[:]))
         place_rows(nc.scalar, picked_bytes, picked_spread)
         nc.vector.tensor_copy(out=skip_spread[:], in_=x_bytes[:].indirect(skip_sb[:]))
         place_rows(nc.sync, skip_bytes, skip_spread)
 
-        w2_raw = place([P, N], U32, "w2_raw", 10 * KB + S // 2)
-        w3_raw = place([P, N], U32, "w3_raw", 30 * KB)
+        w2_raw = place([P, N], U32, "w2_raw", 16 * KB)
+        w3_raw = place([P, N], U32, "w3_raw", 18 * KB)
         nc.sync.dma_start(out=w2_raw[:].bitcast(I32), in_=words_view(w2_words))
-        w_bytes_raw = place([P, N], U8, "w_bytes_raw", 10 * KB - S // 2)
+        w_bytes_raw = place([P, N], U8, "w_bytes_raw", 8 * KB)
         nc.gpsimd.memset(w_bytes_raw[:W2_ROWS_AT, :].bitcast(I32), 0)
         nc.sync.dma_start(out=w_bytes_raw[W2_ROWS_AT:ROWS_AT, :].bitcast(I32), in_=w2_scales[0].bitcast(I32))
         nc.sync.dma_start(out=w_bytes_raw[ROWS_AT:, :].bitcast(I32), in_=w3_scales[0].bitcast(I32))
         nc.sync.dma_start(out=w3_raw[:].bitcast(I32), in_=words_view(w3_words))
 
-        w1_codes = tile([P, H], U32, "w1_codes")
+        w1_codes = [tile([P, H // 2], U32, "w1_codes0"), place([P, H // 2], U32, "w1_codes1", 40 * KB)]
         w1_bytes = tile([P, H], U8, "w1_bytes")
         for u in (1, 0):
             w1_grouped = tile([P, 2, P, PACK], BF16, f"w1_grouped{u}")
@@ -129,14 +130,14 @@ def tile_picked_segunpool_relu_po_kernel(
                 )
             cols = slice(2 * u * P, 2 * (u + 1) * P)
             nc.vector.quantize_mx(
-                out=w1_codes[:, cols].bitcast(FP8X4), scales=w1_bytes[:, cols], in_=w1_grouped[:].rearrange("p t m j -> p (t m j)")
+                out=w1_codes[u][:].bitcast(FP8X4), scales=w1_bytes[:, cols], in_=w1_grouped[:].rearrange("p t m j -> p (t m j)")
             )
 
         picked_codes = place([P, S], U32, "picked_codes", 20 * KB)
         for lo, hi in ((0, FIRST), (FIRST, S // 2), (S // 2, S)):
             nc.vector.tensor_copy(out=picked_codes[:, lo:hi], in_=x_codes[:].indirect(offs_sb[:, lo // 16 : hi // 16]))
-        skip_codes = place([P, U], U32, "skip_codes", 22 * KB)
-        nc.vector.tensor_copy(out=skip_codes[:], in_=x_codes[:].indirect(skip_sb[:]))
+        skip_first = place([P, PIECE], U32, "skip_first", 22 * KB)
+        nc.vector.tensor_copy(out=skip_first[:], in_=x_codes[:].indirect(skip_sb[:, : PIECE // 16]))
 
         def relu_on_scalar(out, in_):
             nc.scalar.activation(out=out, in_=in_, func=ACT.Relu)
@@ -144,18 +145,19 @@ def tile_picked_segunpool_relu_po_kernel(
         def relu_on_vector(out, in_):
             nc.vector.tensor_scalar_max(out, in_, 0.0)
 
-        def activate(relu, t, lo, hi, number, out):
+        def activate(relu, t, cuts, number, out):
             cols = slice(t * P, (t + 1) * P)
-            acc = bank([P, hi - lo], number, f"acc_y{t}_{lo}")
-            nc.tensor.matmul_mx(
-                out=acc[:],
-                lhsT=w1_codes[:, cols].bitcast(FP8X4),
-                lhsT_scale=w1_bytes[:, cols],
-                rhs=picked_codes[:, lo:hi].bitcast(FP8X4),
-                rhs_scale=picked_bytes[:, lo:hi],
-                start=True,
-                stop=True,
-            )
+            acc = bank([P, cuts[-1] - cuts[0]], number, f"acc_y{t}_{cuts[0]}")
+            for lo, hi in zip(cuts, cuts[1:]):
+                nc.tensor.matmul_mx(
+                    out=acc[:, lo - cuts[0] : hi - cuts[0]],
+                    lhsT=w1_codes[t // 2][:, t % 2 * P : (t % 2 + 1) * P].bitcast(FP8X4),
+                    lhsT_scale=w1_bytes[:, cols],
+                    rhs=picked_codes[:, lo:hi].bitcast(FP8X4),
+                    rhs_scale=picked_bytes[:, lo:hi],
+                    start=True,
+                    stop=True,
+                )
             relu(out, acc[:])
 
         def scatter(by_scalar, t, values, lo, hi):
@@ -165,35 +167,32 @@ def tile_picked_segunpool_relu_po_kernel(
             else:
                 nc.vector.tensor_copy(out=target, in_=values)
 
-        y_first = place([P, FIRST], F32, "y_first", 36 * KB)
-        y_second = tile([P, FIRST], F32, "y_second")
-        y_rest = place([P, S // 2], F32, "y_rest", 35 * KB + 2 * FIRST)
-        y_early = place([P, S], F32, "y_early", 36 * KB + 2 * FIRST)
-        y_late = place([P, 2, S], F32, "y_late", 12 * KB)
-        y = {3: y_early[:], 0: y_late[:, 0, :], 1: y_late[:, 1, :]}
-        activate(relu_on_scalar, 2, 0, FIRST, 0, y_first[:])
-        activate(relu_on_scalar, 2, FIRST, S // 2, 1, y_second[:])
+        y_first = tile([P, FIRST], F32, "y_first")
+        y_rest = place([P, S - FIRST], F32, "y_rest", 12 * KB)
+        y_early = place([P, S], F32, "y_early", 36 * KB)
+        y_late = place([P, 2, S], F32, "y_late", 12 * KB + KB // 2)
+        activate(relu_on_scalar, 2, (0, FIRST), 0, y_first[:])
         scatter(True, 2, y_first[:], 0, FIRST)
-        scatter(True, 2, y_second[:], FIRST, S // 2)
-        activate(relu_on_scalar, 2, S // 2, S, 2, y_rest[:])
-        scatter(True, 2, y_rest[:], S // 2, S)
-        for number, t in enumerate((3, 0, 1)):
-            activate(relu_on_vector, t, 0, S, 3 + number, y[t])
-        scatter(True, 3, y[3], 0, S)
-        scatter(False, 0, y[0][:, :SHARE], 0, SHARE)
-        scatter(False, 1, y[1], 0, S)
-        scatter(True, 0, y[0][:, SHARE:], SHARE, S)
+        activate(relu_on_vector, 2, (FIRST, S // 2, S), 1, y_rest[:])
+        scatter(True, 2, y_rest[:], FIRST, S)
+        activate(relu_on_vector, 3, (0, S), 2, y_early[:])
+        skip_rest = place([P, U - PIECE], U32, "skip_rest", 40 * KB)
+        nc.vector.tensor_copy(out=skip_rest[:], in_=x_codes[:].indirect(skip_sb[:, PIECE // 16 :]))
+        scatter(False, 3, y_early[:], 0, S)
+        for t in (0, 1):
+            activate(relu_on_scalar, t, (0, S), 3 + t, y_late[:, t, :])
+        scatter(True, 0, y_late[:, 0, :SHARE], 0, SHARE)
+        scatter(True, 1, y_late[:, 1, :], 0, S)
+        scatter(False, 0, y_late[:, 0, SHARE:], SHARE, S)
 
         w2_codes = tile([P, N], U32, "w2_codes")
         deal(nc.gpsimd, w2_codes[:], w2_raw[:], 4)
         w_bytes_spread = tile([P, N], U8, "w_bytes_spread")
         deal(nc.gpsimd, w_bytes_spread[:], w_bytes_raw[:], 16)
-        w3_codes = tile([P, N], U32, "w3_codes")
-        deal(nc.gpsimd, w3_codes[:], w3_raw[:], 4)
         place_rows(nc.sync, w_bytes, w_bytes_spread, ROWS_AT, W3_ROW)
         place_rows(nc.sync, w_bytes, w_bytes_spread, W2_ROWS_AT)
 
-        z_pairs = place([P, PIECES, 2, PIECE, 2], BF16, "z_pairs", 3 * KB)
+        z_pairs = place([P, PIECES, 2, PIECE, 2], BF16, "z_pairs", 4 * KB + KB // 2)
 
         def cells(first, end):
             return slice(first * PIECE, end * PIECE)
@@ -205,23 +204,33 @@ def tile_picked_segunpool_relu_po_kernel(
             )
 
         pair_up(on_gpsimd, 2, 0, PIECES)
-        pair_up(on_gpsimd, 3, 0, PIECES // 2)
-        pair_up(on_gpsimd, 3, PIECES // 2, PIECES)
+        w3_codes = [tile([P, N // 2], U32, "w3_codes0"), place([P, N // 2], U32, "w3_codes1", 35 * KB + KB // 2)]
+        deal(nc.gpsimd, w3_codes[0][:], w3_raw[:], 4, 0, 2)
+        pair_up(on_gpsimd, 3, 0, 4)
+        deal(nc.gpsimd, w3_codes[1][:], w3_raw[:], 4, 2, PACK)
+        pair_up(on_gpsimd, 3, 4, PIECES)
 
         z_codes = tile([P, U], U32, "z_codes")
         z_bytes = tile([P, U], U8, "z_bytes")
 
-        groups = [(0, 1, 0, 4), (1, 2, 0, 4), (2, 4, 0, 2), (2, 4, 2, 4), (4, 6, 0, 2), (4, 6, 2, 4), (6, 7, 0, 4), (7, 8, 0, 4)]
+        spans = ((0, 1), (1, 3), (3, 5), (5, 7), (7, 8))
+        groups = [
+            (first, end, plane, plane + PACK // (end - first)) for first, end in spans for plane in range(0, PACK, PACK // (end - first))
+        ]
 
-        def add_product(acc, group, skip_side):
+        def skip_cells(first, end):
+            return skip_rest[:, cells(first - 1, end - 1)] if first else skip_first[:]
+
+        def add_product(acc, group, skip_side, planes=range(PACK)):
             first, end, first_plane, end_plane = group
-            for t in range(first_plane, end_plane):
+            for t in range(max(first_plane, planes.start), min(end_plane, planes.stop)):
                 cols = slice(t * P, (t + 1) * P)
+                w3_plane = w3_codes[t // 2][:, t % 2 * P : (t % 2 + 1) * P]
                 nc.tensor.matmul_mx(
                     out=acc[:, t - first_plane, :],
-                    lhsT=(w3_codes if skip_side else w2_codes)[:, cols].bitcast(FP8X4),
+                    lhsT=(w3_plane if skip_side else w2_codes[:, cols]).bitcast(FP8X4),
                     lhsT_scale=w_bytes[W3_ROW if skip_side else 0 : P, cols],
-                    rhs=(skip_codes if skip_side else z_codes)[:, cells(first, end)].bitcast(FP8X4),
+                    rhs=(skip_cells(first, end) if skip_side else z_codes[:, cells(first, end)]).bitcast(FP8X4),
                     rhs_scale=(skip_bytes if skip_side else z_bytes)[:, cells(first, end)],
                     start=skip_side and t == first_plane,
                     stop=not skip_side and t == end_plane - 1,
@@ -231,7 +240,9 @@ def tile_picked_segunpool_relu_po_kernel(
         for number, group in enumerate(groups):
             first, end, first_plane, end_plane = group
             accs[group] = bank([P, end_plane - first_plane, (end - first) * PIECE], number, f"acc{number}")
-            add_product(accs[group], group, True)
+        for planes in (range(2), range(2, PACK)):
+            for group in groups:
+                add_product(accs[group], group, True, planes)
 
         z_grouped = {}
 
@@ -250,68 +261,57 @@ def tile_picked_segunpool_relu_po_kernel(
                 in_=z_grouped[first][:].rearrange("p c t -> p (c t)"),
             )
 
-        pair_up(on_vector, 1, 0, 4)
-        pair_up(on_vector, 0, 0, 1)
-        pair_up(on_vector, 0, 1, 4)
-        for first in (4, 6):
-            pair_up(on_scalar, 1, first, first + 2)
-            pair_up(on_scalar, 0, first, first + 2)
-        weave(0, 1)
-        weave(1, 2)
-        quantize_z(0, 1)
-        quantize_z(1, 2)
-        weave(2, 4)
-        weave(4, 6)
-        quantize_z(2, 4)
-        weave(6, 8)
-        quantize_z(4, 6)
-        quantize_z(6, 8)
+        pair_up(on_vector, 0, 0, 4)
+        pair_up(on_vector, 1, 0, 1)
+        pair_up(on_vector, 1, 1, 4)
+        pair_up(on_scalar, 0, 4, PIECES)
+        pair_up(on_scalar, 1, 4, 6)
+        pair_up(on_scalar, 1, 6, PIECES)
+        for batch in (spans[:2], spans[2:4], spans[4:]):
+            for span in batch:
+                weave(*span)
+            for span in batch:
+                quantize_z(*span)
 
         out_rows = out_0.rearrange("(p t) w -> p t w", t=PACK)
-        out_bytes = tile([P, HALF], U8, "out_bytes")
+        out_bytes = tile([P, U], U8, "out_bytes")
         out_codes = tile([P, U], U32, "out_codes")
-        result = [tile([P, PACK, QUARTER], F32, f"result{c}") for c in range(4)]
-        spans = ((0, 2), (2, 4), (4, 6), (6, 8))
+        out_grouped = tile([P, U, PACK], BF16, "out_grouped")
 
-        def result_cells(first, end, first_plane, end_plane):
-            at = first % 2 * PIECE
-            return result[first // 2][:, first_plane:end_plane, at : at + (end - first) * PIECE]
+        def interleave(first, end, planes):
+            on_vector(
+                out=out_grouped[:, cells(first, end), :].rearrange("p (c i) t -> p c t i", i=4),
+                in_=planes.rearrange("p t (c i) -> p c t i", i=4),
+            )
 
-        def quantize_out(grouped, first, end):
-            half, at = divmod(first * PIECE, HALF)
+        def quantize_out(first, end):
             nc.vector.quantize_mx(
                 out=out_codes[:, cells(first, end)].bitcast(FP8X4),
-                scales=out_bytes[4 * half : P, at : at + (end - first) * PIECE],
-                in_=grouped[:].rearrange("p c t -> p (c t)"),
+                scales=out_bytes[:, cells(first, end)],
+                in_=out_grouped[:, cells(first, end), :].rearrange("p c t -> p (c t)"),
             )
 
-        waiting = None
         for first, end in spans:
-            grouped = tile([P, (end - first) * PIECE, PACK], BF16, f"out_grouped{first}")
+            result = tile([P, PACK, (end - first) * PIECE], F32, f"result{first}")
             for group in groups:
-                if first <= group[0] < end:
+                if group[0] == first:
                     add_product(accs[group], group, False)
-                    if group == groups[-1]:
-                        on_vector(
-                            out=grouped[:, PIECE:, :].rearrange("p (c i) t -> p c t i", i=4),
-                            in_=accs[group][:].rearrange("p t (c i) -> p c t i", i=4),
-                        )
-                    on_scalar(out=result_cells(*group), in_=accs[group][:])
-                    nc.sync.dma_start(out=out_rows[:, group[2] : group[3], cells(*group[:2])], in_=result_cells(*group))
-            copied = min(end, PIECES - 1)
-            on_vector(
-                out=grouped[:, : (copied - first) * PIECE, :].rearrange("p (c i) t -> p c t i", i=4),
-                in_=result_cells(first, copied, 0, PACK).rearrange("p t (c i) -> p c t i", i=4),
-            )
-            if waiting:
-                quantize_out(*waiting)
-            waiting = (grouped, first, end)
-        quantize_out(*waiting)
-        split = U - QUARTER
+                    if end == PIECES:
+                        interleave(first, end, accs[group][:])
+                    for lo in range(group[2], group[3], PACK if end == PIECES else 2):
+                        hi = min(lo + (PACK if end == PIECES else 2), group[3])
+                        on_scalar(out=result[:, lo:hi, :], in_=accs[group][:, lo - group[2] : hi - group[2], :])
+                        nc.sync.dma_start(out=out_rows[:, lo:hi, cells(first, end)], in_=result[:, lo:hi, :])
+            if end < PIECES:
+                interleave(first, end, result[:])
+            if first == 3:
+                quantize_out(0, 3)
+        for first, end in ((3, 5), (7, 8), (5, 7)):
+            quantize_out(first, end)
+        split = 5 * PIECE
         nc.sync.dma_start(out=words_view(out_1)[:, :split], in_=out_codes[:, :split].bitcast(I32))
         nc.scalar.dma_start(out=words_view(out_1)[:, split:], in_=out_codes[:, split:].bitcast(I32))
         for q in range(4):
             (nc.sync if q < 3 else nc.scalar).dma_start(
-                out=out_2[0, 4 * q : 4 * q + 4, :].bitcast(I32).rearrange("r (c w) -> c r w", c=2),
-                in_=out_bytes[32 * q : 32 * q + 8, :].bitcast(I32),
+                out=out_2[0, 4 * q : 4 * q + 4, :].bitcast(I32), in_=out_bytes[32 * q : 32 * q + 4, :].bitcast(I32)
             )

@@ -71,7 +71,7 @@ def tile_picked_segunpool_relu_po_kernel(
         picked_bytes = tile([P, S], U8, "picked_bytes")
         skip_bytes = tile([P, U], U8, "skip_bytes")
         x_codes = tile([P, T], U32, "x_codes")
-        w1_raw = [place([P, PACK, H // 2], F32, "w1_raw0", 16 * KB), place([P, PACK, H // 2], F32, "w1_raw1", 20 * KB)]
+        w1_raw = [place([P, PACK, H // 2], F32, "w1_raw0", 24 * KB), place([P, PACK, H // 2], F32, "w1_raw1", 20 * KB)]
         w_bytes = tile([P, N], U8, "w_bytes")
         windows = {t: tile([P, U], F32, f"window{t}") for t in (0, 1, 3)}
         windows[2] = place([P, U], F32, "window2", 32 * KB)
@@ -110,8 +110,8 @@ def tile_picked_segunpool_relu_po_kernel(
         nc.vector.tensor_copy(out=skip_spread[:], in_=x_bytes[:].indirect(skip_sb[:]))
         place_rows(nc.sync, skip_bytes, skip_spread)
 
-        w2_raw = place([P, N], U32, "w2_raw", 16 * KB)
-        w3_raw = place([P, N], U32, "w3_raw", 18 * KB)
+        w2_raw = place([P, N], U32, "w2_raw", 24 * KB)
+        w3_raw = place([P, N], U32, "w3_raw", 26 * KB)
         nc.sync.dma_start(out=w2_raw[:].bitcast(I32), in_=words_view(w2_words))
         w_bytes_raw = place([P, N], U8, "w_bytes_raw", 8 * KB)
         nc.gpsimd.memset(w_bytes_raw[:W2_ROWS_AT, :].bitcast(I32), 0)

from contextlib import ExitStack

import concourse.mybir as mybir

K, T, S, N, U, H = 512, 2048, 512, 512, 1024, 512
FLOPS = 2 * K * H * S + 2 * H * N * U + 2 * K * N * U

F32 = mybir.dt.float32
BF16 = mybir.dt.bfloat16
I32 = mybir.dt.int32
U32 = mybir.dt.uint32
U16 = mybir.dt.uint16
U8 = mybir.dt.uint8
FP8X4 = mybir.dt.float8_e4m3fn_x4
ACT = mybir.ActivationFunctionType
ALU = mybir.AluOpType

P = 128
PACK = 4
HALF = U // 2
QUARTER = U // 4
PIECE = U // 8
PIECES = 8
ROWS_AT = 112
W3_ROW = 4
FIRST = 128
SHARE = 192
W2_ROWS_AT = 96
KB = 1024


def words_view(dram):
    return dram[0].rearrange("p c r -> p (c r)").bitcast(I32)


def deal(engine, out, in_, run, first_plane=0, end_plane=PACK):
    engine.tensor_copy(
        out=out.rearrange("p (t b i) -> p b t i", t=end_plane - first_plane, i=run),
        in_=in_.rearrange("p (b i t) -> p b t i", t=PACK, i=run)[:, :, first_plane:end_plane, :],
    )


def tile_picked_segunpool_relu_po_kernel(
    tc, x_words, x_scales, w1, w2_words, w2_scales, w3_words, w3_scales, offs, where, skip, out_0, out_1, out_2
):
    nc = tc.nc
    with ExitStack() as ctx:
        lists = ctx.enter_context(tc.tile_pool(name="lists", bufs=1))
        sb = ctx.enter_context(tc.tile_pool(name="sb", bufs=1))
        placed = ctx.enter_context(tc.tile_pool(name="placed", bufs=1))
        psum = ctx.enter_context(tc.psum_pool(name="psum", bufs=1))

        def tile(shape, dtype, name):
            return sb.tile(shape, dtype, name=name, tag=name, align_bytes=256)

        def place(shape, dtype, name, offset):
            return placed.tile(shape, dtype, name=name, offset=offset, align_bytes=256)

        def bank(shape, number, name):
            return psum.tile(shape, F32, name=name, tag=f"bank{number}")

        def on_gpsimd(out, in_):
            nc.gpsimd.tensor_scalar(out=out, in0=in_, scalar1=1.0, scalar2=0.0, op0=ALU.mult, op1=ALU.add)

        on_scalar, on_vector = nc.scalar.copy, nc.vector.tensor_copy

        offs_sb = lists.tile([P, S // 16], U16, name="offs_sb")
        skip_sb = lists.tile([P, U // 16], U16, name="skip_sb")
        where_sb = lists.tile([P, S // 16], U16, name="where_sb")
        x_bytes = tile([P, T], U8, "x_bytes")
        picked_bytes = tile([P, S], U8, "picked_bytes")
        skip_bytes = tile([P, U], U8, "skip_bytes")
        x_codes = tile([P, T], U32, "x_codes")
        w1_raw = [place([P, PACK, H // 2], F32, "w1_raw0", 24 * KB), place([P, PACK, H // 2], F32, "w1_raw1", 20 * KB)]
        w_bytes = tile([P, N], U8, "w_bytes")
        windows = {t: tile([P, U], F32, f"window{t}") for t in (0, 1, 3)}
        windows[2] = place([P, U], F32, "window2", 32 * KB)

        nc.gpsimd.memset(x_bytes[:ROWS_AT, :].bitcast(I32), 0)
        nc.gpsimd.memset(picked_bytes[:].bitcast(I32), 0)
        nc.gpsimd.memset(skip_bytes[:].bitcast(I32), 0)
        nc.gpsimd.memset(w_bytes[:].bitcast(I32), 0)
        for t in (0, 1):
            nc.gpsimd.memset(windows[t][:], 0.0)
        nc.sync.dma_start(offs_sb[:], offs)
        nc.scalar.dma_start(out=x_bytes[ROWS_AT:, :].bitcast(I32), in_=x_scales[0].bitcast(I32))
        warm = tile([P, 2], F32, "warm")
        nc.vector.memset(warm[:, 0:1], 0.0)
        nc.scalar.activation(out=warm[:, 1:2], in_=warm[:, 0:1], func=ACT.Relu)
        for t in (2, 3):
            nc.vector.memset(windows[t][:], 0.0)
        w1_rows = w1.rearrange("(p j) h -> p j h", j=PACK)
        nc.sync.dma_start(out=w1_raw[0][:], in_=w1_rows[:, :, : H // 2])
        nc.sync.dma_start(skip_sb[:], skip)
        nc.sync.dma_start(out=w1_raw[1][:], in_=w1_rows[:, :, H // 2 :])
        nc.sync.dma_start(out=x_codes[:].bitcast(I32), in_=words_view(x_words))
        nc.sync.dma_start(where_sb[:], where)

        def place_rows(queue, dst, src, rows_at=ROWS_AT, first_row=0):
            for q in range(4):
                queue.dma_start(
                    out=dst[32 * q + first_row : 32 * q + first_row + 4, :].bitcast(I32),
                    in_=src[rows_at + 4 * q : rows_at + 4 * q + 4, :].bitcast(I32),
                )

        picked_spread = place([P, S], U8, "picked_spread", 8 * KB)
        skip_spread = place([P, U], U8, "skip_spread", 0)
        nc.vector.tensor_copy(out=picked_spread[:], in_=x_bytes[:].indirect(offs_sb[:]))
        place_rows(nc.scalar, picked_bytes, picked_spread)
        nc.vector.tensor_copy(out=skip_spread[:], in_=x_bytes[:].indirect(skip_sb[:]))
        place_rows(nc.sync, skip_bytes, skip_spread)

        w2_raw = place([P, N], U32, "w2_raw", 24 * KB)
        w3_raw = place([P, N], U32, "w3_raw", 26 * KB)
        nc.sync.dma_start(out=w2_raw[:].bitcast(I32), in_=words_view(w2_words))
        w_bytes_raw = place([P, N], U8, "w_bytes_raw", 8 * KB)
        nc.gpsimd.memset(w_bytes_raw[:W2_ROWS_AT, :].bitcast(I32), 0)
        nc.sync.dma_start(out=w_bytes_raw[W2_ROWS_AT:ROWS_AT, :].bitcast(I32), in_=w2_scales[0].bitcast(I32))
        nc.sync.dma_start(out=w_bytes_raw[ROWS_AT:, :].bitcast(I32), in_=w3_scales[0].bitcast(I32))
        nc.sync.dma_start(out=w3_raw[:].bitcast(I32), in_=words_view(w3_words))

        w1_codes = [tile([P, H // 2], U32, "w1_codes0"), place([P, H // 2], U32, "w1_codes1", 40 * KB)]
        w1_bytes = tile([P, H], U8, "w1_bytes")
        for u in (1, 0):
            w1_grouped = tile([P, 2, P, PACK], BF16, f"w1_grouped{u}")
            for a in range(2):
                (on_vector if (u, a) == (0, 1) else on_scalar)(
                    out=w1_grouped[:, :, a * P // 2 : (a + 1) * P // 2, :].rearrange("p t m j -> p m j t"),
                    in_=w1_raw[a][:].rearrange("p j (m t) -> p m j t", t=PACK)[:, :, :, 2 * u : 2 * u + 2],
                )
            cols = slice(2 * u * P, 2 * (u + 1) * P)
            nc.vector.quantize_mx(
                out=w1_codes[u][:].bitcast(FP8X4), scales=w1_bytes[:, cols], in_=w1_grouped[:].rearrange("p t m j -> p (t m j)")
            )

        picked_codes = place([P, S], U32, "picked_codes", 20 * KB)
        for lo, hi in ((0, FIRST), (FIRST, S // 2), (S // 2, S)):
            nc.vector.tensor_copy(out=picked_codes[:, lo:hi], in_=x_codes[:].indirect(offs_sb[:, lo // 16 : hi // 16]))
        skip_first = place([P, PIECE], U32, "skip_first", 22 * KB)
        nc.vector.tensor_copy(out=skip_first[:], in_=x_codes[:].indirect(skip_sb[:, : PIECE // 16]))

        def relu_on_scalar(out, in_):
            nc.scalar.activation(out=out, in_=in_, func=ACT.Relu)

        def relu_on_vector(out, in_):
            nc.vector.tensor_scalar_max(out, in_, 0.0)

        def activate(relu, t, cuts, number, out):
            cols = slice(t * P, (t + 1) * P)
            acc = bank([P, cuts[-1] - cuts[0]], number, f"acc_y{t}_{cuts[0]}")
            for lo, hi in zip(cuts, cuts[1:]):
                nc.tensor.matmul_mx(
                    out=acc[:, lo - cuts[0] : hi - cuts[0]],
                    lhsT=w1_codes[t // 2][:, t % 2 * P : (t % 2 + 1) * P].bitcast(FP8X4),
                    lhsT_scale=w1_bytes[:, cols],
                    rhs=picked_codes[:, lo:hi].bitcast(FP8X4),
                    rhs_scale=picked_bytes[:, lo:hi],
                    start=True,
                    stop=True,
                )
            relu(out, acc[:])

        def scatter(by_scalar, t, values, lo, hi):
            target = windows[t][:].indirect(where_sb[:, lo // 16 : hi // 16])
            if by_scalar:
                nc.scalar.activation(out=target, in_=values, func=ACT.Copy)
            else:
                nc.vector.tensor_copy(out=target, in_=values)

        y_first = tile([P, FIRST], F32, "y_first")
        y_rest = place([P, S - FIRST], F32, "y_rest", 12 * KB)
        y_early = place([P, S], F32, "y_early", 36 * KB)
        y_late = place([P, 2, S], F32, "y_late", 12 * KB + KB // 2)
        activate(relu_on_scalar, 2, (0, FIRST), 0, y_first[:])
        scatter(True, 2, y_first[:], 0, FIRST)
        activate(relu_on_vector, 2, (FIRST, S // 2, S), 1, y_rest[:])
        scatter(True, 2, y_rest[:], FIRST, S)
        activate(relu_on_vector, 3, (0, S), 2, y_early[:])
        skip_rest = place([P, U - PIECE], U32, "skip_rest", 40 * KB)
        nc.vector.tensor_copy(out=skip_rest[:], in_=x_codes[:].indirect(skip_sb[:, PIECE // 16 :]))
        scatter(False, 3, y_early[:], 0, S)
        for t in (0, 1):
            activate(relu_on_scalar, t, (0, S), 3 + t, y_late[:, t, :])
        scatter(True, 0, y_late[:, 0, :SHARE], 0, SHARE)
        scatter(True, 1, y_late[:, 1, :], 0, S)
        scatter(False, 0, y_late[:, 0, SHARE:], SHARE, S)

        w2_codes = tile([P, N], U32, "w2_codes")
        deal(nc.gpsimd, w2_codes[:], w2_raw[:], 4)
        w_bytes_spread = tile([P, N], U8, "w_bytes_spread")
        deal(nc.gpsimd, w_bytes_spread[:], w_bytes_raw[:], 16)
        place_rows(nc.sync, w_bytes, w_bytes_spread, ROWS_AT, W3_ROW)
        place_rows(nc.sync, w_bytes, w_bytes_spread, W2_ROWS_AT)

        z_pairs = place([P, PIECES, 2, PIECE, 2], BF16, "z_pairs", 4 * KB + KB // 2)

        def cells(first, end):
            return slice(first * PIECE, end * PIECE)

        def pair_up(copy, t, first, end):
            copy(
                out=z_pairs[:, first:end, t // 2, :, t % 2],
                in_=windows[t][:, first * PIECE : end * PIECE].rearrange("p (a c) -> p a c", c=PIECE),
            )

        pair_up(on_gpsimd, 2, 0, PIECES)
        w3_codes = [tile([P, N // 2], U32, "w3_codes0"), place([P, N // 2], U32, "w3_codes1", 35 * KB + KB // 2)]
        deal(nc.gpsimd, w3_codes[0][:], w3_raw[:], 4, 0, 2)
        pair_up(on_gpsimd, 3, 0, 4)
        deal(nc.gpsimd, w3_codes[1][:], w3_raw[:], 4, 2, PACK)
        pair_up(on_gpsimd, 3, 4, PIECES)

        z_codes = tile([P, U], U32, "z_codes")
        z_bytes = tile([P, U], U8, "z_bytes")

        spans = ((0, 1), (1, 3), (3, 5), (5, 7), (7, 8))
        groups = [
            (first, end, plane, plane + PACK // (end - first)) for first, end in spans for plane in range(0, PACK, PACK // (end - first))
        ]

        def skip_cells(first, end):
            return skip_rest[:, cells(first - 1, end - 1)] if first else skip_first[:]

        def add_product(acc, group, skip_side, planes=range(PACK)):
            first, end, first_plane, end_plane = group
            for t in range(max(first_plane, planes.start), min(end_plane, planes.stop)):
                cols = slice(t * P, (t + 1) * P)
                w3_plane = w3_codes[t // 2][:, t % 2 * P : (t % 2 + 1) * P]
                nc.tensor.matmul_mx(
                    out=acc[:, t - first_plane, :],
                    lhsT=(w3_plane if skip_side else w2_codes[:, cols]).bitcast(FP8X4),
                    lhsT_scale=w_bytes[W3_ROW if skip_side else 0 : P, cols],
                    rhs=(skip_cells(first, end) if skip_side else z_codes[:, cells(first, end)]).bitcast(FP8X4),
                    rhs_scale=(skip_bytes if skip_side else z_bytes)[:, cells(first, end)],
                    start=skip_side and t == first_plane,
                    stop=not skip_side and t == end_plane - 1,
                )

        accs = {}
        for number, group in enumerate(groups):
            first, end, first_plane, end_plane = group
            accs[group] = bank([P, end_plane - first_plane, (end - first) * PIECE], number, f"acc{number}")
        for planes in (range(2), range(2, PACK)):
            for group in groups:
                add_product(accs[group], group, True, planes)

        z_grouped = {}

        def weave(first, end):
            grouped = tile([P, (end - first) * PIECE, PACK], BF16, f"z_grouped{first}")
            z_grouped[first] = grouped
            nc.vector.tensor_copy(
                out=grouped[:].rearrange("p c t -> p (c t)").bitcast(I32).rearrange("p (a c u) -> p a c u", c=PIECE, u=2),
                in_=z_pairs[:, first:end].rearrange("p a u c e -> p (a u c e)").bitcast(I32).rearrange("p (a u c) -> p a c u", c=PIECE, u=2),
            )

        def quantize_z(first, end):
            nc.vector.quantize_mx(
                out=z_codes[:, cells(first, end)].bitcast(FP8X4),
                scales=z_bytes[:, cells(first, end)],
                in_=z_grouped[first][:].rearrange("p c t -> p (c t)"),
            )

        pair_up(on_vector, 0, 0, 4)
        pair_up(on_vector, 1, 0, 1)
        pair_up(on_vector, 1, 1, 4)
        pair_up(on_scalar, 0, 4, PIECES)
        pair_up(on_scalar, 1, 4, 6)
        pair_up(on_scalar, 1, 6, PIECES)
        for batch in (spans[:2], spans[2:4], spans[4:]):
            for span in batch:
                weave(*span)
            for span in batch:
                quantize_z(*span)

        out_rows = out_0.rearrange("(p t) w -> p t w", t=PACK)
        out_bytes = tile([P, U], U8, "out_bytes")
        out_codes = tile([P, U], U32, "out_codes")
        out_grouped = tile([P, U, PACK], BF16, "out_grouped")

        def interleave(first, end, planes):
            on_vector(
                out=out_grouped[:, cells(first, end), :].rearrange("p (c i) t -> p c t i", i=4),
                in_=planes.rearrange("p t (c i) -> p c t i", i=4),
            )

        def quantize_out(first, end):
            nc.vector.quantize_mx(
                out=out_codes[:, cells(first, end)].bitcast(FP8X4),
                scales=out_bytes[:, cells(first, end)],
                in_=out_grouped[:, cells(first, end), :].rearrange("p c t -> p (c t)"),
            )

        for first, end in spans:
            result = tile([P, PACK, (end - first) * PIECE], F32, f"result{first}")
            for group in groups:
                if group[0] == first:
                    add_product(accs[group], group, False)
                    if end == PIECES:
                        interleave(first, end, accs[group][:])
                    for lo in range(group[2], group[3], PACK if end == PIECES else 2):
                        hi = min(lo + (PACK if end == PIECES else 2), group[3])
                        on_scalar(out=result[:, lo:hi, :], in_=accs[group][:, lo - group[2] : hi - group[2], :])
                        nc.sync.dma_start(out=out_rows[:, lo:hi, cells(first, end)], in_=result[:, lo:hi, :])
            if end < PIECES:
                interleave(first, end, result[:])
            if first == 3:
                quantize_out(0, 3)
        for first, end in ((3, 5), (7, 8), (5, 7)):
            quantize_out(first, end)
        split = 5 * PIECE
        nc.sync.dma_start(out=words_view(out_1)[:, :split], in_=out_codes[:, :split].bitcast(I32))
        nc.scalar.dma_start(out=words_view(out_1)[:, split:], in_=out_codes[:, split:].bitcast(I32))
        for q in range(4):
            (nc.sync if q < 3 else nc.scalar).dma_start(
                out=out_2[0, 4 * q : 4 * q + 4, :].bitcast(I32), in_=out_bytes[32 * q : 32 * q + 4, :].bitcast(I32)
            )
